import numpy as np
import ml_dtypes


def mxq(x, axis, fmt="e4m3"):
    dtype, down = {"e4m3": (ml_dtypes.float8_e4m3fn, 7), "e5m2": (ml_dtypes.float8_e5m2, 14)}[fmt]
    v = np.moveaxis(np.asarray(x, np.float32).astype(ml_dtypes.bfloat16).astype(np.float64), axis, -1)
    blocks = v.reshape(v.shape[:-1] + (-1, 32))
    amax = np.abs(blocks).max(-1, keepdims=True)
    byte = np.maximum(np.where(amax > 0, np.frexp(amax)[1] - 1 + 127, 0) - down, 1)
    scale = np.exp2(byte - 127.0)
    codes = (blocks / scale).astype(np.float32).astype(dtype).astype(np.float64)
    return np.moveaxis((codes * scale).reshape(v.shape), -1, axis)


WIDE = False


def mx_kscale(k):
    if not WIDE:
        return np.ones(k)
    levels = np.array([10, -10, 5, -5, 0])
    if k % 512:
        return np.exp2(np.random.permutation(np.resize(levels, k // 32))).repeat(32)
    a = np.empty((k // 512, 16))
    for p in range(k // 512):
        a[p, :8] = np.random.permutation(np.resize(levels, 8))
        for g in range(8):
            far = levels[np.abs(levels - a[p, g]) >= 10]
            a[p, g + 8] = far[np.random.randint(len(far))]
    return np.exp2(a.ravel()).repeat(32)


def f64(x):
    return np.asarray(x).astype(np.float64)


def striped(idx):
    return np.tile(idx.reshape(-1, 16).T, (8, 1)).astype(np.uint16)


def unstriped(offs):
    return offs[:16].T.reshape(-1).astype(np.int64)


E2M1 = np.array([0.0, 0.5, 1.0, 1.5, 2.0, 3.0, 4.0, 6.0, -0.0, -0.5, -1.0, -1.5, -2.0, -3.0, -4.0, -6.0])


def pack_weight(w, fmt):
    k, n = w.shape
    w = f64(np.asarray(w, np.float32).astype(ml_dtypes.bfloat16)).reshape(k // 32, 32, n)
    amax = np.abs(w).max(1)
    if fmt == "e4m3":
        byte = np.frexp(amax)[1] - 1 + 127 - 7
    else:
        mant, ex = np.frexp(amax / 6.0)
        byte = np.where(mant > 0.5, ex, ex - 1) + 127
    byte = np.clip(np.where(amax > 0, byte, 1), 1, 254)
    scaled = (w * np.exp2(127.0 - byte)[:, None, :]).reshape(k, n).astype(np.float32)
    by_word = np.ascontiguousarray(scaled.reshape(k // 512, 128, 4, n).transpose(0, 1, 3, 2))
    if fmt == "e4m3":
        words = by_word.astype(ml_dtypes.float8_e4m3fn).view(np.uint8)
    else:
        c = by_word.astype(ml_dtypes.float4_e2m1fn).view(np.uint8) & 0xF
        words = (c[..., 0::2] | (c[..., 1::2] << 4)).reshape(k // 512, 128, 2 * n)
    return np.ascontiguousarray(words), np.ascontiguousarray(byte.astype(np.uint8).reshape(k // 512, 16, n))


def unpack_weight(words, scales, fmt):
    g, _, n = scales.shape
    words = np.ascontiguousarray(words).reshape(g, 128, n, -1)
    if fmt == "e4m3":
        vals = words.view(ml_dtypes.float8_e4m3fn).astype(np.float64)
    else:
        nib = np.empty((g, 128, n, 4), np.uint8)
        nib[..., 0::2] = words & 0xF
        nib[..., 1::2] = words >> 4
        vals = E2M1[nib]
    vals = vals * np.repeat(np.exp2(scales.astype(np.float64) - 127.0), 8, axis=1)[..., None]
    return vals.transpose(0, 1, 3, 2).reshape(g * 512, n)


def gelu(v):
    return 0.5 * v * (1.0 + np.tanh(np.sqrt(2.0 / np.pi) * (v + 0.044715 * v**3)))


def bf(x):
    return np.asarray(x, np.float32).astype(ml_dtypes.bfloat16)


def planes(Y):
    n, m = Y.shape
    b = f64(bf(Y)).reshape(n // 32, 32, m)
    amax = np.abs(b).max(1)
    byte = np.clip(np.where(amax > 0, np.frexp(amax)[1] - 1 + 127 - 7, 1), 1, 254)
    codes = (b * np.exp2(127.0 - byte)[:, None, :]).reshape(n, m).astype(np.float32).astype(ml_dtypes.float8_e4m3fn).view(np.uint8)
    words = codes.reshape(n // 512, 128, 4, m).transpose(0, 1, 3, 2)
    return np.ascontiguousarray(words), np.ascontiguousarray(byte.astype(np.uint8).reshape(n // 512, 16, m))


K, T, S, H, N = 1024, 4096, 1024, 512, 256

def setup_inputs():
    n = np.random.standard_normal
    s = mx_kscale(K)[:, None]
    u = mx_kscale(H)[:, None]
    tab_words, tab_scales = pack_weight(n((K, T)) * s, "e4m3")
    w2_words, w2_scales = pack_weight(n((K, H)) / np.sqrt(K) / s, "e2m1")
    w3_words, w3_scales = pack_weight(n((K, H)) / np.sqrt(K) / s * u.T, "e4m3")
    wo_words, wo_scales = pack_weight(n((H, N)) / np.sqrt(H) / u, "e2m1")
    return {
        "tab_words": tab_words, "tab_scales": tab_scales,
        "offs": striped(np.random.permutation(T)[:S]),
        "w1": (n((K, H)) / np.sqrt(K) / s * u.T).astype(np.float32),
        "w2_words": w2_words, "w2_scales": w2_scales,
        "w3_words": w3_words, "w3_scales": w3_scales,
        "pe": n((H, S)).astype(np.float32),
        "wd": (n((K, N)) / np.sqrt(K) / s).astype(np.float32),
        "wo_words": wo_words, "wo_scales": wo_scales,
    }

def reference(tab_words, tab_scales, offs, w1, w2_words, w2_scales, w3_words, w3_scales,
              pe, wd, wo_words, wo_scales):
    v = unpack_weight(tab_words, tab_scales, "e4m3")[:, unstriped(offs)]
    f1 = mxq(f64(w1), 0, "e4m3").T @ v
    f2 = unpack_weight(w2_words, w2_scales, "e2m1").T @ v
    f3 = unpack_weight(w3_words, w3_scales, "e4m3").T @ v
    h = f1 * f2 - f3 * f64(pe)
    d = mxq(f64(wd), 0, "e4m3").T @ v
    e = unpack_weight(wo_words, wo_scales, "e2m1").T @ mxq(h, 0, "e4m3")
    y = e / np.sqrt(1.0 + np.square(d))
    words, scales = planes(h)
    return y, h, words, scales

@@ -1,0 +1,284 @@
+from contextlib import ExitStack
+
+import concourse.mybir as mybir
+
+K, T, S, H, N = 1024, 4096, 1024, 512, 256
+FLOPS = 2 * S * (3 * K * H + K * N + H * N)
+
+F32 = mybir.dt.float32
+BF16 = mybir.dt.bfloat16
+I32 = mybir.dt.int32
+U32 = mybir.dt.uint32
+U16 = mybir.dt.uint16
+U8 = mybir.dt.uint8
+FP8X4 = mybir.dt.float8_e4m3fn_x4
+FP4X4 = mybir.dt.float4_e2m1fn_x4
+ALU = mybir.AluOpType
+ACT = mybir.ActivationFunctionType
+
+P = 128
+PACK = 4
+PASSES = K // (P * PACK)
+HALF = S // 2
+CHUNK = 256
+CHUNKS = S // CHUNK
+W2_AT = S
+W3_AT = S + H
+WO_AT = S + 2 * H
+
+
+def tile_list_autofocus_phase_step_kernel(
+    tc, tab_words, tab_scales, offs, w1, w2_words, w2_scales, w3_words, w3_scales,
+    pe, wd, wo_words, wo_scales, out_0, out_1, out_2, out_3,
+):
+    nc = tc.nc
+    with ExitStack() as ctx:
+        lists = ctx.enter_context(tc.tile_pool(name="lists", bufs=1))
+        keep = ctx.enter_context(tc.tile_pool(name="keep", bufs=1))
+        big = ctx.enter_context(tc.tile_pool(name="big", bufs=1))
+        ring = ctx.enter_context(tc.tile_pool(name="ring", bufs=3))
+        psum = ctx.enter_context(tc.psum_pool(name="psum", bufs=8))
+
+        offsets = lists.tile([P, S // 16], U16, name="offsets")
+        nc.sync.dma_start(offsets[:], offs)
+
+        rows = PASSES * 16
+        tab_rows = keep.tile([P, T], U8, name="tab_rows", align_bytes=64)
+        w_rows = keep.tile([P, 2 * H], U8, name="w_rows", align_bytes=64)
+        plane0 = keep.tile([P, WO_AT + N], U8, name="plane0", align_bytes=64)
+        plane1 = keep.tile([P, WO_AT], U8, name="plane1", align_bytes=64)
+        planes = [plane0, plane1]
+        nc.sync.dma_start(tab_rows[0:rows, :].bitcast(I32), tab_scales.rearrange("a q c -> (a q) c").bitcast(I32))
+        nc.sync.dma_start(w_rows[0:rows, 0:H].bitcast(I32), w2_scales.rearrange("a q c -> (a q) c").bitcast(I32))
+        nc.sync.dma_start(w_rows[0:rows, H:].bitcast(I32), w3_scales.rearrange("a q c -> (a q) c").bitcast(I32))
+        w2_raw = keep.tile([P, PASSES, 2 * H], U8, name="w2_raw", align_bytes=64)
+        nc.sync.dma_start(w2_raw[:].bitcast(I32), w2_words.rearrange("a p c -> p a c").bitcast(I32))
+        tables = []
+        for a in range(PASSES):
+            table = big.tile([P, T], I32, name="table%d" % a, offset=a * 4 * T)
+            nc.sync.dma_start(table[:], tab_words[a].rearrange("p t i -> p (t i)").bitcast(I32))
+            tables.append(table)
+            if a == 0:
+                w3_raw = keep.tile([P, PASSES, H], I32, name="w3_raw", align_bytes=64)
+                nc.sync.dma_start(w3_raw[:], w3_words.rearrange("a p c i -> p a (c i)").bitcast(I32))
+
+        for lo, hi in ((32, 64), (64, P)):
+            nc.vector.memset(tab_rows[lo:hi, :].bitcast(I32), 0)
+            nc.vector.memset(w_rows[lo:hi, :].bitcast(I32), 0)
+        nc.vector.memset(plane0[:, WO_AT:].bitcast(I32), 0)
+        nc.vector.memset(plane1[:].bitcast(I32), 0)
+        one = keep.tile([P, 1], F32, name="one")
+        nc.vector.memset(one[:], 1.0)
+        warm = keep.tile([P, 1], F32, name="warm")
+        nc.scalar.activation(warm[:], one[:], ACT.Abs_reciprocal_sqrt)
+        nc.gpsimd.dma_start(plane0[0:16, WO_AT:].bitcast(I32), wo_scales[0].bitcast(I32))
+        wo_codes = keep.tile([P, 2 * N], U8, name="wo_codes", align_bytes=64)
+        nc.gpsimd.dma_start(wo_codes[:].bitcast(I32), wo_words[0].bitcast(I32))
+
+        w2_codes = keep.tile([P, PASSES, 2 * H], U8, name="w2_codes", align_bytes=64)
+        for a in range(PASSES):
+            nc.vector.tensor_copy(
+                w2_codes[:, a, :].bitcast(U16).rearrange("p (t b m) -> p b t m", t=PACK, m=8),
+                w2_raw[:, a, :].bitcast(U16).rearrange("p (b m t) -> p b t m", t=PACK, m=8),
+            )
+
+        picked_rows = keep.tile([P, S], U8, name="picked_rows", align_bytes=64)
+        nc.vector.tensor_copy(picked_rows[:], tab_rows[:].indirect(offsets[:]))
+        nc.vector.tensor_copy(
+            plane0[:, W2_AT:WO_AT].rearrange("p (w t b m) -> p w b t m", w=2, t=PACK, m=16),
+            w_rows[:].rearrange("p (w b m t) -> p w b t m", w=2, t=PACK, m=16),
+        )
+        nc.vector.tensor_copy(plane0[:, 0:S].bitcast(I32), picked_rows[:].bitcast(I32))
+        for quad in range(1, 4):
+            nc.scalar.dma_start(
+                plane0[32 * quad:32 * quad + 4, :].bitcast(I32), plane0[4 * quad:4 * quad + 4, :].bitcast(I32))
+        for quad in range(4):
+            queue = nc.scalar if quad < 2 else nc.gpsimd
+            queue.dma_start(
+                plane1[32 * quad:32 * quad + 4, :].bitcast(I32),
+                plane0[16 + 4 * quad:20 + 4 * quad, 0:WO_AT].bitcast(I32))
+
+        picked = {}
+        for a in range(PASSES):
+            for hf in range(2):
+                g = keep.tile([P, HALF], U32, name="picked%d%d" % (a, hf), align_bytes=64)
+                nc.vector.tensor_copy(g[:], tables[a][:].bitcast(U32).indirect(offsets[:, hf * 32:(hf + 1) * 32]))
+                picked[a, hf] = g
+            if a == 0:
+                w3_codes = keep.tile([P, PASSES, H], I32, name="w3_codes", align_bytes=64)
+                nc.vector.tensor_copy(
+                    w3_codes[:].rearrange("p a (t b m) -> p a b t m", t=PACK, m=4),
+                    w3_raw[:].rearrange("p a (b m t) -> p a b t m", t=PACK, m=4),
+                )
+
+
+        def table_product(out, codes, scales, a, col0, width):
+            hf, c = divmod(col0, HALF)
+            nc.tensor.matmul_mx(
+                out, lhsT=codes, lhsT_scale=scales,
+                rhs=picked[a, hf][:, c:c + width].bitcast(FP8X4),
+                rhs_scale=planes[a][:, col0:col0 + width],
+                start=(a == 0), stop=(a == PASSES - 1),
+            )
+
+        w1_v = w1.rearrange("(a p j) c -> a p j c", p=P, j=PACK)
+        w1_raw0 = big.tile([P, PACK, H], F32, name="w1_raw0", offset=0)
+        nc.sync.dma_start(w1_raw0[:], w1_v[0])
+        w1_raw1 = []
+        for s in range(2):
+            raw = big.tile([P, PACK, H // 2], F32, name="w1_raw1%d" % s, offset=(2 + s) * T)
+            nc.sync.dma_start(raw[:], w1_v[1][:, :, s * (H // 2):(s + 1) * (H // 2)])
+            w1_raw1.append(raw)
+        pe_v = pe.rearrange("(p t) j -> p t j", t=PACK)
+        pe0 = big.tile([P, PACK, HALF], F32, name="pe0", offset=4 * T)
+        nc.sync.dma_start(pe0[:], pe_v[:, :, 0:HALF])
+        wd_raw = big.tile([P, PASSES, PACK * N], F32, name="wd_raw", offset=6 * T)
+        nc.sync.dma_start(wd_raw[:], wd.rearrange("(a p j) n -> p a (j n)", p=P, j=PACK))
+
+        f2_banks = {}
+        for hf in range(2):
+            for t in range(PACK):
+                f2_banks[hf, t] = psum.tile([P, HALF], F32, name="bank")
+        for a in range(PASSES):
+            for hf in range(2):
+                for t in range(PACK):
+                    table_product(
+                        f2_banks[hf, t][:], w2_codes[:, a, 2 * P * t:2 * P * (t + 1)].bitcast(FP4X4),
+                        planes[a][:, W2_AT + P * t:W2_AT + P * (t + 1)], a, hf * HALF, HALF)
+
+        f2 = [keep.tile([P, PACK, HALF], F32, name="f2_%d" % hf) for hf in range(2)]
+        for t in range(PACK):
+            nc.scalar.copy(f2[0][:, t, :], f2_banks[0, t][:])
+
+        w1_bf = [keep.tile([P, PACK * H], BF16, name="w1_bf%d" % a, align_bytes=64) for a in range(PASSES)]
+        w1_codes = keep.tile([P, PASSES, H], I32, name="w1_codes", align_bytes=64)
+        w1_scales = keep.tile([P, PASSES, H], U8, name="w1_scales", align_bytes=64)
+
+        def dealt(a):
+            return w1_bf[a][:].rearrange("p (t m j) -> p m j t", t=PACK, j=PACK)
+
+        def by_column(raw):
+            return raw[:].rearrange("p j (m t) -> p m j t", t=PACK)
+
+        def quantise_w1(a):
+            for u in range(2):
+                nc.vector.quantize_mx(
+                    w1_codes[:, a, 256 * u:256 * (u + 1)].bitcast(FP8X4),
+                    w1_scales[:, a, 256 * u:256 * (u + 1)],
+                    w1_bf[a][:, 1024 * u:1024 * (u + 1)])
+
+        nc.vector.tensor_copy(dealt(0), by_column(w1_raw0))
+        nc.scalar.copy(dealt(1)[:, 0:64], by_column(w1_raw1[0]))
+        quantise_w1(0)
+        nc.vector.tensor_copy(dealt(1)[:, 64:128], by_column(w1_raw1[1]))
+        quantise_w1(1)
+        pe1 = big.tile([P, PACK, HALF], F32, name="pe1", offset=0)
+        nc.sync.dma_start(pe1[:], pe_v[:, :, HALF:])
+        pes = [pe0, pe1]
+
+        for t in range(PACK):
+            nc.scalar.copy(f2[1][:, t, :], f2_banks[1, t][:])
+
+        h_v = out_1.rearrange("(p t) j -> p t j", t=PACK)
+        y_v = out_0.rearrange("(n p) j -> p n j", p=P)
+        words_v = out_2[0].rearrange("p m t -> p (m t)").bitcast(I32)
+        h_codes = keep.tile([P, S], I32, name="h_codes", align_bytes=64)
+        h_scales = keep.tile([P, S], U8, name="h_scales", align_bytes=64)
+        wd_bf = keep.tile([P, PASSES * PACK * N], BF16, name="wd_bf", align_bytes=64)
+        wd_codes = keep.tile([P, PASSES * N], I32, name="wd_codes", align_bytes=64)
+        wd_scales = keep.tile([P, PASSES * N], U8, name="wd_scales", align_bytes=64)
+        h_tiles = {}
+        damp = {}
+        e_banks = {}
+
+        def make_h(q):
+            col0 = q * CHUNK
+            hf, c = divmod(col0, HALF)
+            h = keep.tile([P, PACK, CHUNK], F32, name="h%d" % q)
+            h_tiles[q] = h
+            for u in range(2):
+                f3_bank = psum.tile([P, 2, CHUNK], F32, name="bank")
+                f1_bank = psum.tile([P, 2, CHUNK], F32, name="bank")
+                for i in range(2):
+                    t = 2 * u + i
+                    for a in range(PASSES):
+                        table_product(
+                            f3_bank[:, i, :], w3_codes[:, a, P * t:P * (t + 1)].bitcast(FP8X4),
+                            planes[a][:, W3_AT + P * t:W3_AT + P * (t + 1)], a, col0, CHUNK)
+                for i in range(2):
+                    t = 2 * u + i
+                    for a in range(PASSES):
+                        table_product(
+                            f1_bank[:, i, :], w1_codes[:, a, P * t:P * (t + 1)].bitcast(FP8X4),
+                            w1_scales[:, a, P * t:P * (t + 1)], a, col0, CHUNK)
+                f3pe = ring.tile([P, 2, CHUNK], F32, name="f3pe")
+                nc.vector.tensor_tensor(f3pe[:], f3_bank[:], pes[hf][:, 2 * u:2 * u + 2, c:c + CHUNK], ALU.mult)
+                f1f2 = ring.tile([P, 2, CHUNK], F32, name="f1f2")
+                nc.vector.tensor_tensor(f1f2[:], f1_bank[:], f2[hf][:, 2 * u:2 * u + 2, c:c + CHUNK], ALU.mult)
+                eng = nc.vector if u == 1 else nc.gpsimd
+                eng.tensor_tensor(h[:, 2 * u:2 * u + 2, :], f1f2[:], f3pe[:], ALU.subtract)
+            nc.sync.dma_start(h_v[:, :, col0:col0 + CHUNK], h[:])
+
+        def quantise_h(q):
+            cols = slice(q * CHUNK, (q + 1) * CHUNK)
+            h_bf = ring.tile([P, PACK * CHUNK], BF16, name="h_bf", align_bytes=64)
+            dst = h_bf[:].rearrange("p (c i t) -> p c t i", t=PACK, i=4)
+            src = h_tiles[q][:].rearrange("p t (c i) -> p c t i", i=4)
+            if q == CHUNKS - 1:
+                nc.vector.tensor_copy(dst, src)
+            else:
+                nc.scalar.copy(dst, src)
+            nc.vector.quantize_mx(h_codes[:, cols].bitcast(FP8X4), h_scales[:, cols], h_bf[:])
+            nc.sync.dma_start(words_v[:, cols], h_codes[:, cols])
+            e_bank = psum.tile([P, 2, CHUNK], F32, name="bank")
+            e_banks[q] = e_bank
+            for n in range(2):
+                nc.tensor.matmul_mx(
+                    e_bank[:, n, :], lhsT=wo_codes[:, 2 * P * n:2 * P * (n + 1)].bitcast(FP4X4),
+                    lhsT_scale=plane0[:, WO_AT + P * n:WO_AT + P * (n + 1)],
+                    rhs=h_codes[:, cols].bitcast(FP8X4), rhs_scale=h_scales[:, cols],
+                    start=True, stop=True)
+
+        def quantise_wd():
+            for a in range(PASSES):
+                nc.scalar.copy(
+                    wd_bf[:, a * PACK * N:(a + 1) * PACK * N].rearrange("p (c i j) -> p c j i", j=PACK, i=4),
+                    wd_raw[:, a, :].rearrange("p (j c i) -> p c j i", j=PACK, i=4))
+            nc.vector.quantize_mx(wd_codes[:].bitcast(FP8X4), wd_scales[:], wd_bf[:])
+
+        def make_damp(q):
+            d_bank = psum.tile([P, 2, CHUNK], F32, name="bank")
+            for n in range(2):
+                for a in range(PASSES):
+                    at = slice(a * N + P * n, a * N + P * (n + 1))
+                    table_product(d_bank[:, n, :], wd_codes[:, at].bitcast(FP8X4), wd_scales[:, at], a, q * CHUNK, CHUNK)
+            d2 = ring.tile([P, 2, CHUNK], F32, name="d2")
+            nc.scalar.activation(d2[:], d_bank[:], ACT.Square)
+            damp[q] = keep.tile([P, 2, CHUNK], F32, name="damp%d" % q)
+            nc.scalar.activation(damp[q][:], d2[:], ACT.Abs_reciprocal_sqrt, bias=one[:])
+
+        def make_y(q):
+            y = keep.tile([P, 2, CHUNK], F32, name="y%d" % q)
+            nc.vector.tensor_tensor(y[:], e_banks[q][:], damp[q][:], ALU.mult)
+            nc.sync.dma_start(y_v[:, :, q * CHUNK:(q + 1) * CHUNK], y[:])
+
+        make_h(0)
+        make_h(1)
+        quantise_h(0)
+        quantise_wd()
+        make_damp(0)
+        make_h(2)
+        quantise_h(1)
+        make_damp(1)
+        make_y(0)
+        make_h(3)
+        quantise_h(2)
+        make_damp(2)
+        make_damp(3)
+        make_y(1)
+        quantise_h(3)
+        make_y(2)
+        for quad in range(4):
+            nc.scalar.dma_start(
+                out_3[0][4 * quad:4 * quad + 4, :].bitcast(I32), h_scales[32 * quad:32 * quad + 4, :].bitcast(I32))
+        make_y(3)

@@ -37,7 +37,8 @@ def tile_list_autofocus_phase_step_kernel(
         keep = ctx.enter_context(tc.tile_pool(name="keep", bufs=1))
         big = ctx.enter_context(tc.tile_pool(name="big", bufs=1))
         ring = ctx.enter_context(tc.tile_pool(name="ring", bufs=3))
-        psum = ctx.enter_context(tc.psum_pool(name="psum", bufs=8))
+        psum = ctx.enter_context(tc.psum_pool(name="psum", bufs=6))
+        psum_de = ctx.enter_context(tc.psum_pool(name="psum_de", bufs=1))
 
         offsets = lists.tile([P, S // 16], U16, name="offsets")
         nc.sync.dma_start(offsets[:], offs)
@@ -45,44 +46,43 @@ def tile_list_autofocus_phase_step_kernel(
         rows = PASSES * 16
         tab_rows = keep.tile([P, T], U8, name="tab_rows", align_bytes=64)
         w_rows = keep.tile([P, 2 * H], U8, name="w_rows", align_bytes=64)
-        plane0 = keep.tile([P, WO_AT + N], U8, name="plane0", align_bytes=64)
+        plane0 = keep.tile([P, WO_AT], U8, name="plane0", align_bytes=64)
         plane1 = keep.tile([P, WO_AT], U8, name="plane1", align_bytes=64)
         planes = [plane0, plane1]
         nc.sync.dma_start(tab_rows[0:rows, :].bitcast(I32), tab_scales.rearrange("a q c -> (a q) c").bitcast(I32))
         nc.sync.dma_start(w_rows[0:rows, 0:H].bitcast(I32), w2_scales.rearrange("a q c -> (a q) c").bitcast(I32))
         nc.sync.dma_start(w_rows[0:rows, H:].bitcast(I32), w3_scales.rearrange("a q c -> (a q) c").bitcast(I32))
-        w2_raw = keep.tile([P, PASSES, 2 * H], U8, name="w2_raw", align_bytes=64)
+        w2_raw = big.tile([P, PASSES, 2 * H], U8, name="w2_raw", align_bytes=64, offset=11 * T - 1024)
         nc.sync.dma_start(w2_raw[:].bitcast(I32), w2_words.rearrange("a p c -> p a c").bitcast(I32))
-        tables = []
-        for a in range(PASSES):
-            table = big.tile([P, T], I32, name="table%d" % a, offset=a * 4 * T)
-            nc.sync.dma_start(table[:], tab_words[a].rearrange("p t i -> p (t i)").bitcast(I32))
-            tables.append(table)
-            if a == 0:
-                w3_raw = keep.tile([P, PASSES, H], I32, name="w3_raw", align_bytes=64)
-                nc.sync.dma_start(w3_raw[:], w3_words.rearrange("a p c i -> p a (c i)").bitcast(I32))
+        tables = [big.tile([P, T], I32, name="table%d" % a, offset=a * 4 * T) for a in range(PASSES)]
+
+        def load_table(a):
+            nc.sync.dma_start(tables[a][:], tab_words[a].rearrange("p t i -> p (t i)").bitcast(I32))
+
+        load_table(0)
+        w3_raw = keep.tile([P, PASSES, H], I32, name="w3_raw", align_bytes=64)
+        nc.sync.dma_start(w3_raw[:], w3_words.rearrange("a p c i -> p a (c i)").bitcast(I32))
+        w1_v = w1.rearrange("(a p j) c -> a p j c", p=P, j=PACK)
+        w1_early = keep.tile([P, PACK, H // 2], F32, name="w1_early")
+        nc.sync.dma_start(w1_early[:], w1_v[1][:, :, 0:H // 2])
 
         for lo, hi in ((32, 64), (64, P)):
             nc.vector.memset(tab_rows[lo:hi, :].bitcast(I32), 0)
             nc.vector.memset(w_rows[lo:hi, :].bitcast(I32), 0)
-        nc.vector.memset(plane0[:, WO_AT:].bitcast(I32), 0)
+        wo_plane = keep.tile([P, N], U8, name="wo_plane", align_bytes=64)
+        nc.gpsimd.memset(wo_plane[:].bitcast(I32), 0)
         nc.vector.memset(plane1[:].bitcast(I32), 0)
         one = keep.tile([P, 1], F32, name="one")
         nc.vector.memset(one[:], 1.0)
         warm = keep.tile([P, 1], F32, name="warm")
         nc.scalar.activation(warm[:], one[:], ACT.Abs_reciprocal_sqrt)
-        nc.gpsimd.dma_start(plane0[0:16, WO_AT:].bitcast(I32), wo_scales[0].bitcast(I32))
+        for quad in range(4):
+            nc.gpsimd.dma_start(
+                wo_plane[32 * quad:32 * quad + 4, :].bitcast(I32), wo_scales[0][4 * quad:4 * quad + 4, :].bitcast(I32))
         wo_codes = keep.tile([P, 2 * N], U8, name="wo_codes", align_bytes=64)
         nc.gpsimd.dma_start(wo_codes[:].bitcast(I32), wo_words[0].bitcast(I32))
 
-        w2_codes = keep.tile([P, PASSES, 2 * H], U8, name="w2_codes", align_bytes=64)
-        for a in range(PASSES):
-            nc.vector.tensor_copy(
-                w2_codes[:, a, :].bitcast(U16).rearrange("p (t b m) -> p b t m", t=PACK, m=8),
-                w2_raw[:, a, :].bitcast(U16).rearrange("p (b m t) -> p b t m", t=PACK, m=8),
-            )
-
-        picked_rows = keep.tile([P, S], U8, name="picked_rows", align_bytes=64)
+        picked_rows = big.tile([P, S], U8, name="picked_rows", align_bytes=64, offset=8 * T - 512)
         nc.vector.tensor_copy(picked_rows[:], tab_rows[:].indirect(offsets[:]))
         nc.vector.tensor_copy(
             plane0[:, W2_AT:WO_AT].rearrange("p (w t b m) -> p w b t m", w=2, t=PACK, m=16),
@@ -90,13 +90,20 @@ def tile_list_autofocus_phase_step_kernel(
         )
         nc.vector.tensor_copy(plane0[:, 0:S].bitcast(I32), picked_rows[:].bitcast(I32))
         for quad in range(1, 4):
-            nc.scalar.dma_start(
+            nc.sync.dma_start(
                 plane0[32 * quad:32 * quad + 4, :].bitcast(I32), plane0[4 * quad:4 * quad + 4, :].bitcast(I32))
+        load_table(1)
         for quad in range(4):
-            queue = nc.scalar if quad < 2 else nc.gpsimd
-            queue.dma_start(
+            nc.sync.dma_start(
                 plane1[32 * quad:32 * quad + 4, :].bitcast(I32),
                 plane0[16 + 4 * quad:20 + 4 * quad, 0:WO_AT].bitcast(I32))
+
+        w2_codes = keep.tile([P, PASSES, 2 * H], U8, name="w2_codes", align_bytes=64)
+        for a in range(PASSES):
+            nc.vector.tensor_copy(
+                w2_codes[:, a, :].bitcast(U16).rearrange("p (t b m) -> p b t m", t=PACK, m=8),
+                w2_raw[:, a, :].bitcast(U16).rearrange("p (b m t) -> p b t m", t=PACK, m=8),
+            )
 
         picked = {}
         for a in range(PASSES):
@@ -121,36 +128,32 @@ def tile_list_autofocus_phase_step_kernel(
                 start=(a == 0), stop=(a == PASSES - 1),
             )
 
-        w1_v = w1.rearrange("(a p j) c -> a p j c", p=P, j=PACK)
-        w1_raw0 = big.tile([P, PACK, H], F32, name="w1_raw0", offset=0)
+        w1_raw0 = big.tile([P, PACK, H], F32, name="w1_raw0", offset=8 * T)
         nc.sync.dma_start(w1_raw0[:], w1_v[0])
-        w1_raw1 = []
-        for s in range(2):
-            raw = big.tile([P, PACK, H // 2], F32, name="w1_raw1%d" % s, offset=(2 + s) * T)
-            nc.sync.dma_start(raw[:], w1_v[1][:, :, s * (H // 2):(s + 1) * (H // 2)])
-            w1_raw1.append(raw)
+        w1_late = big.tile([P, PACK, H // 2], F32, name="w1_late", offset=10 * T)
+        nc.sync.dma_start(w1_late[:], w1_v[1][:, :, H // 2:])
         pe_v = pe.rearrange("(p t) j -> p t j", t=PACK)
-        pe0 = big.tile([P, PACK, HALF], F32, name="pe0", offset=4 * T)
+        pe0 = big.tile([P, PACK, HALF], F32, name="pe0", offset=0)
         nc.sync.dma_start(pe0[:], pe_v[:, :, 0:HALF])
-        wd_raw = big.tile([P, PASSES, PACK * N], F32, name="wd_raw", offset=6 * T)
+        wd_raw = big.tile([P, PASSES, PACK * N], F32, name="wd_raw", offset=4 * T)
         nc.sync.dma_start(wd_raw[:], wd.rearrange("(a p j) n -> p a (j n)", p=P, j=PACK))
 
-        f2_banks = {}
-        for hf in range(2):
-            for t in range(PACK):
-                f2_banks[hf, t] = psum.tile([P, HALF], F32, name="bank")
-        for a in range(PASSES):
-            for hf in range(2):
+        f2 = [keep.tile([P, PACK, HALF], F32, name="f2_%d" % hf) for hf in range(2)]
+
+        def make_f2(hf):
+            banks = [psum.tile([P, HALF], F32, name="bank") for t in range(PACK)]
+            for a in range(PASSES):
                 for t in range(PACK):
                     table_product(
-                        f2_banks[hf, t][:], w2_codes[:, a, 2 * P * t:2 * P * (t + 1)].bitcast(FP4X4),
+                        banks[t][:], w2_codes[:, a, 2 * P * t:2 * P * (t + 1)].bitcast(FP4X4),
                         planes[a][:, W2_AT + P * t:W2_AT + P * (t + 1)], a, hf * HALF, HALF)
+            for t in range(PACK):
+                nc.scalar.copy(f2[hf][:, t, :], banks[t][:])
 
-        f2 = [keep.tile([P, PACK, HALF], F32, name="f2_%d" % hf) for hf in range(2)]
-        for t in range(PACK):
-            nc.scalar.copy(f2[0][:, t, :], f2_banks[0, t][:])
 
-        w1_bf = [keep.tile([P, PACK * H], BF16, name="w1_bf%d" % a, align_bytes=64) for a in range(PASSES)]
+        w1_bf = [
+            big.tile([P, PACK * H], BF16, name="w1_bf%d" % a, align_bytes=64, offset=at)
+            for a, at in enumerate((6 * T, 12 * T + 1024))]
         w1_codes = keep.tile([P, PASSES, H], I32, name="w1_codes", align_bytes=64)
         w1_scales = keep.tile([P, PASSES, H], U8, name="w1_scales", align_bytes=64)
 
@@ -160,24 +163,24 @@ def tile_list_autofocus_phase_step_kernel(
         def by_column(raw):
             return raw[:].rearrange("p j (m t) -> p m j t", t=PACK)
 
-        def quantise_w1(a):
-            for u in range(2):
-                nc.vector.quantize_mx(
-                    w1_codes[:, a, 256 * u:256 * (u + 1)].bitcast(FP8X4),
-                    w1_scales[:, a, 256 * u:256 * (u + 1)],
-                    w1_bf[a][:, 1024 * u:1024 * (u + 1)])
+        def quantise_w1(a, u):
+            nc.vector.quantize_mx(
+                w1_codes[:, a, 256 * u:256 * (u + 1)].bitcast(FP8X4),
+                w1_scales[:, a, 256 * u:256 * (u + 1)],
+                w1_bf[a][:, 1024 * u:1024 * (u + 1)])
 
-        nc.vector.tensor_copy(dealt(0), by_column(w1_raw0))
-        nc.scalar.copy(dealt(1)[:, 0:64], by_column(w1_raw1[0]))
-        quantise_w1(0)
-        nc.vector.tensor_copy(dealt(1)[:, 64:128], by_column(w1_raw1[1]))
-        quantise_w1(1)
-        pe1 = big.tile([P, PACK, HALF], F32, name="pe1", offset=0)
+        nc.scalar.copy(dealt(1)[:, 0:64], by_column(w1_early))
+        nc.scalar.copy(dealt(0)[:, 64:128], by_column(w1_raw0)[:, 64:128])
+        make_f2(0)
+        nc.vector.tensor_copy(dealt(0)[:, 0:64], by_column(w1_raw0)[:, 0:64])
+        nc.vector.tensor_copy(dealt(1)[:, 64:128], by_column(w1_late))
+        for u in range(2):
+            for a in range(PASSES):
+                quantise_w1(a, u)
+
+        pe1 = big.tile([P, PACK, HALF], F32, name="pe1", offset=10 * T)
         nc.sync.dma_start(pe1[:], pe_v[:, :, HALF:])
         pes = [pe0, pe1]
-
-        for t in range(PACK):
-            nc.scalar.copy(f2[1][:, t, :], f2_banks[1, t][:])
 
         h_v = out_1.rearrange("(p t) j -> p t j", t=PACK)
         y_v = out_0.rearrange("(n p) j -> p n j", p=P)
@@ -211,11 +214,11 @@ def tile_list_autofocus_phase_step_kernel(
                         table_product(
                             f1_bank[:, i, :], w1_codes[:, a, P * t:P * (t + 1)].bitcast(FP8X4),
                             w1_scales[:, a, P * t:P * (t + 1)], a, col0, CHUNK)
-                f3pe = ring.tile([P, 2, CHUNK], F32, name="f3pe")
+                f3pe = big.tile([P, 2, CHUNK], F32, name="f3pe", bufs=3, offset=12 * T)
                 nc.vector.tensor_tensor(f3pe[:], f3_bank[:], pes[hf][:, 2 * u:2 * u + 2, c:c + CHUNK], ALU.mult)
                 f1f2 = ring.tile([P, 2, CHUNK], F32, name="f1f2")
                 nc.vector.tensor_tensor(f1f2[:], f1_bank[:], f2[hf][:, 2 * u:2 * u + 2, c:c + CHUNK], ALU.mult)
-                eng = nc.vector if u == 1 else nc.gpsimd
+                eng = nc.vector if q == CHUNKS - 1 and u == 1 else nc.gpsimd
                 eng.tensor_tensor(h[:, 2 * u:2 * u + 2, :], f1f2[:], f3pe[:], ALU.subtract)
             nc.sync.dma_start(h_v[:, :, col0:col0 + CHUNK], h[:])
 
@@ -230,12 +233,15 @@ def tile_list_autofocus_phase_step_kernel(
                 nc.scalar.copy(dst, src)
             nc.vector.quantize_mx(h_codes[:, cols].bitcast(FP8X4), h_scales[:, cols], h_bf[:])
             nc.sync.dma_start(words_v[:, cols], h_codes[:, cols])
-            e_bank = psum.tile([P, 2, CHUNK], F32, name="bank")
+
+        def make_e(q):
+            cols = slice(q * CHUNK, (q + 1) * CHUNK)
+            e_bank = psum_de.tile([P, 2, CHUNK], F32, name="e_bank")
             e_banks[q] = e_bank
             for n in range(2):
                 nc.tensor.matmul_mx(
                     e_bank[:, n, :], lhsT=wo_codes[:, 2 * P * n:2 * P * (n + 1)].bitcast(FP4X4),
-                    lhsT_scale=plane0[:, WO_AT + P * n:WO_AT + P * (n + 1)],
+                    lhsT_scale=wo_plane[:, P * n:P * (n + 1)],
                     rhs=h_codes[:, cols].bitcast(FP8X4), rhs_scale=h_scales[:, cols],
                     start=True, stop=True)
 
@@ -247,7 +253,7 @@ def tile_list_autofocus_phase_step_kernel(
             nc.vector.quantize_mx(wd_codes[:].bitcast(FP8X4), wd_scales[:], wd_bf[:])
 
         def make_damp(q):
-            d_bank = psum.tile([P, 2, CHUNK], F32, name="bank")
+            d_bank = psum_de.tile([P, 2, CHUNK], F32, name="d_bank")
             for n in range(2):
                 for a in range(PASSES):
                     at = slice(a * N + P * n, a * N + P * (n + 1))
@@ -263,21 +269,26 @@ def tile_list_autofocus_phase_step_kernel(
             nc.sync.dma_start(y_v[:, :, q * CHUNK:(q + 1) * CHUNK], y[:])
 
         make_h(0)
-        make_h(1)
-        quantise_h(0)
+        make_f2(1)
         quantise_wd()
         make_damp(0)
-        make_h(2)
-        quantise_h(1)
+        make_h(1)
+        quantise_h(0)
+        make_e(0)
         make_damp(1)
         make_y(0)
+        make_h(2)
+        quantise_h(1)
+        make_e(1)
+        make_damp(2)
+        make_y(1)
+        make_damp(3)
         make_h(3)
         quantise_h(2)
-        make_damp(2)
-        make_damp(3)
-        make_y(1)
-        quantise_h(3)
+        make_e(2)
         make_y(2)
+        quantise_h(3)
+        make_e(3)
         for quad in range(4):
             nc.scalar.dma_start(
                 out_3[0][4 * quad:4 * quad + 4, :].bitcast(I32), h_scales[32 * quad:32 * quad + 4, :].bitcast(I32))

@@ -52,7 +52,7 @@ def tile_list_autofocus_phase_step_kernel(
         nc.sync.dma_start(tab_rows[0:rows, :].bitcast(I32), tab_scales.rearrange("a q c -> (a q) c").bitcast(I32))
         nc.sync.dma_start(w_rows[0:rows, 0:H].bitcast(I32), w2_scales.rearrange("a q c -> (a q) c").bitcast(I32))
         nc.sync.dma_start(w_rows[0:rows, H:].bitcast(I32), w3_scales.rearrange("a q c -> (a q) c").bitcast(I32))
-        w2_raw = big.tile([P, PASSES, 2 * H], U8, name="w2_raw", align_bytes=64, offset=11 * T - 1024)
+        w2_raw = keep.tile([P, PASSES, 2 * H], U8, name="w2_raw", align_bytes=64)
         nc.sync.dma_start(w2_raw[:].bitcast(I32), w2_words.rearrange("a p c -> p a c").bitcast(I32))
         tables = [big.tile([P, T], I32, name="table%d" % a, offset=a * 4 * T) for a in range(PASSES)]
 
@@ -63,24 +63,17 @@ def tile_list_autofocus_phase_step_kernel(
         w3_raw = keep.tile([P, PASSES, H], I32, name="w3_raw", align_bytes=64)
         nc.sync.dma_start(w3_raw[:], w3_words.rearrange("a p c i -> p a (c i)").bitcast(I32))
         w1_v = w1.rearrange("(a p j) c -> a p j c", p=P, j=PACK)
-        w1_early = keep.tile([P, PACK, H // 2], F32, name="w1_early")
-        nc.sync.dma_start(w1_early[:], w1_v[1][:, :, 0:H // 2])
+        w1_raw1 = keep.tile([P, PACK, H], F32, name="w1_raw1")
+        nc.sync.dma_start(w1_raw1[:], w1_v[1])
 
         for lo, hi in ((32, 64), (64, P)):
             nc.vector.memset(tab_rows[lo:hi, :].bitcast(I32), 0)
             nc.vector.memset(w_rows[lo:hi, :].bitcast(I32), 0)
-        wo_plane = keep.tile([P, N], U8, name="wo_plane", align_bytes=64)
-        nc.gpsimd.memset(wo_plane[:].bitcast(I32), 0)
         nc.vector.memset(plane1[:].bitcast(I32), 0)
         one = keep.tile([P, 1], F32, name="one")
         nc.vector.memset(one[:], 1.0)
         warm = keep.tile([P, 1], F32, name="warm")
         nc.scalar.activation(warm[:], one[:], ACT.Abs_reciprocal_sqrt)
-        for quad in range(4):
-            nc.gpsimd.dma_start(
-                wo_plane[32 * quad:32 * quad + 4, :].bitcast(I32), wo_scales[0][4 * quad:4 * quad + 4, :].bitcast(I32))
-        wo_codes = keep.tile([P, 2 * N], U8, name="wo_codes", align_bytes=64)
-        nc.gpsimd.dma_start(wo_codes[:].bitcast(I32), wo_words[0].bitcast(I32))
 
         picked_rows = big.tile([P, S], U8, name="picked_rows", align_bytes=64, offset=8 * T - 512)
         nc.vector.tensor_copy(picked_rows[:], tab_rows[:].indirect(offsets[:]))
@@ -112,7 +105,7 @@ def tile_list_autofocus_phase_step_kernel(
                 nc.vector.tensor_copy(g[:], tables[a][:].bitcast(U32).indirect(offsets[:, hf * 32:(hf + 1) * 32]))
                 picked[a, hf] = g
             if a == 0:
-                w3_codes = keep.tile([P, PASSES, H], I32, name="w3_codes", align_bytes=64)
+                w3_codes = big.tile([P, PASSES, H], I32, name="w3_codes", align_bytes=64, offset=2 * T)
                 nc.vector.tensor_copy(
                     w3_codes[:].rearrange("p a (t b m) -> p a b t m", t=PACK, m=4),
                     w3_raw[:].rearrange("p a (b m t) -> p a b t m", t=PACK, m=4),
@@ -130,13 +123,19 @@ def tile_list_autofocus_phase_step_kernel(
 
         w1_raw0 = big.tile([P, PACK, H], F32, name="w1_raw0", offset=8 * T)
         nc.sync.dma_start(w1_raw0[:], w1_v[0])
-        w1_late = big.tile([P, PACK, H // 2], F32, name="w1_late", offset=10 * T)
-        nc.sync.dma_start(w1_late[:], w1_v[1][:, :, H // 2:])
         pe_v = pe.rearrange("(p t) j -> p t j", t=PACK)
         pe0 = big.tile([P, PACK, HALF], F32, name="pe0", offset=0)
         nc.sync.dma_start(pe0[:], pe_v[:, :, 0:HALF])
         wd_raw = big.tile([P, PASSES, PACK * N], F32, name="wd_raw", offset=4 * T)
         nc.sync.dma_start(wd_raw[:], wd.rearrange("(a p j) n -> p a (j n)", p=P, j=PACK))
+
+        wo_codes = big.tile([P, 2 * N], U8, name="wo_codes", align_bytes=64, offset=7 * T + 2048)
+        nc.sync.dma_start(wo_codes[:].bitcast(I32), wo_words[0].bitcast(I32))
+        wo_plane = big.tile([P, N], U8, name="wo_plane", align_bytes=64, offset=7 * T + 2560)
+        nc.gpsimd.memset(wo_plane[:].bitcast(I32), 0)
+        for quad in range(4):
+            nc.sync.dma_start(
+                wo_plane[32 * quad:32 * quad + 4, :].bitcast(I32), wo_scales[0][4 * quad:4 * quad + 4, :].bitcast(I32))
 
         f2 = [keep.tile([P, PACK, HALF], F32, name="f2_%d" % hf) for hf in range(2)]
 
@@ -153,8 +152,10 @@ def tile_list_autofocus_phase_step_kernel(
 
         w1_bf = [
             big.tile([P, PACK * H], BF16, name="w1_bf%d" % a, align_bytes=64, offset=at)
-            for a, at in enumerate((6 * T, 12 * T + 1024))]
-        w1_codes = keep.tile([P, PASSES, H], I32, name="w1_codes", align_bytes=64)
+            for a, at in enumerate((6 * T + 1024, 10 * T))]
+        w1_codes = [
+            big.tile([P, H], I32, name="w1_codes%d" % a, align_bytes=64, offset=at)
+            for a, at in enumerate((11 * T, 3 * T))]
         w1_scales = keep.tile([P, PASSES, H], U8, name="w1_scales", align_bytes=64)
 
         def dealt(a):
@@ -165,20 +166,20 @@ def tile_list_autofocus_phase_step_kernel(
 
         def quantise_w1(a, u):
             nc.vector.quantize_mx(
-                w1_codes[:, a, 256 * u:256 * (u + 1)].bitcast(FP8X4),
+                w1_codes[a][:, 256 * u:256 * (u + 1)].bitcast(FP8X4),
                 w1_scales[:, a, 256 * u:256 * (u + 1)],
                 w1_bf[a][:, 1024 * u:1024 * (u + 1)])
 
-        nc.scalar.copy(dealt(1)[:, 0:64], by_column(w1_early))
+        nc.scalar.copy(dealt(1), by_column(w1_raw1))
+        for u in range(2):
+            quantise_w1(1, u)
         nc.scalar.copy(dealt(0)[:, 64:128], by_column(w1_raw0)[:, 64:128])
         make_f2(0)
         nc.vector.tensor_copy(dealt(0)[:, 0:64], by_column(w1_raw0)[:, 0:64])
-        nc.vector.tensor_copy(dealt(1)[:, 64:128], by_column(w1_late))
         for u in range(2):
-            for a in range(PASSES):
-                quantise_w1(a, u)
+            quantise_w1(0, u)
 
-        pe1 = big.tile([P, PACK, HALF], F32, name="pe1", offset=10 * T)
+        pe1 = big.tile([P, PACK, HALF], F32, name="pe1", offset=8 * T)
         nc.sync.dma_start(pe1[:], pe_v[:, :, HALF:])
         pes = [pe0, pe1]
 
@@ -194,49 +195,62 @@ def tile_list_autofocus_phase_step_kernel(
         damp = {}
         e_banks = {}
 
-        def make_h(q):
+        def make_products(q, u):
             col0 = q * CHUNK
             hf, c = divmod(col0, HALF)
-            h = keep.tile([P, PACK, CHUNK], F32, name="h%d" % q)
-            h_tiles[q] = h
-            for u in range(2):
-                f3_bank = psum.tile([P, 2, CHUNK], F32, name="bank")
-                f1_bank = psum.tile([P, 2, CHUNK], F32, name="bank")
-                for i in range(2):
-                    t = 2 * u + i
-                    for a in range(PASSES):
-                        table_product(
-                            f3_bank[:, i, :], w3_codes[:, a, P * t:P * (t + 1)].bitcast(FP8X4),
-                            planes[a][:, W3_AT + P * t:W3_AT + P * (t + 1)], a, col0, CHUNK)
-                for i in range(2):
-                    t = 2 * u + i
-                    for a in range(PASSES):
-                        table_product(
-                            f1_bank[:, i, :], w1_codes[:, a, P * t:P * (t + 1)].bitcast(FP8X4),
-                            w1_scales[:, a, P * t:P * (t + 1)], a, col0, CHUNK)
-                f3pe = big.tile([P, 2, CHUNK], F32, name="f3pe", bufs=3, offset=12 * T)
-                nc.vector.tensor_tensor(f3pe[:], f3_bank[:], pes[hf][:, 2 * u:2 * u + 2, c:c + CHUNK], ALU.mult)
-                f1f2 = ring.tile([P, 2, CHUNK], F32, name="f1f2")
-                nc.vector.tensor_tensor(f1f2[:], f1_bank[:], f2[hf][:, 2 * u:2 * u + 2, c:c + CHUNK], ALU.mult)
-                eng = nc.vector if q == CHUNKS - 1 and u == 1 else nc.gpsimd
-                eng.tensor_tensor(h[:, 2 * u:2 * u + 2, :], f1f2[:], f3pe[:], ALU.subtract)
-            nc.sync.dma_start(h_v[:, :, col0:col0 + CHUNK], h[:])
+            if q < CHUNKS - 1:
+                ts, lo, width = range(2 * u, 2 * u + 2), 0, CHUNK
+            else:
+                ts, lo, width = range(PACK), u * CHUNK // 2, CHUNK // 2
+            f3_bank = psum.tile([P, len(ts), width], F32, name="bank")
+            f1_bank = psum.tile([P, len(ts), width], F32, name="bank")
+            for i, t in enumerate(ts):
+                for a in range(PASSES):
+                    table_product(
+                        f3_bank[:, i, :], w3_codes[:, a, P * t:P * (t + 1)].bitcast(FP8X4),
+                        planes[a][:, W3_AT + P * t:W3_AT + P * (t + 1)], a, col0 + lo, width)
+            for i, t in enumerate(ts):
+                for a in range(PASSES):
+                    table_product(
+                        f1_bank[:, i, :], w1_codes[a][:, P * t:P * (t + 1)].bitcast(FP8X4),
+                        w1_scales[:, a, P * t:P * (t + 1)], a, col0 + lo, width)
+            part = (slice(None), slice(ts.start, ts.stop), slice(c + lo, c + lo + width))
+            f3pe = big.tile([P, len(ts), width], F32, name="f3pe", bufs=3, offset=6 * T)
+            nc.vector.tensor_tensor(f3pe[:], f3_bank[:], pes[hf][part], ALU.mult)
+            f1f2 = ring.tile([P, len(ts), width], F32, name="f1f2")
+            nc.vector.tensor_tensor(f1f2[:], f1_bank[:], f2[hf][part], ALU.mult)
+            if q < CHUNKS - 1:
+                return h_tiles[q][0][:, ts.start:ts.stop, :], f1f2[:], f3pe[:]
+            return h_tiles[q][u][:], f1f2[:], f3pe[:]
+
+        def make_h(q):
+            parts = 1 if q < CHUNKS - 1 else 2
+            h_tiles[q] = [keep.tile([P, PACK, CHUNK // parts], F32, name="h%d_%d" % (q, s)) for s in range(parts)]
+            nc.gpsimd.tensor_tensor(*make_products(q, 0), ALU.subtract)
+            second = make_products(q, 1)
+            if q >= 2:
+                make_y(q - 2)
+            nc.vector.tensor_tensor(*second, ALU.subtract)
+            for s in range(parts):
+                col0 = q * CHUNK + s * CHUNK // 2
+                nc.sync.dma_start(h_v[:, :, col0:col0 + CHUNK // parts], h_tiles[q][s][:])
 
         def quantise_h(q):
             cols = slice(q * CHUNK, (q + 1) * CHUNK)
             h_bf = ring.tile([P, PACK * CHUNK], BF16, name="h_bf", align_bytes=64)
             dst = h_bf[:].rearrange("p (c i t) -> p c t i", t=PACK, i=4)
-            src = h_tiles[q][:].rearrange("p t (c i) -> p c t i", i=4)
+            src = [part[:].rearrange("p t (c i) -> p c t i", i=4) for part in h_tiles[q]]
             if q == CHUNKS - 1:
-                nc.vector.tensor_copy(dst, src)
+                nc.scalar.copy(dst[:, 0:32], src[0])
+                nc.vector.tensor_copy(dst[:, 32:64], src[1])
             else:
-                nc.scalar.copy(dst, src)
+                nc.scalar.copy(dst, src[0])
             nc.vector.quantize_mx(h_codes[:, cols].bitcast(FP8X4), h_scales[:, cols], h_bf[:])
             nc.sync.dma_start(words_v[:, cols], h_codes[:, cols])
 
         def make_e(q):
             cols = slice(q * CHUNK, (q + 1) * CHUNK)
-            e_bank = psum_de.tile([P, 2, CHUNK], F32, name="e_bank")
+            e_bank = psum_de.tile([P, 2, CHUNK], F32, name="e_bank", tag="e_bank" if q < CHUNKS - 1 else "d_bank")
             e_banks[q] = e_bank
             for n in range(2):
                 nc.tensor.matmul_mx(
@@ -253,7 +267,7 @@ def tile_list_autofocus_phase_step_kernel(
             nc.vector.quantize_mx(wd_codes[:].bitcast(FP8X4), wd_scales[:], wd_bf[:])
 
         def make_damp(q):
-            d_bank = psum_de.tile([P, 2, CHUNK], F32, name="d_bank")
+            d_bank = psum_de.tile([P, 2, CHUNK], F32, name="d_bank", tag="d_bank")
             for n in range(2):
                 for a in range(PASSES):
                     at = slice(a * N + P * n, a * N + P * (n + 1))
@@ -270,25 +284,23 @@ def tile_list_autofocus_phase_step_kernel(
 
         make_h(0)
         make_f2(1)
-        quantise_wd()
-        make_damp(0)
         make_h(1)
         quantise_h(0)
         make_e(0)
+        quantise_wd()
+        make_damp(0)
         make_damp(1)
-        make_y(0)
         make_h(2)
         quantise_h(1)
         make_e(1)
         make_damp(2)
-        make_y(1)
         make_damp(3)
         make_h(3)
         quantise_h(2)
         make_e(2)
-        make_y(2)
         quantise_h(3)
         make_e(3)
+        make_y(2)
         for quad in range(4):
             nc.scalar.dma_start(
                 out_3[0][4 * quad:4 * quad + 4, :].bitcast(I32), h_scales[32 * quad:32 * quad + 4, :].bitcast(I32))

@@ -159,10 +159,10 @@ def tile_list_autofocus_phase_step_kernel(
         w1_scales = keep.tile([P, PASSES, H], U8, name="w1_scales", align_bytes=64)
 
         def dealt(a):
-            return w1_bf[a][:].rearrange("p (t m j) -> p m j t", t=PACK, j=PACK)
+            return w1_bf[a][:].rearrange("p (t m j) -> p m t j", t=PACK, j=PACK)
 
         def by_column(raw):
-            return raw[:].rearrange("p j (m t) -> p m j t", t=PACK)
+            return raw[:].rearrange("p j (m t) -> p m t j", t=PACK)
 
         def quantise_w1(a, u):
             nc.vector.quantize_mx(
@@ -173,9 +173,8 @@ def tile_list_autofocus_phase_step_kernel(
         nc.scalar.copy(dealt(1), by_column(w1_raw1))
         for u in range(2):
             quantise_w1(1, u)
-        nc.scalar.copy(dealt(0)[:, 64:128], by_column(w1_raw0)[:, 64:128])
         make_f2(0)
-        nc.vector.tensor_copy(dealt(0)[:, 0:64], by_column(w1_raw0)[:, 0:64])
+        nc.vector.tensor_copy(dealt(0), by_column(w1_raw0))
         for u in range(2):
             quantise_w1(0, u)
 
@@ -192,6 +191,7 @@ def tile_list_autofocus_phase_step_kernel(
         wd_codes = keep.tile([P, PASSES * N], I32, name="wd_codes", align_bytes=64)
         wd_scales = keep.tile([P, PASSES * N], U8, name="wd_scales", align_bytes=64)
         h_tiles = {}
+        h_bf = {}
         damp = {}
         e_banks = {}
 
@@ -227,25 +227,35 @@ def tile_list_autofocus_phase_step_kernel(
             parts = 1 if q < CHUNKS - 1 else 2
             h_tiles[q] = [keep.tile([P, PACK, CHUNK // parts], F32, name="h%d_%d" % (q, s)) for s in range(parts)]
             nc.gpsimd.tensor_tensor(*make_products(q, 0), ALU.subtract)
+            if q >= 2:
+                quantise_h(q - 2)
+                make_e(q - 2)
             second = make_products(q, 1)
             if q >= 2:
                 make_y(q - 2)
-            nc.vector.tensor_tensor(*second, ALU.subtract)
+            if q < CHUNKS - 1:
+                nc.gpsimd.tensor_tensor(*second, ALU.subtract)
+            else:
+                quantise_h(q - 1)
+                make_e(q - 1)
+                nc.vector.tensor_tensor(*second, ALU.subtract)
             for s in range(parts):
                 col0 = q * CHUNK + s * CHUNK // 2
                 nc.sync.dma_start(h_v[:, :, col0:col0 + CHUNK // parts], h_tiles[q][s][:])
 
-        def quantise_h(q):
-            cols = slice(q * CHUNK, (q + 1) * CHUNK)
-            h_bf = ring.tile([P, PACK * CHUNK], BF16, name="h_bf", align_bytes=64)
-            dst = h_bf[:].rearrange("p (c i t) -> p c t i", t=PACK, i=4)
+        def round_h(q):
+            h_bf[q] = ring.tile([P, PACK * CHUNK], BF16, name="h_bf", align_bytes=64)
+            dst = h_bf[q][:].rearrange("p (c i t) -> p c t i", t=PACK, i=4)
             src = [part[:].rearrange("p t (c i) -> p c t i", i=4) for part in h_tiles[q]]
             if q == CHUNKS - 1:
                 nc.scalar.copy(dst[:, 0:32], src[0])
                 nc.vector.tensor_copy(dst[:, 32:64], src[1])
             else:
                 nc.scalar.copy(dst, src[0])
-            nc.vector.quantize_mx(h_codes[:, cols].bitcast(FP8X4), h_scales[:, cols], h_bf[:])
+
+        def quantise_h(q):
+            cols = slice(q * CHUNK, (q + 1) * CHUNK)
+            nc.vector.quantize_mx(h_codes[:, cols].bitcast(FP8X4), h_scales[:, cols], h_bf[q][:])
             nc.sync.dma_start(words_v[:, cols], h_codes[:, cols])
 
         def make_e(q):
@@ -284,23 +294,21 @@ def tile_list_autofocus_phase_step_kernel(
 
         make_h(0)
         make_f2(1)
+        round_h(0)
         make_h(1)
-        quantise_h(0)
-        make_e(0)
         quantise_wd()
         make_damp(0)
+        round_h(1)
         make_damp(1)
         make_h(2)
-        quantise_h(1)
-        make_e(1)
+        round_h(2)
         make_damp(2)
         make_damp(3)
         make_h(3)
-        quantise_h(2)
-        make_e(2)
+        make_y(2)
+        round_h(3)
         quantise_h(3)
         make_e(3)
-        make_y(2)
         for quad in range(4):
             nc.scalar.dma_start(
                 out_3[0][4 * quad:4 * quad + 4, :].bitcast(I32), h_scales[32 * quad:32 * quad + 4, :].bitcast(I32))

@@ -19,12 +19,31 @@ ACT = mybir.ActivationFunctionType
 P = 128
 PACK = 4
 PASSES = K // (P * PACK)
+QUADS = 4
+BLOCKS = 16
 HALF = S // 2
 CHUNK = 256
 CHUNKS = S // CHUNK
+RUN = 2
+LAG = 2
+
 W2_AT = S
 W3_AT = S + H
-WO_AT = S + 2 * H
+PLANE_WIDTH = S + 2 * H
+
+KIB = 1024
+TABLE_AT = (0, 16 * KIB)
+PICKED_ROWS_AT = 32 * KIB - 512
+W1_RAW0_AT = 32 * KIB
+PE0_AT = 0
+W3_CODES_AT = 8 * KIB
+W1_CODES_AT = (44 * KIB, 12 * KIB)
+WD_RAW_AT = 16 * KIB
+W1_BF_AT = (25 * KIB, 40 * KIB)
+F3PE_AT = 24 * KIB
+WO_CODES_AT = 30 * KIB
+WO_PLANE_AT = 30 * KIB + 512
+PE1_AT = 32 * KIB
 
 
 def tile_list_autofocus_phase_step_kernel(
@@ -43,18 +62,18 @@ def tile_list_autofocus_phase_step_kernel(
         offsets = lists.tile([P, S // 16], U16, name="offsets")
         nc.sync.dma_start(offsets[:], offs)
 
-        rows = PASSES * 16
+        rows = PASSES * BLOCKS
         tab_rows = keep.tile([P, T], U8, name="tab_rows", align_bytes=64)
         w_rows = keep.tile([P, 2 * H], U8, name="w_rows", align_bytes=64)
-        plane0 = keep.tile([P, WO_AT], U8, name="plane0", align_bytes=64)
-        plane1 = keep.tile([P, WO_AT], U8, name="plane1", align_bytes=64)
+        plane0 = keep.tile([P, PLANE_WIDTH], U8, name="plane0", align_bytes=64)
+        plane1 = keep.tile([P, PLANE_WIDTH], U8, name="plane1", align_bytes=64)
         planes = [plane0, plane1]
         nc.sync.dma_start(tab_rows[0:rows, :].bitcast(I32), tab_scales.rearrange("a q c -> (a q) c").bitcast(I32))
         nc.sync.dma_start(w_rows[0:rows, 0:H].bitcast(I32), w2_scales.rearrange("a q c -> (a q) c").bitcast(I32))
         nc.sync.dma_start(w_rows[0:rows, H:].bitcast(I32), w3_scales.rearrange("a q c -> (a q) c").bitcast(I32))
         w2_raw = keep.tile([P, PASSES, 2 * H], U8, name="w2_raw", align_bytes=64)
         nc.sync.dma_start(w2_raw[:].bitcast(I32), w2_words.rearrange("a p c -> p a c").bitcast(I32))
-        tables = [big.tile([P, T], I32, name="table%d" % a, offset=a * 4 * T) for a in range(PASSES)]
+        tables = [big.tile([P, T], I32, name="table%d" % a, offset=TABLE_AT[a]) for a in range(PASSES)]
 
         def load_table(a):
             nc.sync.dma_start(tables[a][:], tab_words[a].rearrange("p t i -> p (t i)").bitcast(I32))
@@ -72,24 +91,24 @@ def tile_list_autofocus_phase_step_kernel(
         nc.vector.memset(plane1[:].bitcast(I32), 0)
         one = keep.tile([P, 1], F32, name="one")
         nc.vector.memset(one[:], 1.0)
-        warm = keep.tile([P, 1], F32, name="warm")
-        nc.scalar.activation(warm[:], one[:], ACT.Abs_reciprocal_sqrt)
+        root_one = keep.tile([P, 1], F32, name="root_one")
+        nc.scalar.activation(root_one[:], one[:], ACT.Abs_reciprocal_sqrt)
 
-        picked_rows = big.tile([P, S], U8, name="picked_rows", align_bytes=64, offset=8 * T - 512)
+        picked_rows = big.tile([P, S], U8, name="picked_rows", align_bytes=64, offset=PICKED_ROWS_AT)
         nc.vector.tensor_copy(picked_rows[:], tab_rows[:].indirect(offsets[:]))
         nc.vector.tensor_copy(
-            plane0[:, W2_AT:WO_AT].rearrange("p (w t b m) -> p w b t m", w=2, t=PACK, m=16),
+            plane0[:, W2_AT:PLANE_WIDTH].rearrange("p (w t b m) -> p w b t m", w=2, t=PACK, m=16),
             w_rows[:].rearrange("p (w b m t) -> p w b t m", w=2, t=PACK, m=16),
         )
         nc.vector.tensor_copy(plane0[:, 0:S].bitcast(I32), picked_rows[:].bitcast(I32))
-        for quad in range(1, 4):
+        for quad in range(1, QUADS):
             nc.sync.dma_start(
                 plane0[32 * quad:32 * quad + 4, :].bitcast(I32), plane0[4 * quad:4 * quad + 4, :].bitcast(I32))
         load_table(1)
-        for quad in range(4):
+        for quad in range(QUADS):
             nc.sync.dma_start(
                 plane1[32 * quad:32 * quad + 4, :].bitcast(I32),
-                plane0[16 + 4 * quad:20 + 4 * quad, 0:WO_AT].bitcast(I32))
+                plane0[BLOCKS + 4 * quad:BLOCKS + 4 * quad + 4, 0:PLANE_WIDTH].bitcast(I32))
 
         w2_codes = keep.tile([P, PASSES, 2 * H], U8, name="w2_codes", align_bytes=64)
         for a in range(PASSES):
@@ -99,18 +118,21 @@ def tile_list_autofocus_phase_step_kernel(
             )
 
         picked = {}
-        for a in range(PASSES):
-            for hf in range(2):
-                g = keep.tile([P, HALF], U32, name="picked%d%d" % (a, hf), align_bytes=64)
-                nc.vector.tensor_copy(g[:], tables[a][:].bitcast(U32).indirect(offsets[:, hf * 32:(hf + 1) * 32]))
-                picked[a, hf] = g
-            if a == 0:
-                w3_codes = big.tile([P, PASSES, H], I32, name="w3_codes", align_bytes=64, offset=2 * T)
-                nc.vector.tensor_copy(
-                    w3_codes[:].rearrange("p a (t b m) -> p a b t m", t=PACK, m=4),
-                    w3_raw[:].rearrange("p a (b m t) -> p a b t m", t=PACK, m=4),
-                )
 
+        def gather_words(a):
+            columns = HALF // 16
+            for hf in range(2):
+                picked[a, hf] = keep.tile([P, HALF], U32, name="picked%d%d" % (a, hf), align_bytes=64)
+                nc.vector.tensor_copy(
+                    picked[a, hf][:], tables[a][:].bitcast(U32).indirect(offsets[:, hf * columns:(hf + 1) * columns]))
+
+        gather_words(0)
+        w3_codes = big.tile([P, PASSES, H], I32, name="w3_codes", align_bytes=64, offset=W3_CODES_AT)
+        nc.vector.tensor_copy(
+            w3_codes[:].rearrange("p a (t b m) -> p a b t m", t=PACK, m=4),
+            w3_raw[:].rearrange("p a (b m t) -> p a b t m", t=PACK, m=4),
+        )
+        gather_words(1)
 
         def table_product(out, codes, scales, a, col0, width):
             hf, c = divmod(col0, HALF)
@@ -121,19 +143,19 @@ def tile_list_autofocus_phase_step_kernel(
                 start=(a == 0), stop=(a == PASSES - 1),
             )
 
-        w1_raw0 = big.tile([P, PACK, H], F32, name="w1_raw0", offset=8 * T)
+        w1_raw0 = big.tile([P, PACK, H], F32, name="w1_raw0", offset=W1_RAW0_AT)
         nc.sync.dma_start(w1_raw0[:], w1_v[0])
         pe_v = pe.rearrange("(p t) j -> p t j", t=PACK)
-        pe0 = big.tile([P, PACK, HALF], F32, name="pe0", offset=0)
+        pe0 = big.tile([P, PACK, HALF], F32, name="pe0", offset=PE0_AT)
         nc.sync.dma_start(pe0[:], pe_v[:, :, 0:HALF])
-        wd_raw = big.tile([P, PASSES, PACK * N], F32, name="wd_raw", offset=4 * T)
+        wd_raw = big.tile([P, PASSES, PACK * N], F32, name="wd_raw", offset=WD_RAW_AT)
         nc.sync.dma_start(wd_raw[:], wd.rearrange("(a p j) n -> p a (j n)", p=P, j=PACK))
 
-        wo_codes = big.tile([P, 2 * N], U8, name="wo_codes", align_bytes=64, offset=7 * T + 2048)
+        wo_codes = big.tile([P, 2 * N], U8, name="wo_codes", align_bytes=64, offset=WO_CODES_AT)
         nc.sync.dma_start(wo_codes[:].bitcast(I32), wo_words[0].bitcast(I32))
-        wo_plane = big.tile([P, N], U8, name="wo_plane", align_bytes=64, offset=7 * T + 2560)
+        wo_plane = big.tile([P, N], U8, name="wo_plane", align_bytes=64, offset=WO_PLANE_AT)
         nc.gpsimd.memset(wo_plane[:].bitcast(I32), 0)
-        for quad in range(4):
+        for quad in range(QUADS):
             nc.sync.dma_start(
                 wo_plane[32 * quad:32 * quad + 4, :].bitcast(I32), wo_scales[0][4 * quad:4 * quad + 4, :].bitcast(I32))
 
@@ -149,36 +171,35 @@ def tile_list_autofocus_phase_step_kernel(
             for t in range(PACK):
                 nc.scalar.copy(f2[hf][:, t, :], banks[t][:])
 
-
         w1_bf = [
-            big.tile([P, PACK * H], BF16, name="w1_bf%d" % a, align_bytes=64, offset=at)
-            for a, at in enumerate((6 * T + 1024, 10 * T))]
+            big.tile([P, PACK * H], BF16, name="w1_bf%d" % a, align_bytes=64, offset=W1_BF_AT[a])
+            for a in range(PASSES)]
         w1_codes = [
-            big.tile([P, H], I32, name="w1_codes%d" % a, align_bytes=64, offset=at)
-            for a, at in enumerate((11 * T, 3 * T))]
+            big.tile([P, H], I32, name="w1_codes%d" % a, align_bytes=64, offset=W1_CODES_AT[a])
+            for a in range(PASSES)]
         w1_scales = keep.tile([P, PASSES, H], U8, name="w1_scales", align_bytes=64)
 
         def dealt(a):
-            return w1_bf[a][:].rearrange("p (t m j) -> p m t j", t=PACK, j=PACK)
+            return w1_bf[a][:].rearrange("p (u i m j) -> p m u j i", u=2, i=2, j=PACK)
 
         def by_column(raw):
-            return raw[:].rearrange("p j (m t) -> p m t j", t=PACK)
+            return raw[:].rearrange("p j (m u i) -> p m u j i", u=2, i=2)
 
-        def quantise_w1(a, u):
-            nc.vector.quantize_mx(
-                w1_codes[a][:, 256 * u:256 * (u + 1)].bitcast(FP8X4),
-                w1_scales[:, a, 256 * u:256 * (u + 1)],
-                w1_bf[a][:, 1024 * u:1024 * (u + 1)])
+        def quantise_w1(a):
+            half = H // 2
+            for s in range(2):
+                nc.vector.quantize_mx(
+                    w1_codes[a][:, half * s:half * (s + 1)].bitcast(FP8X4),
+                    w1_scales[:, a, half * s:half * (s + 1)],
+                    w1_bf[a][:, PACK * half * s:PACK * half * (s + 1)])
 
         nc.scalar.copy(dealt(1), by_column(w1_raw1))
-        for u in range(2):
-            quantise_w1(1, u)
+        quantise_w1(1)
         make_f2(0)
         nc.vector.tensor_copy(dealt(0), by_column(w1_raw0))
-        for u in range(2):
-            quantise_w1(0, u)
+        quantise_w1(0)
 
-        pe1 = big.tile([P, PACK, HALF], F32, name="pe1", offset=8 * T)
+        pe1 = big.tile([P, PACK, HALF], F32, name="pe1", offset=PE1_AT)
         nc.sync.dma_start(pe1[:], pe_v[:, :, HALF:])
         pes = [pe0, pe1]
 
@@ -190,6 +211,7 @@ def tile_list_autofocus_phase_step_kernel(
         wd_bf = keep.tile([P, PASSES * PACK * N], BF16, name="wd_bf", align_bytes=64)
         wd_codes = keep.tile([P, PASSES * N], I32, name="wd_codes", align_bytes=64)
         wd_scales = keep.tile([P, PASSES * N], U8, name="wd_scales", align_bytes=64)
+        last = CHUNKS - 1
         h_tiles = {}
         h_bf = {}
         damp = {}
@@ -198,7 +220,7 @@ def tile_list_autofocus_phase_step_kernel(
         def make_products(q, u):
             col0 = q * CHUNK
             hf, c = divmod(col0, HALF)
-            if q < CHUNKS - 1:
+            if q < last:
                 ts, lo, width = range(2 * u, 2 * u + 2), 0, CHUNK
             else:
                 ts, lo, width = range(PACK), u * CHUNK // 2, CHUNK // 2
@@ -215,25 +237,25 @@ def tile_list_autofocus_phase_step_kernel(
                         f1_bank[:, i, :], w1_codes[a][:, P * t:P * (t + 1)].bitcast(FP8X4),
                         w1_scales[:, a, P * t:P * (t + 1)], a, col0 + lo, width)
             part = (slice(None), slice(ts.start, ts.stop), slice(c + lo, c + lo + width))
-            f3pe = big.tile([P, len(ts), width], F32, name="f3pe", bufs=3, offset=6 * T)
+            f3pe = big.tile([P, len(ts), width], F32, name="f3pe", bufs=3, offset=F3PE_AT)
             nc.vector.tensor_tensor(f3pe[:], f3_bank[:], pes[hf][part], ALU.mult)
             f1f2 = ring.tile([P, len(ts), width], F32, name="f1f2")
             nc.vector.tensor_tensor(f1f2[:], f1_bank[:], f2[hf][part], ALU.mult)
-            if q < CHUNKS - 1:
+            if q < last:
                 return h_tiles[q][0][:, ts.start:ts.stop, :], f1f2[:], f3pe[:]
             return h_tiles[q][u][:], f1f2[:], f3pe[:]
 
         def make_h(q):
-            parts = 1 if q < CHUNKS - 1 else 2
+            parts = 1 if q < last else 2
             h_tiles[q] = [keep.tile([P, PACK, CHUNK // parts], F32, name="h%d_%d" % (q, s)) for s in range(parts)]
             nc.gpsimd.tensor_tensor(*make_products(q, 0), ALU.subtract)
-            if q >= 2:
-                quantise_h(q - 2)
-                make_e(q - 2)
+            if q >= LAG:
+                quantise_h(q - LAG)
+                make_e(q - LAG)
             second = make_products(q, 1)
-            if q >= 2:
-                make_y(q - 2)
-            if q < CHUNKS - 1:
+            if q >= LAG:
+                make_y(q - LAG)
+            if q < last:
                 nc.gpsimd.tensor_tensor(*second, ALU.subtract)
             else:
                 quantise_h(q - 1)
@@ -245,11 +267,12 @@ def tile_list_autofocus_phase_step_kernel(
 
         def round_h(q):
             h_bf[q] = ring.tile([P, PACK * CHUNK], BF16, name="h_bf", align_bytes=64)
-            dst = h_bf[q][:].rearrange("p (c i t) -> p c t i", t=PACK, i=4)
-            src = [part[:].rearrange("p t (c i) -> p c t i", i=4) for part in h_tiles[q]]
-            if q == CHUNKS - 1:
-                nc.scalar.copy(dst[:, 0:32], src[0])
-                nc.vector.tensor_copy(dst[:, 32:64], src[1])
+            dst = h_bf[q][:].rearrange("p (c i t) -> p c t i", t=PACK, i=RUN)
+            src = [part[:].rearrange("p t (c i) -> p c t i", i=RUN) for part in h_tiles[q]]
+            if q == last:
+                runs = CHUNK // 2 // RUN
+                nc.scalar.copy(dst[:, 0:runs], src[0])
+                nc.vector.tensor_copy(dst[:, runs:2 * runs], src[1])
             else:
                 nc.scalar.copy(dst, src[0])
 
@@ -260,9 +283,9 @@ def tile_list_autofocus_phase_step_kernel(
 
         def make_e(q):
             cols = slice(q * CHUNK, (q + 1) * CHUNK)
-            e_bank = psum_de.tile([P, 2, CHUNK], F32, name="e_bank", tag="e_bank" if q < CHUNKS - 1 else "d_bank")
+            e_bank = psum_de.tile([P, 2, CHUNK], F32, name="e_bank", tag="e_bank" if q < last else "d_bank")
             e_banks[q] = e_bank
-            for n in range(2):
+            for n in range(N // P):
                 nc.tensor.matmul_mx(
                     e_bank[:, n, :], lhsT=wo_codes[:, 2 * P * n:2 * P * (n + 1)].bitcast(FP4X4),
                     lhsT_scale=wo_plane[:, P * n:P * (n + 1)],
@@ -272,20 +295,20 @@ def tile_list_autofocus_phase_step_kernel(
         def quantise_wd():
             for a in range(PASSES):
                 nc.scalar.copy(
-                    wd_bf[:, a * PACK * N:(a + 1) * PACK * N].rearrange("p (c i j) -> p c j i", j=PACK, i=4),
-                    wd_raw[:, a, :].rearrange("p (j c i) -> p c j i", j=PACK, i=4))
+                    wd_bf[:, a * PACK * N:(a + 1) * PACK * N].rearrange("p (c i j) -> p c j i", j=PACK, i=RUN),
+                    wd_raw[:, a, :].rearrange("p (j c i) -> p c j i", j=PACK, i=RUN))
             nc.vector.quantize_mx(wd_codes[:].bitcast(FP8X4), wd_scales[:], wd_bf[:])
 
         def make_damp(q):
             d_bank = psum_de.tile([P, 2, CHUNK], F32, name="d_bank", tag="d_bank")
-            for n in range(2):
+            for n in range(N // P):
                 for a in range(PASSES):
                     at = slice(a * N + P * n, a * N + P * (n + 1))
                     table_product(d_bank[:, n, :], wd_codes[:, at].bitcast(FP8X4), wd_scales[:, at], a, q * CHUNK, CHUNK)
             d2 = ring.tile([P, 2, CHUNK], F32, name="d2")
             nc.scalar.activation(d2[:], d_bank[:], ACT.Square)
             damp[q] = keep.tile([P, 2, CHUNK], F32, name="damp%d" % q)
-            nc.scalar.activation(damp[q][:], d2[:], ACT.Abs_reciprocal_sqrt, bias=one[:])
+            nc.scalar.activation(damp[q][:], d2[:], ACT.Abs_reciprocal_sqrt, bias=root_one[:])
 
         def make_y(q):
             y = keep.tile([P, 2, CHUNK], F32, name="y%d" % q)
@@ -309,7 +332,7 @@ def tile_list_autofocus_phase_step_kernel(
         round_h(3)
         quantise_h(3)
         make_e(3)
-        for quad in range(4):
+        for quad in range(QUADS):
             nc.scalar.dma_start(
                 out_3[0][4 * quad:4 * quad + 4, :].bitcast(I32), h_scales[32 * quad:32 * quad + 4, :].bitcast(I32))
         make_y(3)

@@ -25,25 +25,24 @@ HALF = S // 2
 CHUNK = 256
 CHUNKS = S // CHUNK
 RUN = 2
-LAG = 2
+D_BANK, E_BANK = 6, 7
 
 W2_AT = S
 W3_AT = S + H
 PLANE_WIDTH = S + 2 * H
 
 KIB = 1024
-TABLE_AT = (0, 16 * KIB)
-PICKED_ROWS_AT = 32 * KIB - 512
-W1_RAW0_AT = 32 * KIB
-PE0_AT = 0
-W3_CODES_AT = 8 * KIB
-W1_CODES_AT = (44 * KIB, 12 * KIB)
-WD_RAW_AT = 16 * KIB
-W1_BF_AT = (25 * KIB, 40 * KIB)
-F3PE_AT = 24 * KIB
-WO_CODES_AT = 30 * KIB
-WO_PLANE_AT = 30 * KIB + 512
-PE1_AT = 32 * KIB
+TABLE_AT = (8 * KIB - 64, 26 * KIB)
+PICKED_ROWS_AT = 42 * KIB - 512
+W1_RAW_AT = (42 * KIB, 0)
+W3_RAW_AT = 50 * KIB
+PE_AT = (8 * KIB, 21 * KIB, W3_RAW_AT)
+WD_RAW_AT = (12 * KIB, 16 * KIB)
+WO_CODES_AT = 32 * KIB
+WO_PLANE_AT = 32 * KIB + 512
+W1_BF_AT = 27 * KIB
+F3PE_AT = 26 * KIB
+W1_SPLIT = 80
 
 
 def tile_list_autofocus_phase_step_kernel(
@@ -56,11 +55,10 @@ def tile_list_autofocus_phase_step_kernel(
         keep = ctx.enter_context(tc.tile_pool(name="keep", bufs=1))
         big = ctx.enter_context(tc.tile_pool(name="big", bufs=1))
         ring = ctx.enter_context(tc.tile_pool(name="ring", bufs=3))
-        psum = ctx.enter_context(tc.psum_pool(name="psum", bufs=6))
-        psum_de = ctx.enter_context(tc.psum_pool(name="psum_de", bufs=1))
+        psum = ctx.enter_context(tc.psum_pool(name="psum", bufs=1))
 
-        offsets = lists.tile([P, S // 16], U16, name="offsets")
-        nc.sync.dma_start(offsets[:], offs)
+        def bank(b, shape):
+            return psum.tile(shape, F32, name="bank%d" % b, tag="bank%d" % b)
 
         rows = PASSES * BLOCKS
         tab_rows = keep.tile([P, T], U8, name="tab_rows", align_bytes=64)
@@ -68,38 +66,37 @@ def tile_list_autofocus_phase_step_kernel(
         plane0 = keep.tile([P, PLANE_WIDTH], U8, name="plane0", align_bytes=64)
         plane1 = keep.tile([P, PLANE_WIDTH], U8, name="plane1", align_bytes=64)
         planes = [plane0, plane1]
-        nc.sync.dma_start(tab_rows[0:rows, :].bitcast(I32), tab_scales.rearrange("a q c -> (a q) c").bitcast(I32))
         nc.sync.dma_start(w_rows[0:rows, 0:H].bitcast(I32), w2_scales.rearrange("a q c -> (a q) c").bitcast(I32))
         nc.sync.dma_start(w_rows[0:rows, H:].bitcast(I32), w3_scales.rearrange("a q c -> (a q) c").bitcast(I32))
-        w2_raw = keep.tile([P, PASSES, 2 * H], U8, name="w2_raw", align_bytes=64)
-        nc.sync.dma_start(w2_raw[:].bitcast(I32), w2_words.rearrange("a p c -> p a c").bitcast(I32))
+        nc.sync.dma_start(tab_rows[0:rows, :].bitcast(I32), tab_scales.rearrange("a q c -> (a q) c").bitcast(I32))
+        offsets = lists.tile([P, S // 16], U16, name="offsets")
+        nc.sync.dma_start(offsets[:], offs)
         tables = [big.tile([P, T], I32, name="table%d" % a, offset=TABLE_AT[a]) for a in range(PASSES)]
 
         def load_table(a):
             nc.sync.dma_start(tables[a][:], tab_words[a].rearrange("p t i -> p (t i)").bitcast(I32))
 
         load_table(0)
-        w3_raw = keep.tile([P, PASSES, H], I32, name="w3_raw", align_bytes=64)
+        w2_raw = keep.tile([P, PASSES, 2 * H], U8, name="w2_raw", align_bytes=64)
+        nc.sync.dma_start(w2_raw[:].bitcast(I32), w2_words.rearrange("a p c -> p a c").bitcast(I32))
+        w3_raw = big.tile([P, PASSES, H], I32, name="w3_raw", align_bytes=64, offset=W3_RAW_AT)
         nc.sync.dma_start(w3_raw[:], w3_words.rearrange("a p c i -> p a (c i)").bitcast(I32))
-        w1_v = w1.rearrange("(a p j) c -> a p j c", p=P, j=PACK)
-        w1_raw1 = keep.tile([P, PACK, H], F32, name="w1_raw1")
-        nc.sync.dma_start(w1_raw1[:], w1_v[1])
 
-        for lo, hi in ((32, 64), (64, P)):
-            nc.vector.memset(tab_rows[lo:hi, :].bitcast(I32), 0)
-            nc.vector.memset(w_rows[lo:hi, :].bitcast(I32), 0)
-        nc.vector.memset(plane1[:].bitcast(I32), 0)
+        for staged in (w_rows, tab_rows):
+            for lo, hi in ((32, 64), (64, P)):
+                nc.vector.memset(staged[lo:hi, :].bitcast(I32), 0)
+        nc.gpsimd.memset(plane1[:].bitcast(I32), 0)
         one = keep.tile([P, 1], F32, name="one")
-        nc.vector.memset(one[:], 1.0)
+        nc.gpsimd.memset(one[:], 1.0)
         root_one = keep.tile([P, 1], F32, name="root_one")
         nc.scalar.activation(root_one[:], one[:], ACT.Abs_reciprocal_sqrt)
 
-        picked_rows = big.tile([P, S], U8, name="picked_rows", align_bytes=64, offset=PICKED_ROWS_AT)
-        nc.vector.tensor_copy(picked_rows[:], tab_rows[:].indirect(offsets[:]))
         nc.vector.tensor_copy(
             plane0[:, W2_AT:PLANE_WIDTH].rearrange("p (w t b m) -> p w b t m", w=2, t=PACK, m=16),
             w_rows[:].rearrange("p (w b m t) -> p w b t m", w=2, t=PACK, m=16),
         )
+        picked_rows = big.tile([P, S], U8, name="picked_rows", align_bytes=64, offset=PICKED_ROWS_AT)
+        nc.vector.tensor_copy(picked_rows[:], tab_rows[:].indirect(offsets[:]))
         nc.vector.tensor_copy(plane0[:, 0:S].bitcast(I32), picked_rows[:].bitcast(I32))
         for quad in range(1, QUADS):
             nc.sync.dma_start(
@@ -109,48 +106,64 @@ def tile_list_autofocus_phase_step_kernel(
             nc.sync.dma_start(
                 plane1[32 * quad:32 * quad + 4, :].bitcast(I32),
                 plane0[BLOCKS + 4 * quad:BLOCKS + 4 * quad + 4, 0:PLANE_WIDTH].bitcast(I32))
+        w1_v = w1.rearrange("(a p j) c -> a p j c", p=P, j=PACK)
+        w1_raw = [big.tile([P, PACK, H], F32, name="w1_raw%d" % a, offset=W1_RAW_AT[a]) for a in range(PASSES)]
+        nc.sync.dma_start(w1_raw[0][:], w1_v[0])
+
+        picked = {}
+
+        def gather_words(a, hf):
+            columns = HALF // 16
+            picked[a, hf] = keep.tile([P, HALF], U32, name="picked%d%d" % (a, hf), align_bytes=64)
+            nc.vector.tensor_copy(
+                picked[a, hf][:], tables[a][:].bitcast(U32).indirect(offsets[:, hf * columns:(hf + 1) * columns]))
 
         w2_codes = keep.tile([P, PASSES, 2 * H], U8, name="w2_codes", align_bytes=64)
-        for a in range(PASSES):
+
+        def deal_w2(a):
             nc.vector.tensor_copy(
                 w2_codes[:, a, :].bitcast(U16).rearrange("p (t b m) -> p b t m", t=PACK, m=8),
                 w2_raw[:, a, :].bitcast(U16).rearrange("p (b m t) -> p b t m", t=PACK, m=8),
             )
 
-        picked = {}
-
-        def gather_words(a):
-            columns = HALF // 16
-            for hf in range(2):
-                picked[a, hf] = keep.tile([P, HALF], U32, name="picked%d%d" % (a, hf), align_bytes=64)
-                nc.vector.tensor_copy(
-                    picked[a, hf][:], tables[a][:].bitcast(U32).indirect(offsets[:, hf * columns:(hf + 1) * columns]))
-
-        gather_words(0)
-        w3_codes = big.tile([P, PASSES, H], I32, name="w3_codes", align_bytes=64, offset=W3_CODES_AT)
+        gather_words(0, 0)
+        gather_words(0, 1)
+        deal_w2(0)
+        deal_w2(1)
+        w3_codes = keep.tile([P, PASSES, H], I32, name="w3_codes", align_bytes=64)
         nc.vector.tensor_copy(
             w3_codes[:].rearrange("p a (t b m) -> p a b t m", t=PACK, m=4),
             w3_raw[:].rearrange("p a (b m t) -> p a b t m", t=PACK, m=4),
         )
-        gather_words(1)
+        gather_words(1, 0)
+        gather_words(1, 1)
 
-        def table_product(out, codes, scales, a, col0, width):
+        def table_product(out, codes, scales, a, col0, width, start, stop):
             hf, c = divmod(col0, HALF)
             nc.tensor.matmul_mx(
                 out, lhsT=codes, lhsT_scale=scales,
                 rhs=picked[a, hf][:, c:c + width].bitcast(FP8X4),
                 rhs_scale=planes[a][:, col0:col0 + width],
-                start=(a == 0), stop=(a == PASSES - 1),
+                start=start, stop=stop,
             )
 
-        w1_raw0 = big.tile([P, PACK, H], F32, name="w1_raw0", offset=W1_RAW0_AT)
-        nc.sync.dma_start(w1_raw0[:], w1_v[0])
+        nc.sync.dma_start(w1_raw[1][:], w1_v[1])
         pe_v = pe.rearrange("(p t) j -> p t j", t=PACK)
-        pe0 = big.tile([P, PACK, HALF], F32, name="pe0", offset=PE0_AT)
-        nc.sync.dma_start(pe0[:], pe_v[:, :, 0:HALF])
-        wd_raw = big.tile([P, PASSES, PACK * N], F32, name="wd_raw", offset=WD_RAW_AT)
-        nc.sync.dma_start(wd_raw[:], wd.rearrange("(a p j) n -> p a (j n)", p=P, j=PACK))
+        pe_cols = ((0, CHUNK), (CHUNK, HALF), (HALF, S))
+        pes = [
+            big.tile([P, PACK, hi - lo], F32, name="pe%d" % i, offset=PE_AT[i]) for i, (lo, hi) in enumerate(pe_cols)]
 
+        def load_pe(i):
+            lo, hi = pe_cols[i]
+            nc.sync.dma_start(pes[i][:], pe_v[:, :, lo:hi])
+
+        load_pe(0)
+        wd_v = wd.rearrange("(a p j) n -> a p (j n)", p=P, j=PACK)
+        wd_raw = [big.tile([P, PACK * N], F32, name="wd_raw%d" % a, offset=WD_RAW_AT[a]) for a in range(PASSES)]
+        for a in range(PASSES):
+            nc.sync.dma_start(wd_raw[a][:], wd_v[a])
+        load_pe(1)
+        load_pe(2)
         wo_codes = big.tile([P, 2 * N], U8, name="wo_codes", align_bytes=64, offset=WO_CODES_AT)
         nc.sync.dma_start(wo_codes[:].bitcast(I32), wo_words[0].bitcast(I32))
         wo_plane = big.tile([P, N], U8, name="wo_plane", align_bytes=64, offset=WO_PLANE_AT)
@@ -160,48 +173,40 @@ def tile_list_autofocus_phase_step_kernel(
                 wo_plane[32 * quad:32 * quad + 4, :].bitcast(I32), wo_scales[0][4 * quad:4 * quad + 4, :].bitcast(I32))
 
         f2 = [keep.tile([P, PACK, HALF], F32, name="f2_%d" % hf) for hf in range(2)]
-
-        def make_f2(hf):
-            banks = [psum.tile([P, HALF], F32, name="bank") for t in range(PACK)]
-            for a in range(PASSES):
+        f2_banks = [[bank(b, [P, HALF]) for b in bs] for bs in ((0, 2, 1, 3), (4, 5, 6, 7))]
+        for a in range(PASSES):
+            for hf in range(2):
                 for t in range(PACK):
                     table_product(
-                        banks[t][:], w2_codes[:, a, 2 * P * t:2 * P * (t + 1)].bitcast(FP4X4),
-                        planes[a][:, W2_AT + P * t:W2_AT + P * (t + 1)], a, hf * HALF, HALF)
-            for t in range(PACK):
-                nc.scalar.copy(f2[hf][:, t, :], banks[t][:])
+                        f2_banks[hf][t][:], w2_codes[:, a, 2 * P * t:2 * P * (t + 1)].bitcast(FP4X4),
+                        planes[a][:, W2_AT + P * t:W2_AT + P * (t + 1)], a, hf * HALF, HALF,
+                        a == 0, a == PASSES - 1)
 
-        w1_bf = [
-            big.tile([P, PACK * H], BF16, name="w1_bf%d" % a, align_bytes=64, offset=W1_BF_AT[a])
-            for a in range(PASSES)]
-        w1_codes = [
-            big.tile([P, H], I32, name="w1_codes%d" % a, align_bytes=64, offset=W1_CODES_AT[a])
-            for a in range(PASSES)]
+        def empty_f2(hf):
+            for t in range(PACK):
+                nc.scalar.copy(f2[hf][:, t, :], f2_banks[hf][t][:])
+
+        w1_codes = keep.tile([P, PASSES, H], I32, name="w1_codes", align_bytes=64)
         w1_scales = keep.tile([P, PASSES, H], U8, name="w1_scales", align_bytes=64)
 
-        def dealt(a):
-            return w1_bf[a][:].rearrange("p (u i m j) -> p m u j i", u=2, i=2, j=PACK)
-
-        def by_column(raw):
-            return raw[:].rearrange("p j (m u i) -> p m u j i", u=2, i=2)
-
-        def quantise_w1(a):
+        def quantise_w1(a, split):
+            w1_bf = big.tile([P, PACK * H], BF16, name="w1_bf%d" % a, align_bytes=64, offset=W1_BF_AT)
+            dealt = w1_bf[:].rearrange("p (u i m j) -> p m u j i", u=2, i=2, j=PACK)
+            by_column = w1_raw[a][:].rearrange("p j (m u i) -> p m u j i", u=2, i=2)
+            nc.vector.tensor_copy(dealt[:, 0:split], by_column[:, 0:split])
+            if split < P:
+                nc.scalar.copy(dealt[:, split:P], by_column[:, split:P])
             half = H // 2
             for s in range(2):
                 nc.vector.quantize_mx(
-                    w1_codes[a][:, half * s:half * (s + 1)].bitcast(FP8X4),
+                    w1_codes[:, a, half * s:half * (s + 1)].bitcast(FP8X4),
                     w1_scales[:, a, half * s:half * (s + 1)],
-                    w1_bf[a][:, PACK * half * s:PACK * half * (s + 1)])
+                    w1_bf[:, PACK * half * s:PACK * half * (s + 1)])
 
-        nc.scalar.copy(dealt(1), by_column(w1_raw1))
-        quantise_w1(1)
-        make_f2(0)
-        nc.vector.tensor_copy(dealt(0), by_column(w1_raw0))
-        quantise_w1(0)
-
-        pe1 = big.tile([P, PACK, HALF], F32, name="pe1", offset=PE1_AT)
-        nc.sync.dma_start(pe1[:], pe_v[:, :, HALF:])
-        pes = [pe0, pe1]
+        empty_f2(0)
+        empty_f2(1)
+        quantise_w1(0, P)
+        quantise_w1(1, P)
 
         h_v = out_1.rearrange("(p t) j -> p t j", t=PACK)
         y_v = out_0.rearrange("(n p) j -> p n j", p=P)
@@ -224,57 +229,49 @@ def tile_list_autofocus_phase_step_kernel(
                 ts, lo, width = range(2 * u, 2 * u + 2), 0, CHUNK
             else:
                 ts, lo, width = range(PACK), u * CHUNK // 2, CHUNK // 2
-            f3_bank = psum.tile([P, len(ts), width], F32, name="bank")
-            f1_bank = psum.tile([P, len(ts), width], F32, name="bank")
-            for i, t in enumerate(ts):
-                for a in range(PASSES):
-                    table_product(
-                        f3_bank[:, i, :], w3_codes[:, a, P * t:P * (t + 1)].bitcast(FP8X4),
-                        planes[a][:, W3_AT + P * t:W3_AT + P * (t + 1)], a, col0 + lo, width)
-            for i, t in enumerate(ts):
-                for a in range(PASSES):
-                    table_product(
-                        f1_bank[:, i, :], w1_codes[a][:, P * t:P * (t + 1)].bitcast(FP8X4),
-                        w1_scales[:, a, P * t:P * (t + 1)], a, col0 + lo, width)
+            pair = (2 * q + u) % 3
+            f3_bank = bank(2 * pair, [P, len(ts), width])
+            f1_bank = bank(2 * pair + 1, [P, len(ts), width])
+            steps = [(a, i, t) for a in range(PASSES) for i, t in enumerate(ts)]
+            for step in steps:
+                a, i, t = step
+                table_product(
+                    f3_bank[:, i, :], w3_codes[:, a, P * t:P * (t + 1)].bitcast(FP8X4),
+                    planes[a][:, W3_AT + P * t:W3_AT + P * (t + 1)], a, col0 + lo, width,
+                    step == steps[0], step == steps[-1])
+            for step in steps:
+                a, i, t = step
+                table_product(
+                    f1_bank[:, i, :], w1_codes[:, a, P * t:P * (t + 1)].bitcast(FP8X4),
+                    w1_scales[:, a, P * t:P * (t + 1)], a, col0 + lo, width,
+                    step == steps[0], step == steps[-1])
             part = (slice(None), slice(ts.start, ts.stop), slice(c + lo, c + lo + width))
+            piece = min(q, 2)
+            pe_lo = col0 + lo - pe_cols[piece][0]
             f3pe = big.tile([P, len(ts), width], F32, name="f3pe", bufs=3, offset=F3PE_AT)
-            nc.vector.tensor_tensor(f3pe[:], f3_bank[:], pes[hf][part], ALU.mult)
+            nc.vector.tensor_tensor(
+                f3pe[:], f3_bank[:], pes[piece][:, ts.start:ts.stop, pe_lo:pe_lo + width], ALU.mult)
             f1f2 = ring.tile([P, len(ts), width], F32, name="f1f2")
             nc.vector.tensor_tensor(f1f2[:], f1_bank[:], f2[hf][part], ALU.mult)
             if q < last:
                 return h_tiles[q][0][:, ts.start:ts.stop, :], f1f2[:], f3pe[:]
             return h_tiles[q][u][:], f1f2[:], f3pe[:]
 
-        def make_h(q):
+        def open_h(q):
             parts = 1 if q < last else 2
             h_tiles[q] = [keep.tile([P, PACK, CHUNK // parts], F32, name="h%d_%d" % (q, s)) for s in range(parts)]
-            nc.gpsimd.tensor_tensor(*make_products(q, 0), ALU.subtract)
-            if q >= LAG:
-                quantise_h(q - LAG)
-                make_e(q - LAG)
-            second = make_products(q, 1)
-            if q >= LAG:
-                make_y(q - LAG)
-            if q < last:
-                nc.gpsimd.tensor_tensor(*second, ALU.subtract)
-            else:
-                quantise_h(q - 1)
-                make_e(q - 1)
-                nc.vector.tensor_tensor(*second, ALU.subtract)
-            for s in range(parts):
-                col0 = q * CHUNK + s * CHUNK // 2
-                nc.sync.dma_start(h_v[:, :, col0:col0 + CHUNK // parts], h_tiles[q][s][:])
 
-        def round_h(q):
-            h_bf[q] = ring.tile([P, PACK * CHUNK], BF16, name="h_bf", align_bytes=64)
+        def store_h(q, s):
+            width = CHUNK // len(h_tiles[q])
+            col0 = q * CHUNK + s * width
+            nc.sync.dma_start(h_v[:, :, col0:col0 + width], h_tiles[q][s][:])
+
+        def round_h(q, s, copy):
+            if s == 0:
+                h_bf[q] = ring.tile([P, PACK * CHUNK], BF16, name="h_bf", align_bytes=64)
+            runs = CHUNK // len(h_tiles[q]) // RUN
             dst = h_bf[q][:].rearrange("p (c i t) -> p c t i", t=PACK, i=RUN)
-            src = [part[:].rearrange("p t (c i) -> p c t i", i=RUN) for part in h_tiles[q]]
-            if q == last:
-                runs = CHUNK // 2 // RUN
-                nc.scalar.copy(dst[:, 0:runs], src[0])
-                nc.vector.tensor_copy(dst[:, runs:2 * runs], src[1])
-            else:
-                nc.scalar.copy(dst, src[0])
+            copy(dst[:, s * runs:(s + 1) * runs], h_tiles[q][s][:].rearrange("p t (c i) -> p c t i", i=RUN))
 
         def quantise_h(q):
             cols = slice(q * CHUNK, (q + 1) * CHUNK)
@@ -283,7 +280,7 @@ def tile_list_autofocus_phase_step_kernel(
 
         def make_e(q):
             cols = slice(q * CHUNK, (q + 1) * CHUNK)
-            e_bank = psum_de.tile([P, 2, CHUNK], F32, name="e_bank", tag="e_bank" if q < last else "d_bank")
+            e_bank = bank(E_BANK if q < last else D_BANK, [P, 2, CHUNK])
             e_banks[q] = e_bank
             for n in range(N // P):
                 nc.tensor.matmul_mx(
@@ -292,19 +289,23 @@ def tile_list_autofocus_phase_step_kernel(
                     rhs=h_codes[:, cols].bitcast(FP8X4), rhs_scale=h_scales[:, cols],
                     start=True, stop=True)
 
-        def quantise_wd():
+        def round_wd():
             for a in range(PASSES):
                 nc.scalar.copy(
                     wd_bf[:, a * PACK * N:(a + 1) * PACK * N].rearrange("p (c i j) -> p c j i", j=PACK, i=RUN),
-                    wd_raw[:, a, :].rearrange("p (j c i) -> p c j i", j=PACK, i=RUN))
+                    wd_raw[a][:].rearrange("p (j c i) -> p c j i", j=PACK, i=RUN))
+
+        def quantise_wd():
             nc.vector.quantize_mx(wd_codes[:].bitcast(FP8X4), wd_scales[:], wd_bf[:])
 
         def make_damp(q):
-            d_bank = psum_de.tile([P, 2, CHUNK], F32, name="d_bank", tag="d_bank")
+            d_bank = bank(D_BANK, [P, 2, CHUNK])
             for n in range(N // P):
                 for a in range(PASSES):
                     at = slice(a * N + P * n, a * N + P * (n + 1))
-                    table_product(d_bank[:, n, :], wd_codes[:, at].bitcast(FP8X4), wd_scales[:, at], a, q * CHUNK, CHUNK)
+                    table_product(
+                        d_bank[:, n, :], wd_codes[:, at].bitcast(FP8X4), wd_scales[:, at], a, q * CHUNK, CHUNK,
+                        a == 0, a == PASSES - 1)
             d2 = ring.tile([P, 2, CHUNK], F32, name="d2")
             nc.scalar.activation(d2[:], d_bank[:], ACT.Square)
             damp[q] = keep.tile([P, 2, CHUNK], F32, name="damp%d" % q)
@@ -315,24 +316,44 @@ def tile_list_autofocus_phase_step_kernel(
             nc.vector.tensor_tensor(y[:], e_banks[q][:], damp[q][:], ALU.mult)
             nc.sync.dma_start(y_v[:, :, q * CHUNK:(q + 1) * CHUNK], y[:])
 
-        make_h(0)
-        make_f2(1)
-        round_h(0)
-        make_h(1)
-        quantise_wd()
-        make_damp(0)
-        round_h(1)
-        make_damp(1)
-        make_h(2)
-        round_h(2)
-        make_damp(2)
-        make_damp(3)
-        make_h(3)
-        make_y(2)
-        round_h(3)
-        quantise_h(3)
-        make_e(3)
+        def subtract(engine, operands):
+            engine.tensor_tensor(*operands, ALU.subtract)
+
+        round_wd()
+        for q in range(CHUNKS):
+            open_h(q)
+            first = make_products(q, 0)
+            if q >= 2:
+                quantise_h(q - 2)
+                make_e(q - 2)
+            subtract(nc.gpsimd, first)
+            if q == last:
+                store_h(q, 0)
+            if q >= 1:
+                round_h(q - 1, 0, nc.scalar.copy)
+            second = make_products(q, 1)
+            if q == 1:
+                quantise_wd()
+                make_damp(0)
+                make_damp(1)
+            if q == 2:
+                make_damp(2)
+            if q >= 2:
+                make_y(q - 2)
+            if q < last:
+                subtract(nc.gpsimd, second)
+                store_h(q, 0)
+        subtract(nc.vector, second)
+        store_h(last, 1)
+        round_h(last, 0, nc.scalar.copy)
+        make_damp(last)
+        quantise_h(last - 1)
+        make_e(last - 1)
+        round_h(last, 1, nc.vector.tensor_copy)
+        quantise_h(last)
+        make_e(last)
+        make_y(last - 1)
         for quad in range(QUADS):
             nc.scalar.dma_start(
                 out_3[0][4 * quad:4 * quad + 4, :].bitcast(I32), h_scales[32 * quad:32 * quad + 4, :].bitcast(I32))
-        make_y(3)
+        make_y(last)

@@ -25,7 +25,8 @@ HALF = S // 2
 CHUNK = 256
 CHUNKS = S // CHUNK
 RUN = 2
-D_BANK, E_BANK = 6, 7
+D_BANKS = (6, 7, 6, 4)
+E_BANKS = (7, 7, 6, 5)
 
 W2_AT = S
 W3_AT = S + H
@@ -35,14 +36,21 @@ KIB = 1024
 TABLE_AT = (8 * KIB - 64, 26 * KIB)
 PICKED_ROWS_AT = 42 * KIB - 512
 W1_RAW_AT = (42 * KIB, 0)
-W3_RAW_AT = 50 * KIB
-PE_AT = (8 * KIB, 21 * KIB, W3_RAW_AT)
-WD_RAW_AT = (12 * KIB, 16 * KIB)
-WO_CODES_AT = 32 * KIB
-WO_PLANE_AT = 32 * KIB + 512
+W3_RAW_AT = 52 * KIB
+PE_AT = (8 * KIB, 50 * KIB, 54 * KIB)
+WD_RAW_AT = (16 * KIB, 20 * KIB)
+WO_CODES_AT = 43 * KIB
+WO_PLANE_AT = 43 * KIB + 512
 W1_BF_AT = 27 * KIB
-F3PE_AT = 26 * KIB
-W1_SPLIT = 80
+PRODUCTS_AT = (26 * KIB, 34 * KIB, 58 * KIB, 71 * KIB)
+WD_BF_AT = 64 * KIB
+H_BF_AT = (78 * KIB, 86 * KIB, 88 * KIB, 90 * KIB)
+H_AT = {1: 66 * KIB, 2: 79 * KIB}
+WD_CODES_AT = PRODUCTS_AT[0]
+WD_SCALES_AT = PE_AT[0]
+H_CODES_AT = (PRODUCTS_AT[1], PRODUCTS_AT[2] - 512, 84 * KIB, 85 * KIB)
+H_SCALES_AT = PE_AT[1]
+D2_AT = (92 * KIB, H_BF_AT[1], 94 * KIB, H_BF_AT[2])
 
 
 def tile_list_autofocus_phase_step_kernel(
@@ -54,7 +62,6 @@ def tile_list_autofocus_phase_step_kernel(
         lists = ctx.enter_context(tc.tile_pool(name="lists", bufs=1))
         keep = ctx.enter_context(tc.tile_pool(name="keep", bufs=1))
         big = ctx.enter_context(tc.tile_pool(name="big", bufs=1))
-        ring = ctx.enter_context(tc.tile_pool(name="ring", bufs=3))
         psum = ctx.enter_context(tc.psum_pool(name="psum", bufs=1))
 
         def bank(b, shape):
@@ -149,7 +156,7 @@ def tile_list_autofocus_phase_step_kernel(
 
         nc.sync.dma_start(w1_raw[1][:], w1_v[1])
         pe_v = pe.rearrange("(p t) j -> p t j", t=PACK)
-        pe_cols = ((0, CHUNK), (CHUNK, HALF), (HALF, S))
+        pe_cols = ((0, HALF), (HALF, HALF + CHUNK), (HALF + CHUNK, S))
         pes = [
             big.tile([P, PACK, hi - lo], F32, name="pe%d" % i, offset=PE_AT[i]) for i, (lo, hi) in enumerate(pe_cols)]
 
@@ -189,13 +196,11 @@ def tile_list_autofocus_phase_step_kernel(
         w1_codes = keep.tile([P, PASSES, H], I32, name="w1_codes", align_bytes=64)
         w1_scales = keep.tile([P, PASSES, H], U8, name="w1_scales", align_bytes=64)
 
-        def quantise_w1(a, split):
+        def quantise_w1(a):
             w1_bf = big.tile([P, PACK * H], BF16, name="w1_bf%d" % a, align_bytes=64, offset=W1_BF_AT)
             dealt = w1_bf[:].rearrange("p (u i m j) -> p m u j i", u=2, i=2, j=PACK)
             by_column = w1_raw[a][:].rearrange("p j (m u i) -> p m u j i", u=2, i=2)
-            nc.vector.tensor_copy(dealt[:, 0:split], by_column[:, 0:split])
-            if split < P:
-                nc.scalar.copy(dealt[:, split:P], by_column[:, split:P])
+            nc.vector.tensor_copy(dealt, by_column)
             half = H // 2
             for s in range(2):
                 nc.vector.quantize_mx(
@@ -205,61 +210,96 @@ def tile_list_autofocus_phase_step_kernel(
 
         empty_f2(0)
         empty_f2(1)
-        quantise_w1(0, P)
-        quantise_w1(1, P)
+        quantise_w1(0)
+        quantise_w1(1)
 
         h_v = out_1.rearrange("(p t) j -> p t j", t=PACK)
         y_v = out_0.rearrange("(n p) j -> p n j", p=P)
         words_v = out_2[0].rearrange("p m t -> p (m t)").bitcast(I32)
-        h_codes = keep.tile([P, S], I32, name="h_codes", align_bytes=64)
-        h_scales = keep.tile([P, S], U8, name="h_scales", align_bytes=64)
-        wd_bf = keep.tile([P, PASSES * PACK * N], BF16, name="wd_bf", align_bytes=64)
-        wd_codes = keep.tile([P, PASSES * N], I32, name="wd_codes", align_bytes=64)
-        wd_scales = keep.tile([P, PASSES * N], U8, name="wd_scales", align_bytes=64)
+        h_codes = [
+            big.tile([P, CHUNK], I32, name="h_codes%d" % q, align_bytes=64, offset=H_CODES_AT[q])
+            for q in range(CHUNKS)]
+        h_scales = big.tile([P, S], U8, name="h_scales", align_bytes=64, offset=H_SCALES_AT)
+        wd_bf = big.tile([P, PASSES * PACK * N], BF16, name="wd_bf", align_bytes=64, offset=WD_BF_AT)
+        wd_codes = big.tile([P, PASSES * N], I32, name="wd_codes", align_bytes=64, offset=WD_CODES_AT)
+        wd_scales = big.tile([P, PASSES * N], U8, name="wd_scales", align_bytes=64, offset=WD_SCALES_AT)
         last = CHUNKS - 1
         h_tiles = {}
         h_bf = {}
         damp = {}
         e_banks = {}
 
-        def make_products(q, u):
-            col0 = q * CHUNK
-            hf, c = divmod(col0, HALF)
+        def unit_shape(unit):
+            q, u = divmod(unit, 2)
             if q < last:
-                ts, lo, width = range(2 * u, 2 * u + 2), 0, CHUNK
-            else:
-                ts, lo, width = range(PACK), u * CHUNK // 2, CHUNK // 2
-            pair = (2 * q + u) % 3
+                return range(2 * u, 2 * u + 2), q * CHUNK, CHUNK
+            return range(PACK), q * CHUNK + u * CHUNK // 2, CHUNK // 2
+
+        f_banks = {}
+        f3pe = {}
+        f1f2 = {}
+
+        def make_f(unit):
+            ts, col0, width = unit_shape(unit)
+            pair = unit % 3
             f3_bank = bank(2 * pair, [P, len(ts), width])
             f1_bank = bank(2 * pair + 1, [P, len(ts), width])
+            f_banks[unit] = f3_bank, f1_bank
             steps = [(a, i, t) for a in range(PASSES) for i, t in enumerate(ts)]
             for step in steps:
                 a, i, t = step
                 table_product(
                     f3_bank[:, i, :], w3_codes[:, a, P * t:P * (t + 1)].bitcast(FP8X4),
-                    planes[a][:, W3_AT + P * t:W3_AT + P * (t + 1)], a, col0 + lo, width,
+                    planes[a][:, W3_AT + P * t:W3_AT + P * (t + 1)], a, col0, width,
                     step == steps[0], step == steps[-1])
             for step in steps:
                 a, i, t = step
                 table_product(
                     f1_bank[:, i, :], w1_codes[:, a, P * t:P * (t + 1)].bitcast(FP8X4),
-                    w1_scales[:, a, P * t:P * (t + 1)], a, col0 + lo, width,
+                    w1_scales[:, a, P * t:P * (t + 1)], a, col0, width,
                     step == steps[0], step == steps[-1])
-            part = (slice(None), slice(ts.start, ts.stop), slice(c + lo, c + lo + width))
-            piece = min(q, 2)
-            pe_lo = col0 + lo - pe_cols[piece][0]
-            f3pe = big.tile([P, len(ts), width], F32, name="f3pe", bufs=3, offset=F3PE_AT)
+
+        products = [
+            big.tile([P, 4 * HALF], F32, name="products%d" % q, offset=PRODUCTS_AT[q]) for q in range(CHUNKS)]
+
+        def product_slot(unit, which):
+            q, u = divmod(unit, 2)
+            at = (2 * u + which) * HALF
+            return products[q][:, at:at + HALF].rearrange("p (t c) -> p t c", t=len(unit_shape(unit)[0]))
+
+        def make_f3pe(unit):
+            ts, col0, width = unit_shape(unit)
+            piece = max(unit // 2 - 1, 0)
+            lo = col0 - pe_cols[piece][0]
+            f3pe[unit] = product_slot(unit, 0)
             nc.vector.tensor_tensor(
-                f3pe[:], f3_bank[:], pes[piece][:, ts.start:ts.stop, pe_lo:pe_lo + width], ALU.mult)
-            f1f2 = ring.tile([P, len(ts), width], F32, name="f1f2")
-            nc.vector.tensor_tensor(f1f2[:], f1_bank[:], f2[hf][part], ALU.mult)
-            if q < last:
-                return h_tiles[q][0][:, ts.start:ts.stop, :], f1f2[:], f3pe[:]
-            return h_tiles[q][u][:], f1f2[:], f3pe[:]
+                f3pe[unit], f_banks[unit][0][:], pes[piece][:, ts.start:ts.stop, lo:lo + width], ALU.mult)
+
+        def make_f1f2(unit):
+            ts, col0, width = unit_shape(unit)
+            hf, lo = divmod(col0, HALF)
+            f1f2[unit] = product_slot(unit, 1)
+            nc.vector.tensor_tensor(
+                f1f2[unit], f_banks[unit][1][:], f2[hf][:, ts.start:ts.stop, lo:lo + width], ALU.mult)
+
+        def make_products(unit):
+            make_f3pe(unit)
+            make_f1f2(unit)
+
+        def subtract(engine, unit):
+            q, u = divmod(unit, 2)
+            ts = unit_shape(unit)[0]
+            if u == 0:
+                open_h(q)
+            dst = h_tiles[q][0][:, ts.start:ts.stop, :] if q < last else h_tiles[q][u][:]
+            engine.tensor_tensor(dst, f1f2[unit], f3pe[unit], ALU.subtract)
 
         def open_h(q):
             parts = 1 if q < last else 2
-            h_tiles[q] = [keep.tile([P, PACK, CHUNK // parts], F32, name="h%d_%d" % (q, s)) for s in range(parts)]
+            if q in H_AT:
+                h_tiles[q] = [big.tile([P, PACK, CHUNK], F32, name="h%d" % q, offset=H_AT[q])]
+            else:
+                h_tiles[q] = [keep.tile([P, PACK, CHUNK // parts], F32, name="h%d_%d" % (q, s)) for s in range(parts)]
 
         def store_h(q, s):
             width = CHUNK // len(h_tiles[q])
@@ -268,25 +308,25 @@ def tile_list_autofocus_phase_step_kernel(
 
         def round_h(q, s, copy):
             if s == 0:
-                h_bf[q] = ring.tile([P, PACK * CHUNK], BF16, name="h_bf", align_bytes=64)
+                h_bf[q] = big.tile([P, PACK * CHUNK], BF16, name="h_bf%d" % q, align_bytes=64, offset=H_BF_AT[q])
             runs = CHUNK // len(h_tiles[q]) // RUN
             dst = h_bf[q][:].rearrange("p (c i t) -> p c t i", t=PACK, i=RUN)
             copy(dst[:, s * runs:(s + 1) * runs], h_tiles[q][s][:].rearrange("p t (c i) -> p c t i", i=RUN))
 
         def quantise_h(q):
             cols = slice(q * CHUNK, (q + 1) * CHUNK)
-            nc.vector.quantize_mx(h_codes[:, cols].bitcast(FP8X4), h_scales[:, cols], h_bf[q][:])
-            nc.sync.dma_start(words_v[:, cols], h_codes[:, cols])
+            nc.vector.quantize_mx(h_codes[q][:].bitcast(FP8X4), h_scales[:, cols], h_bf[q][:])
+            nc.sync.dma_start(words_v[:, cols], h_codes[q][:])
 
         def make_e(q):
             cols = slice(q * CHUNK, (q + 1) * CHUNK)
-            e_bank = bank(E_BANK if q < last else D_BANK, [P, 2, CHUNK])
+            e_bank = bank(E_BANKS[q], [P, 2, CHUNK])
             e_banks[q] = e_bank
             for n in range(N // P):
                 nc.tensor.matmul_mx(
                     e_bank[:, n, :], lhsT=wo_codes[:, 2 * P * n:2 * P * (n + 1)].bitcast(FP4X4),
                     lhsT_scale=wo_plane[:, P * n:P * (n + 1)],
-                    rhs=h_codes[:, cols].bitcast(FP8X4), rhs_scale=h_scales[:, cols],
+                    rhs=h_codes[q][:].bitcast(FP8X4), rhs_scale=h_scales[:, cols],
                     start=True, stop=True)
 
         def round_wd():
@@ -299,14 +339,14 @@ def tile_list_autofocus_phase_step_kernel(
             nc.vector.quantize_mx(wd_codes[:].bitcast(FP8X4), wd_scales[:], wd_bf[:])
 
         def make_damp(q):
-            d_bank = bank(D_BANK, [P, 2, CHUNK])
+            d_bank = bank(D_BANKS[q], [P, 2, CHUNK])
             for n in range(N // P):
                 for a in range(PASSES):
                     at = slice(a * N + P * n, a * N + P * (n + 1))
                     table_product(
                         d_bank[:, n, :], wd_codes[:, at].bitcast(FP8X4), wd_scales[:, at], a, q * CHUNK, CHUNK,
                         a == 0, a == PASSES - 1)
-            d2 = ring.tile([P, 2, CHUNK], F32, name="d2")
+            d2 = big.tile([P, 2, CHUNK], F32, name="d2_%d" % q, offset=D2_AT[q])
             nc.scalar.activation(d2[:], d_bank[:], ACT.Square)
             damp[q] = keep.tile([P, 2, CHUNK], F32, name="damp%d" % q)
             nc.scalar.activation(damp[q][:], d2[:], ACT.Abs_reciprocal_sqrt, bias=root_one[:])
@@ -316,37 +356,45 @@ def tile_list_autofocus_phase_step_kernel(
             nc.vector.tensor_tensor(y[:], e_banks[q][:], damp[q][:], ALU.mult)
             nc.sync.dma_start(y_v[:, :, q * CHUNK:(q + 1) * CHUNK], y[:])
 
-        def subtract(engine, operands):
-            engine.tensor_tensor(*operands, ALU.subtract)
+        def gpsimd_chunk(q):
+            subtract(nc.gpsimd, 2 * q)
+            subtract(nc.gpsimd, 2 * q + 1)
+            store_h(q, 0)
+            round_h(q, 0, nc.scalar.copy)
 
         round_wd()
-        for q in range(CHUNKS):
-            open_h(q)
-            first = make_products(q, 0)
-            if q >= 2:
-                quantise_h(q - 2)
-                make_e(q - 2)
-            subtract(nc.gpsimd, first)
-            if q == last:
-                store_h(q, 0)
-            if q >= 1:
-                round_h(q - 1, 0, nc.scalar.copy)
-            second = make_products(q, 1)
-            if q == 1:
-                quantise_wd()
-                make_damp(0)
-                make_damp(1)
-            if q == 2:
-                make_damp(2)
-            if q >= 2:
-                make_y(q - 2)
-            if q < last:
-                subtract(nc.gpsimd, second)
-                store_h(q, 0)
-        subtract(nc.vector, second)
-        store_h(last, 1)
+        for unit in range(3):
+            make_f(unit)
+        for unit in range(3):
+            make_products(unit)
+            make_f(unit + 3)
+        gpsimd_chunk(0)
+        make_f3pe(3)
+        quantise_wd()
+        make_f1f2(3)
+        make_damp(0)
+        make_damp(1)
+        make_f(6)
+        gpsimd_chunk(1)
+        make_products(4)
+        make_f(7)
+        make_products(5)
+        make_damp(2)
+        quantise_h(0)
+        make_e(0)
+        make_damp(3)
+        gpsimd_chunk(2)
+        make_products(6)
+        make_y(0)
+        make_products(7)
+        quantise_h(1)
+        make_e(1)
+        subtract(nc.vector, 6)
+        store_h(last, 0)
         round_h(last, 0, nc.scalar.copy)
-        make_damp(last)
+        subtract(nc.vector, 7)
+        store_h(last, 1)
+        make_y(1)
         quantise_h(last - 1)
         make_e(last - 1)
         round_h(last, 1, nc.vector.tensor_copy)

@@ -36,21 +36,24 @@ KIB = 1024
 TABLE_AT = (8 * KIB - 64, 26 * KIB)
 PICKED_ROWS_AT = 42 * KIB - 512
 W1_RAW_AT = (42 * KIB, 0)
+F2_AT = (96 * KIB, W1_RAW_AT[1])
+W1_SPLIT = 82
 W3_RAW_AT = 52 * KIB
-PE_AT = (8 * KIB, 50 * KIB, 54 * KIB)
-WD_RAW_AT = (16 * KIB, 20 * KIB)
+PE_AT = (8 * KIB, 20 * KIB, 50 * KIB, 54 * KIB)
+WD_RAW_AT = (12 * KIB, 16 * KIB)
 WO_CODES_AT = 43 * KIB
 WO_PLANE_AT = 43 * KIB + 512
 W1_BF_AT = 27 * KIB
 PRODUCTS_AT = (26 * KIB, 34 * KIB, 58 * KIB, 71 * KIB)
 WD_BF_AT = 64 * KIB
-H_BF_AT = (78 * KIB, 86 * KIB, 88 * KIB, 90 * KIB)
+H_BF_AT = (78 * KIB, 86 * KIB, 88 * KIB, 112 * KIB)
 H_AT = {1: 66 * KIB, 2: 79 * KIB}
 WD_CODES_AT = PRODUCTS_AT[0]
-WD_SCALES_AT = PE_AT[0]
+WD_SCALES_AT = PE_AT[1]
 H_CODES_AT = (PRODUCTS_AT[1], PRODUCTS_AT[2] - 512, 84 * KIB, 85 * KIB)
-H_SCALES_AT = PE_AT[1]
-D2_AT = (92 * KIB, H_BF_AT[1], 94 * KIB, H_BF_AT[2])
+H_SCALES_AT = PE_AT[2]
+D2_AT = (92 * KIB, H_BF_AT[1], H_BF_AT[2], PRODUCTS_AT[2] + 2 * KIB)
+Y_AT = (104 * KIB, H_BF_AT[3] + KIB, H_BF_AT[3] - KIB, 108 * KIB)
 
 
 def tile_list_autofocus_phase_step_kernel(
@@ -156,7 +159,7 @@ def tile_list_autofocus_phase_step_kernel(
 
         nc.sync.dma_start(w1_raw[1][:], w1_v[1])
         pe_v = pe.rearrange("(p t) j -> p t j", t=PACK)
-        pe_cols = ((0, HALF), (HALF, HALF + CHUNK), (HALF + CHUNK, S))
+        pe_cols = [(q * CHUNK, (q + 1) * CHUNK) for q in range(CHUNKS)]
         pes = [
             big.tile([P, PACK, hi - lo], F32, name="pe%d" % i, offset=PE_AT[i]) for i, (lo, hi) in enumerate(pe_cols)]
 
@@ -171,6 +174,7 @@ def tile_list_autofocus_phase_step_kernel(
             nc.sync.dma_start(wd_raw[a][:], wd_v[a])
         load_pe(1)
         load_pe(2)
+        load_pe(3)
         wo_codes = big.tile([P, 2 * N], U8, name="wo_codes", align_bytes=64, offset=WO_CODES_AT)
         nc.sync.dma_start(wo_codes[:].bitcast(I32), wo_words[0].bitcast(I32))
         wo_plane = big.tile([P, N], U8, name="wo_plane", align_bytes=64, offset=WO_PLANE_AT)
@@ -179,7 +183,7 @@ def tile_list_autofocus_phase_step_kernel(
             nc.sync.dma_start(
                 wo_plane[32 * quad:32 * quad + 4, :].bitcast(I32), wo_scales[0][4 * quad:4 * quad + 4, :].bitcast(I32))
 
-        f2 = [keep.tile([P, PACK, HALF], F32, name="f2_%d" % hf) for hf in range(2)]
+        f2 = [big.tile([P, PACK, HALF], F32, name="f2_%d" % hf, offset=F2_AT[hf]) for hf in range(2)]
         f2_banks = [[bank(b, [P, HALF]) for b in bs] for bs in ((0, 2, 1, 3), (4, 5, 6, 7))]
         for a in range(PASSES):
             for hf in range(2):
@@ -196,11 +200,13 @@ def tile_list_autofocus_phase_step_kernel(
         w1_codes = keep.tile([P, PASSES, H], I32, name="w1_codes", align_bytes=64)
         w1_scales = keep.tile([P, PASSES, H], U8, name="w1_scales", align_bytes=64)
 
-        def quantise_w1(a):
+        def quantise_w1(a, split):
             w1_bf = big.tile([P, PACK * H], BF16, name="w1_bf%d" % a, align_bytes=64, offset=W1_BF_AT)
             dealt = w1_bf[:].rearrange("p (u i m j) -> p m u j i", u=2, i=2, j=PACK)
             by_column = w1_raw[a][:].rearrange("p j (m u i) -> p m u j i", u=2, i=2)
-            nc.vector.tensor_copy(dealt, by_column)
+            nc.vector.tensor_copy(dealt[:, 0:split], by_column[:, 0:split])
+            if split < P:
+                nc.scalar.copy(dealt[:, split:P], by_column[:, split:P])
             half = H // 2
             for s in range(2):
                 nc.vector.quantize_mx(
@@ -209,9 +215,9 @@ def tile_list_autofocus_phase_step_kernel(
                     w1_bf[:, PACK * half * s:PACK * half * (s + 1)])
 
         empty_f2(0)
+        quantise_w1(0, P)
+        quantise_w1(1, W1_SPLIT)
         empty_f2(1)
-        quantise_w1(0)
-        quantise_w1(1)
 
         h_v = out_1.rearrange("(p t) j -> p t j", t=PACK)
         y_v = out_0.rearrange("(n p) j -> p n j", p=P)
@@ -269,7 +275,7 @@ def tile_list_autofocus_phase_step_kernel(
 
         def make_f3pe(unit):
             ts, col0, width = unit_shape(unit)
-            piece = max(unit // 2 - 1, 0)
+            piece = unit // 2
             lo = col0 - pe_cols[piece][0]
             f3pe[unit] = product_slot(unit, 0)
             nc.vector.tensor_tensor(
@@ -283,8 +289,8 @@ def tile_list_autofocus_phase_step_kernel(
                 f1f2[unit], f_banks[unit][1][:], f2[hf][:, ts.start:ts.stop, lo:lo + width], ALU.mult)
 
         def make_products(unit):
-            make_f3pe(unit)
             make_f1f2(unit)
+            make_f3pe(unit)
 
         def subtract(engine, unit):
             q, u = divmod(unit, 2)
@@ -352,7 +358,7 @@ def tile_list_autofocus_phase_step_kernel(
             nc.scalar.activation(damp[q][:], d2[:], ACT.Abs_reciprocal_sqrt, bias=root_one[:])
 
         def make_y(q):
-            y = keep.tile([P, 2, CHUNK], F32, name="y%d" % q)
+            y = big.tile([P, 2, CHUNK], F32, name="y%d" % q, offset=Y_AT[q])
             nc.vector.tensor_tensor(y[:], e_banks[q][:], damp[q][:], ALU.mult)
             nc.sync.dma_start(y_v[:, :, q * CHUNK:(q + 1) * CHUNK], y[:])
 
@@ -382,7 +388,6 @@ def tile_list_autofocus_phase_step_kernel(
         make_damp(2)
         quantise_h(0)
         make_e(0)
-        make_damp(3)
         gpsimd_chunk(2)
         make_products(6)
         make_y(0)
@@ -392,15 +397,16 @@ def tile_list_autofocus_phase_step_kernel(
         subtract(nc.vector, 6)
         store_h(last, 0)
         round_h(last, 0, nc.scalar.copy)
+        make_damp(last)
         subtract(nc.vector, 7)
         store_h(last, 1)
-        make_y(1)
         quantise_h(last - 1)
         make_e(last - 1)
         round_h(last, 1, nc.vector.tensor_copy)
         quantise_h(last)
         make_e(last)
-        make_y(last - 1)
+        make_y(1)
+        make_y(2)
         for quad in range(QUADS):
             nc.scalar.dma_start(
                 out_3[0][4 * quad:4 * quad + 4, :].bitcast(I32), h_scales[32 * quad:32 * quad + 4, :].bitcast(I32))

@@ -26,7 +26,7 @@ CHUNK = 256
 CHUNKS = S // CHUNK
 RUN = 2
 D_BANKS = (6, 7, 6, 4)
-E_BANKS = (7, 7, 6, 5)
+E_BANKS = (5, 7, 6, 5)
 
 W2_AT = S
 W3_AT = S + H
@@ -41,19 +41,21 @@ W1_SPLIT = 82
 W3_RAW_AT = 52 * KIB
 PE_AT = (8 * KIB, 20 * KIB, 50 * KIB, 54 * KIB)
 WD_RAW_AT = (12 * KIB, 16 * KIB)
-WO_CODES_AT = 43 * KIB
-WO_PLANE_AT = 43 * KIB + 512
-W1_BF_AT = 27 * KIB
-PRODUCTS_AT = (26 * KIB, 34 * KIB, 58 * KIB, 71 * KIB)
+WO_CODES_AT = 49 * KIB
+WO_PLANE_AT = 49 * KIB + 512
+W1_BF_AT = (32 * KIB, 34 * KIB)
+PRODUCTS_AT = (26 * KIB, 34 * KIB, 58 * KIB, 41 * KIB)
 WD_BF_AT = 64 * KIB
-H_BF_AT = (78 * KIB, 86 * KIB, 88 * KIB, 112 * KIB)
-H_AT = {1: 66 * KIB, 2: 79 * KIB}
+H_BF_AT = (78 * KIB, 86 * KIB, 112 * KIB, 88 * KIB)
+H_AT = (116 * KIB, 66 * KIB, 79 * KIB, 120 * KIB)
 WD_CODES_AT = PRODUCTS_AT[0]
-WD_SCALES_AT = PE_AT[1]
+WD_SCALES_AT = F2_AT[0]
 H_CODES_AT = (PRODUCTS_AT[1], PRODUCTS_AT[2] - 512, 84 * KIB, 85 * KIB)
 H_SCALES_AT = PE_AT[2]
-D2_AT = (92 * KIB, H_BF_AT[1], H_BF_AT[2], PRODUCTS_AT[2] + 2 * KIB)
-Y_AT = (104 * KIB, H_BF_AT[3] + KIB, H_BF_AT[3] - KIB, 108 * KIB)
+SQUARES_AT = (H_BF_AT[1], 90 * KIB, PRODUCTS_AT[1] + 1 * KIB, PRODUCTS_AT[1] + 3 * KIB)
+DAMP_AT = (124 * KIB, PRODUCTS_AT[1] + 5 * KIB, PRODUCTS_AT[3], PRODUCTS_AT[3] + 2 * KIB)
+HALF_BF_AT = (132 * KIB, 88 * KIB)
+Y_AT = (104 * KIB, HALF_BF_AT[0] + 512, HALF_BF_AT[0] - 1536, 108 * KIB)
 
 
 def tile_list_autofocus_phase_step_kernel(
@@ -201,18 +203,21 @@ def tile_list_autofocus_phase_step_kernel(
         w1_scales = keep.tile([P, PASSES, H], U8, name="w1_scales", align_bytes=64)
 
         def quantise_w1(a, split):
-            w1_bf = big.tile([P, PACK * H], BF16, name="w1_bf%d" % a, align_bytes=64, offset=W1_BF_AT)
-            dealt = w1_bf[:].rearrange("p (u i m j) -> p m u j i", u=2, i=2, j=PACK)
-            by_column = w1_raw[a][:].rearrange("p j (m u i) -> p m u j i", u=2, i=2)
-            nc.vector.tensor_copy(dealt[:, 0:split], by_column[:, 0:split])
-            if split < P:
-                nc.scalar.copy(dealt[:, split:P], by_column[:, split:P])
             half = H // 2
-            for s in range(2):
+            by_column = w1_raw[a][:].rearrange("p j (m u i) -> p u m j i", u=2, i=2)
+            tiles = []
+            for u in range(2):
+                w1_bf = big.tile(
+                    [P, PACK * half], BF16, name="w1_bf%d%d" % (a, u), align_bytes=64, offset=W1_BF_AT[u])
+                tiles.append(w1_bf)
+                dealt = w1_bf[:].rearrange("p (i m j) -> p m j i", i=2, j=PACK)
+                nc.vector.tensor_copy(dealt[:, 0:split], by_column[:, u, 0:split])
+                if split < P:
+                    nc.scalar.copy(dealt[:, split:P], by_column[:, u, split:P])
+            for u in range(2):
                 nc.vector.quantize_mx(
-                    w1_codes[:, a, half * s:half * (s + 1)].bitcast(FP8X4),
-                    w1_scales[:, a, half * s:half * (s + 1)],
-                    w1_bf[:, PACK * half * s:PACK * half * (s + 1)])
+                    w1_codes[:, a, half * u:half * (u + 1)].bitcast(FP8X4),
+                    w1_scales[:, a, half * u:half * (u + 1)], tiles[u][:])
 
         empty_f2(0)
         quantise_w1(0, P)
@@ -232,14 +237,11 @@ def tile_list_autofocus_phase_step_kernel(
         last = CHUNKS - 1
         h_tiles = {}
         h_bf = {}
-        damp = {}
         e_banks = {}
 
         def unit_shape(unit):
             q, u = divmod(unit, 2)
-            if q < last:
-                return range(2 * u, 2 * u + 2), q * CHUNK, CHUNK
-            return range(PACK), q * CHUNK + u * CHUNK // 2, CHUNK // 2
+            return range(2 * u, 2 * u + 2), q * CHUNK, CHUNK
 
         f_banks = {}
         f3pe = {}
@@ -270,7 +272,7 @@ def tile_list_autofocus_phase_step_kernel(
 
         def product_slot(unit, which):
             q, u = divmod(unit, 2)
-            at = (2 * u + which) * HALF
+            at = (2 * which + u) * HALF
             return products[q][:, at:at + HALF].rearrange("p (t c) -> p t c", t=len(unit_shape(unit)[0]))
 
         def make_f3pe(unit):
@@ -289,35 +291,32 @@ def tile_list_autofocus_phase_step_kernel(
                 f1f2[unit], f_banks[unit][1][:], f2[hf][:, ts.start:ts.stop, lo:lo + width], ALU.mult)
 
         def make_products(unit):
-            make_f1f2(unit)
             make_f3pe(unit)
-
-        def subtract(engine, unit):
-            q, u = divmod(unit, 2)
-            ts = unit_shape(unit)[0]
-            if u == 0:
-                open_h(q)
-            dst = h_tiles[q][0][:, ts.start:ts.stop, :] if q < last else h_tiles[q][u][:]
-            engine.tensor_tensor(dst, f1f2[unit], f3pe[unit], ALU.subtract)
+            make_f1f2(unit)
 
         def open_h(q):
-            parts = 1 if q < last else 2
-            if q in H_AT:
-                h_tiles[q] = [big.tile([P, PACK, CHUNK], F32, name="h%d" % q, offset=H_AT[q])]
-            else:
-                h_tiles[q] = [keep.tile([P, PACK, CHUNK // parts], F32, name="h%d_%d" % (q, s)) for s in range(parts)]
+            h_tiles[q] = big.tile([P, PACK, CHUNK], F32, name="h%d" % q, offset=H_AT[q])
 
-        def store_h(q, s):
-            width = CHUNK // len(h_tiles[q])
-            col0 = q * CHUNK + s * width
-            nc.sync.dma_start(h_v[:, :, col0:col0 + width], h_tiles[q][s][:])
+        def subtract_unit(unit):
+            ts = unit_shape(unit)[0]
+            nc.gpsimd.tensor_tensor(
+                h_tiles[unit // 2][:, ts.start:ts.stop, :], f1f2[unit], f3pe[unit], ALU.subtract)
 
-        def round_h(q, s, copy):
-            if s == 0:
-                h_bf[q] = big.tile([P, PACK * CHUNK], BF16, name="h_bf%d" % q, align_bytes=64, offset=H_BF_AT[q])
-            runs = CHUNK // len(h_tiles[q]) // RUN
-            dst = h_bf[q][:].rearrange("p (c i t) -> p c t i", t=PACK, i=RUN)
-            copy(dst[:, s * runs:(s + 1) * runs], h_tiles[q][s][:].rearrange("p t (c i) -> p c t i", i=RUN))
+        def subtract_chunk(engine, q):
+            engine.tensor_tensor(
+                h_tiles[q][:].rearrange("p t c -> p (t c)"),
+                products[q][:, 2 * HALF:4 * HALF], products[q][:, 0:2 * HALF], ALU.subtract)
+
+        def store_h(q):
+            nc.sync.dma_start(h_v[:, :, q * CHUNK:(q + 1) * CHUNK], h_tiles[q][:])
+
+        def interleave(copy, dst, src):
+            copy(dst[:].rearrange("p (c i t) -> p c t i", t=PACK, i=RUN),
+                 src[:].rearrange("p t (c i) -> p c t i", i=RUN))
+
+        def round_h(q):
+            h_bf[q] = big.tile([P, PACK * CHUNK], BF16, name="h_bf%d" % q, align_bytes=64, offset=H_BF_AT[q])
+            interleave(nc.scalar.copy, h_bf[q], h_tiles[q])
 
         def quantise_h(q):
             cols = slice(q * CHUNK, (q + 1) * CHUNK)
@@ -344,18 +343,24 @@ def tile_list_autofocus_phase_step_kernel(
         def quantise_wd():
             nc.vector.quantize_mx(wd_codes[:].bitcast(FP8X4), wd_scales[:], wd_bf[:])
 
-        def make_damp(q):
-            d_bank = bank(D_BANKS[q], [P, 2, CHUNK])
+        squares = [big.tile([P, 2, CHUNK], F32, name="squares%d" % q, offset=SQUARES_AT[q]) for q in range(CHUNKS)]
+        damp = [big.tile([P, 2, CHUNK], F32, name="damp%d" % q, offset=DAMP_AT[q]) for q in range(CHUNKS)]
+        d_banks = {}
+
+        def make_d(q):
+            d_banks[q] = bank(D_BANKS[q], [P, 2, CHUNK])
             for n in range(N // P):
                 for a in range(PASSES):
                     at = slice(a * N + P * n, a * N + P * (n + 1))
                     table_product(
-                        d_bank[:, n, :], wd_codes[:, at].bitcast(FP8X4), wd_scales[:, at], a, q * CHUNK, CHUNK,
+                        d_banks[q][:, n, :], wd_codes[:, at].bitcast(FP8X4), wd_scales[:, at], a, q * CHUNK, CHUNK,
                         a == 0, a == PASSES - 1)
-            d2 = big.tile([P, 2, CHUNK], F32, name="d2_%d" % q, offset=D2_AT[q])
-            nc.scalar.activation(d2[:], d_bank[:], ACT.Square)
-            damp[q] = keep.tile([P, 2, CHUNK], F32, name="damp%d" % q)
-            nc.scalar.activation(damp[q][:], d2[:], ACT.Abs_reciprocal_sqrt, bias=root_one[:])
+
+        def make_squares(q):
+            nc.scalar.activation(squares[q][:], d_banks[q][:], ACT.Square)
+
+        def make_damp(q):
+            nc.scalar.activation(damp[q][:], squares[q][:], ACT.Abs_reciprocal_sqrt, bias=root_one[:])
 
         def make_y(q):
             y = big.tile([P, 2, CHUNK], F32, name="y%d" % q, offset=Y_AT[q])
@@ -363,47 +368,71 @@ def tile_list_autofocus_phase_step_kernel(
             nc.sync.dma_start(y_v[:, :, q * CHUNK:(q + 1) * CHUNK], y[:])
 
         def gpsimd_chunk(q):
-            subtract(nc.gpsimd, 2 * q)
-            subtract(nc.gpsimd, 2 * q + 1)
-            store_h(q, 0)
-            round_h(q, 0, nc.scalar.copy)
+            open_h(q)
+            if q < 2:
+                subtract_unit(2 * q)
+                subtract_unit(2 * q + 1)
+            else:
+                subtract_chunk(nc.gpsimd, q)
+            store_h(q)
+            round_h(q)
 
         round_wd()
         for unit in range(3):
             make_f(unit)
-        for unit in range(3):
+        for unit in range(2):
             make_products(unit)
             make_f(unit + 3)
         gpsimd_chunk(0)
-        make_f3pe(3)
-        quantise_wd()
+        make_f1f2(2)
         make_f1f2(3)
+        make_f3pe(2)
+        make_f(5)
+        quantise_wd()
+        make_f3pe(3)
+        for q in range(2):
+            make_d(q)
+            make_squares(q)
         make_damp(0)
-        make_damp(1)
         make_f(6)
         gpsimd_chunk(1)
         make_products(4)
         make_f(7)
         make_products(5)
-        make_damp(2)
         quantise_h(0)
         make_e(0)
+        make_d(2)
+        make_squares(2)
+        make_damp(1)
+        make_d(3)
         gpsimd_chunk(2)
         make_products(6)
         make_y(0)
         make_products(7)
         quantise_h(1)
         make_e(1)
-        subtract(nc.vector, 6)
-        store_h(last, 0)
-        round_h(last, 0, nc.scalar.copy)
-        make_damp(last)
-        subtract(nc.vector, 7)
-        store_h(last, 1)
-        quantise_h(last - 1)
-        make_e(last - 1)
-        round_h(last, 1, nc.vector.tensor_copy)
-        quantise_h(last)
+        width = CHUNK // 2
+        last_products = products[last][:].rearrange("p (w t c) -> p w t c", w=2, t=PACK)
+        halves = [keep.tile([P, PACK, width], F32, name="h_half%d" % s) for s in range(2)]
+        halves_bf = [
+            big.tile([P, PACK * width], BF16, name="h_half_bf%d" % s, align_bytes=64, offset=HALF_BF_AT[s])
+            for s in range(2)]
+        for s in range(2):
+            cols = slice(s * width, (s + 1) * width)
+            nc.vector.tensor_tensor(halves[s][:], last_products[:, 1, :, cols], last_products[:, 0, :, cols], ALU.subtract)
+            nc.sync.dma_start(h_v[:, :, last * CHUNK + s * width:last * CHUNK + (s + 1) * width], halves[s][:])
+        interleave(nc.scalar.copy, halves_bf[0], halves[0])
+        make_squares(3)
+        make_damp(2)
+        make_damp(3)
+        quantise_h(2)
+        make_e(2)
+        interleave(nc.vector.tensor_copy, halves_bf[1], halves[1])
+        for s in range(2):
+            lo = last * CHUNK + s * width
+            nc.vector.quantize_mx(
+                h_codes[last][:, s * width:(s + 1) * width].bitcast(FP8X4), h_scales[:, lo:lo + width], halves_bf[s][:])
+        nc.sync.dma_start(words_v[:, last * CHUNK:S], h_codes[last][:])
         make_e(last)
         make_y(1)
         make_y(2)

@@ -25,8 +25,6 @@ HALF = S // 2
 CHUNK = 256
 CHUNKS = S // CHUNK
 RUN = 2
-D_BANKS = (6, 7, 6, 4)
-E_BANKS = (5, 7, 6, 5)
 
 W2_AT = S
 W3_AT = S + H
@@ -39,23 +37,24 @@ W1_RAW_AT = (42 * KIB, 0)
 F2_AT = (96 * KIB, W1_RAW_AT[1])
 W1_SPLIT = 82
 W3_RAW_AT = 52 * KIB
-PE_AT = (8 * KIB, 20 * KIB, 50 * KIB, 54 * KIB)
-WD_RAW_AT = (12 * KIB, 16 * KIB)
+PE_AT = (8 * KIB, 12 * KIB, 16 * KIB, 54 * KIB)
+WD_RAW_AT = (20 * KIB, 50 * KIB)
 WO_CODES_AT = 49 * KIB
 WO_PLANE_AT = 49 * KIB + 512
-W1_BF_AT = (32 * KIB, 34 * KIB)
+W1_BF_AT = (32 * KIB, 36 * KIB)
 PRODUCTS_AT = (26 * KIB, 34 * KIB, 58 * KIB, 41 * KIB)
-WD_BF_AT = 64 * KIB
-H_BF_AT = (78 * KIB, 86 * KIB, 112 * KIB, 88 * KIB)
-H_AT = (116 * KIB, 66 * KIB, 79 * KIB, 120 * KIB)
-WD_CODES_AT = PRODUCTS_AT[0]
-WD_SCALES_AT = F2_AT[0]
-H_CODES_AT = (PRODUCTS_AT[1], PRODUCTS_AT[2] - 512, 84 * KIB, 85 * KIB)
-H_SCALES_AT = PE_AT[2]
-SQUARES_AT = (H_BF_AT[1], 90 * KIB, PRODUCTS_AT[1] + 1 * KIB, PRODUCTS_AT[1] + 3 * KIB)
-DAMP_AT = (124 * KIB, PRODUCTS_AT[1] + 5 * KIB, PRODUCTS_AT[3], PRODUCTS_AT[3] + 2 * KIB)
-HALF_BF_AT = (132 * KIB, 88 * KIB)
-Y_AT = (104 * KIB, HALF_BF_AT[0] + 512, HALF_BF_AT[0] - 1536, 108 * KIB)
+WD_BF_AT = 68 * KIB
+H_AT = (104 * KIB, 70 * KIB)
+WD_CODES_AT = PRODUCTS_AT[1]
+WD_SCALES_AT = PE_AT[2]
+H_CODES_AT = (PRODUCTS_AT[2], 80 * KIB)
+H_BF0_AT = 84 * KIB
+H_BF1_AT = (116 * KIB, 120 * KIB)
+SQUARES_AT = (88 * KIB, 90 * KIB, PRODUCTS_AT[3], PRODUCTS_AT[3] + 2 * KIB)
+DAMP_AT = (132 * KIB, 134 * KIB, 124 * KIB, 126 * KIB)
+SCALAR_COLUMNS = 128
+E_BANKS = (4, 5, 0, 1)
+Y_AT = (H_BF1_AT[0] - KIB, H_BF1_AT[0] + KIB, 128 * KIB, 130 * KIB)
 
 
 def tile_list_autofocus_phase_step_kernel(
@@ -161,21 +160,18 @@ def tile_list_autofocus_phase_step_kernel(
 
         nc.sync.dma_start(w1_raw[1][:], w1_v[1])
         pe_v = pe.rearrange("(p t) j -> p t j", t=PACK)
-        pe_cols = [(q * CHUNK, (q + 1) * CHUNK) for q in range(CHUNKS)]
-        pes = [
-            big.tile([P, PACK, hi - lo], F32, name="pe%d" % i, offset=PE_AT[i]) for i, (lo, hi) in enumerate(pe_cols)]
+        pes = [big.tile([P, 2, HALF], F32, name="pe%d" % i, offset=PE_AT[i]) for i in range(4)]
 
         def load_pe(i):
-            lo, hi = pe_cols[i]
-            nc.sync.dma_start(pes[i][:], pe_v[:, :, lo:hi])
+            hf, u = divmod(i, 2)
+            nc.sync.dma_start(pes[i][:], pe_v[:, 2 * u:2 * u + 2, hf * HALF:(hf + 1) * HALF])
 
-        load_pe(0)
+        for i in range(3):
+            load_pe(i)
         wd_v = wd.rearrange("(a p j) n -> a p (j n)", p=P, j=PACK)
         wd_raw = [big.tile([P, PACK * N], F32, name="wd_raw%d" % a, offset=WD_RAW_AT[a]) for a in range(PASSES)]
         for a in range(PASSES):
             nc.sync.dma_start(wd_raw[a][:], wd_v[a])
-        load_pe(1)
-        load_pe(2)
         load_pe(3)
         wo_codes = big.tile([P, 2 * N], U8, name="wo_codes", align_bytes=64, offset=WO_CODES_AT)
         nc.sync.dma_start(wo_codes[:].bitcast(I32), wo_words[0].bitcast(I32))
@@ -227,216 +223,151 @@ def tile_list_autofocus_phase_step_kernel(
         h_v = out_1.rearrange("(p t) j -> p t j", t=PACK)
         y_v = out_0.rearrange("(n p) j -> p n j", p=P)
         words_v = out_2[0].rearrange("p m t -> p (m t)").bitcast(I32)
-        h_codes = [
-            big.tile([P, CHUNK], I32, name="h_codes%d" % q, align_bytes=64, offset=H_CODES_AT[q])
-            for q in range(CHUNKS)]
-        h_scales = big.tile([P, S], U8, name="h_scales", align_bytes=64, offset=H_SCALES_AT)
+        h_flat = [
+            big.tile([P, PACK * HALF], F32, name="h%d" % hf, align_bytes=64, offset=H_AT[hf]) for hf in range(2)]
+        h = [flat[:].rearrange("p (t c) -> p t c", t=PACK) for flat in h_flat]
+        h_bf0 = big.tile([P, PACK * HALF], BF16, name="h_bf0", align_bytes=64, offset=H_BF0_AT)
+        h_bf1 = [big.tile([P, PACK * CHUNK], BF16, name="h_bf1%d" % s, align_bytes=64, offset=H_BF1_AT[s])
+                 for s in range(2)]
+        h_codes = [big.tile([P, HALF], I32, name="h_codes%d" % hf, align_bytes=64, offset=H_CODES_AT[hf])
+                   for hf in range(2)]
+        h_scales = keep.tile([P, S], U8, name="h_scales", align_bytes=64)
         wd_bf = big.tile([P, PASSES * PACK * N], BF16, name="wd_bf", align_bytes=64, offset=WD_BF_AT)
         wd_codes = big.tile([P, PASSES * N], I32, name="wd_codes", align_bytes=64, offset=WD_CODES_AT)
         wd_scales = big.tile([P, PASSES * N], U8, name="wd_scales", align_bytes=64, offset=WD_SCALES_AT)
-        last = CHUNKS - 1
-        h_tiles = {}
-        h_bf = {}
+        products = [big.tile([P, 2, 2, HALF], F32, name="products%d" % i, offset=PRODUCTS_AT[i]) for i in range(4)]
+        f3pe = [tile[:, 0] for tile in products]
+        f1f2 = [tile[:, 1] for tile in products]
+        squares = [big.tile([P, HALF], F32, name="squares%d" % i, offset=SQUARES_AT[i]) for i in range(4)]
+        damp = [big.tile([P, HALF], F32, name="damp%d" % i, offset=DAMP_AT[i]) for i in range(4)]
+        f_banks = {}
+        d_banks = {}
         e_banks = {}
 
-        def unit_shape(unit):
-            q, u = divmod(unit, 2)
-            return range(2 * u, 2 * u + 2), q * CHUNK, CHUNK
-
-        f_banks = {}
-        f3pe = {}
-        f1f2 = {}
-
         def make_f(unit):
-            ts, col0, width = unit_shape(unit)
+            hf, t = divmod(unit, PACK)
             pair = unit % 3
-            f3_bank = bank(2 * pair, [P, len(ts), width])
-            f1_bank = bank(2 * pair + 1, [P, len(ts), width])
-            f_banks[unit] = f3_bank, f1_bank
-            steps = [(a, i, t) for a in range(PASSES) for i, t in enumerate(ts)]
-            for step in steps:
-                a, i, t = step
+            f_banks[unit] = bank(2 * pair, [P, HALF]), bank(2 * pair + 1, [P, HALF])
+            for a in range(PASSES):
                 table_product(
-                    f3_bank[:, i, :], w3_codes[:, a, P * t:P * (t + 1)].bitcast(FP8X4),
-                    planes[a][:, W3_AT + P * t:W3_AT + P * (t + 1)], a, col0, width,
-                    step == steps[0], step == steps[-1])
-            for step in steps:
-                a, i, t = step
+                    f_banks[unit][0][:], w3_codes[:, a, P * t:P * (t + 1)].bitcast(FP8X4),
+                    planes[a][:, W3_AT + P * t:W3_AT + P * (t + 1)], a, hf * HALF, HALF, a == 0, a == PASSES - 1)
+            for a in range(PASSES):
                 table_product(
-                    f1_bank[:, i, :], w1_codes[:, a, P * t:P * (t + 1)].bitcast(FP8X4),
-                    w1_scales[:, a, P * t:P * (t + 1)], a, col0, width,
-                    step == steps[0], step == steps[-1])
-
-        products = [
-            big.tile([P, 4 * HALF], F32, name="products%d" % q, offset=PRODUCTS_AT[q]) for q in range(CHUNKS)]
-
-        def product_slot(unit, which):
-            q, u = divmod(unit, 2)
-            at = (2 * which + u) * HALF
-            return products[q][:, at:at + HALF].rearrange("p (t c) -> p t c", t=len(unit_shape(unit)[0]))
+                    f_banks[unit][1][:], w1_codes[:, a, P * t:P * (t + 1)].bitcast(FP8X4),
+                    w1_scales[:, a, P * t:P * (t + 1)], a, hf * HALF, HALF, a == 0, a == PASSES - 1)
 
         def make_f3pe(unit):
-            ts, col0, width = unit_shape(unit)
-            piece = unit // 2
-            lo = col0 - pe_cols[piece][0]
-            f3pe[unit] = product_slot(unit, 0)
-            nc.vector.tensor_tensor(
-                f3pe[unit], f_banks[unit][0][:], pes[piece][:, ts.start:ts.stop, lo:lo + width], ALU.mult)
+            pair, i = divmod(unit, 2)
+            nc.vector.tensor_tensor(f3pe[pair][:, i], f_banks[unit][0][:], pes[pair][:, i], ALU.mult)
 
         def make_f1f2(unit):
-            ts, col0, width = unit_shape(unit)
-            hf, lo = divmod(col0, HALF)
-            f1f2[unit] = product_slot(unit, 1)
-            nc.vector.tensor_tensor(
-                f1f2[unit], f_banks[unit][1][:], f2[hf][:, ts.start:ts.stop, lo:lo + width], ALU.mult)
+            hf, t = divmod(unit, PACK)
+            nc.vector.tensor_tensor(f1f2[unit // 2][:, unit % 2], f_banks[unit][1][:], f2[hf][:, t], ALU.mult)
 
-        def make_products(unit):
-            make_f3pe(unit)
-            make_f1f2(unit)
+        def subtract(unit):
+            pair, i = divmod(unit, 2)
+            nc.gpsimd.tensor_tensor(h[0][:, unit], f1f2[pair][:, i], f3pe[pair][:, i], ALU.subtract)
 
-        def open_h(q):
-            h_tiles[q] = big.tile([P, PACK, CHUNK], F32, name="h%d" % q, offset=H_AT[q])
-
-        def subtract_unit(unit):
-            ts = unit_shape(unit)[0]
-            nc.gpsimd.tensor_tensor(
-                h_tiles[unit // 2][:, ts.start:ts.stop, :], f1f2[unit], f3pe[unit], ALU.subtract)
-
-        def subtract_chunk(engine, q):
-            engine.tensor_tensor(
-                h_tiles[q][:].rearrange("p t c -> p (t c)"),
-                products[q][:, 2 * HALF:4 * HALF], products[q][:, 0:2 * HALF], ALU.subtract)
-
-        def store_h(q):
-            nc.sync.dma_start(h_v[:, :, q * CHUNK:(q + 1) * CHUNK], h_tiles[q][:])
+        def store_h(hf, lo, hi):
+            nc.sync.dma_start(h_v[:, lo:hi, hf * HALF:(hf + 1) * HALF], h[hf][:, lo:hi])
 
         def interleave(copy, dst, src):
-            copy(dst[:].rearrange("p (c i t) -> p c t i", t=PACK, i=RUN),
-                 src[:].rearrange("p t (c i) -> p c t i", i=RUN))
+            copy(dst.rearrange("p (c i t) -> p c t i", t=PACK, i=RUN), src.rearrange("p t (c i) -> p c t i", i=RUN))
 
-        def round_h(q):
-            h_bf[q] = big.tile([P, PACK * CHUNK], BF16, name="h_bf%d" % q, align_bytes=64, offset=H_BF_AT[q])
-            interleave(nc.scalar.copy, h_bf[q], h_tiles[q])
+        def piece_parts(i):
+            if i < 2:
+                return [(slice(0, HALF), i, 0, HALF)]
+            return [(slice(n * CHUNK, (n + 1) * CHUNK), n, i * CHUNK, CHUNK) for n in range(N // P)]
 
-        def quantise_h(q):
-            cols = slice(q * CHUNK, (q + 1) * CHUNK)
-            nc.vector.quantize_mx(h_codes[q][:].bitcast(FP8X4), h_scales[:, cols], h_bf[q][:])
-            nc.sync.dma_start(words_v[:, cols], h_codes[q][:])
-
-        def make_e(q):
-            cols = slice(q * CHUNK, (q + 1) * CHUNK)
-            e_bank = bank(E_BANKS[q], [P, 2, CHUNK])
-            e_banks[q] = e_bank
-            for n in range(N // P):
+        def make_e(i):
+            e_banks[i] = bank(E_BANKS[i], [P, HALF])
+            for cols, n, col0, width in piece_parts(i):
+                hf, lo = divmod(col0, HALF)
                 nc.tensor.matmul_mx(
-                    e_bank[:, n, :], lhsT=wo_codes[:, 2 * P * n:2 * P * (n + 1)].bitcast(FP4X4),
+                    e_banks[i][:, cols], lhsT=wo_codes[:, 2 * P * n:2 * P * (n + 1)].bitcast(FP4X4),
                     lhsT_scale=wo_plane[:, P * n:P * (n + 1)],
-                    rhs=h_codes[q][:].bitcast(FP8X4), rhs_scale=h_scales[:, cols],
+                    rhs=h_codes[hf][:, lo:lo + width].bitcast(FP8X4), rhs_scale=h_scales[:, col0:col0 + width],
                     start=True, stop=True)
 
-        def round_wd():
-            for a in range(PASSES):
-                nc.scalar.copy(
-                    wd_bf[:, a * PACK * N:(a + 1) * PACK * N].rearrange("p (c i j) -> p c j i", j=PACK, i=RUN),
-                    wd_raw[a][:].rearrange("p (j c i) -> p c j i", j=PACK, i=RUN))
-
-        def quantise_wd():
-            nc.vector.quantize_mx(wd_codes[:].bitcast(FP8X4), wd_scales[:], wd_bf[:])
-
-        squares = [big.tile([P, 2, CHUNK], F32, name="squares%d" % q, offset=SQUARES_AT[q]) for q in range(CHUNKS)]
-        damp = [big.tile([P, 2, CHUNK], F32, name="damp%d" % q, offset=DAMP_AT[q]) for q in range(CHUNKS)]
-        d_banks = {}
-
-        def make_d(q):
-            d_banks[q] = bank(D_BANKS[q], [P, 2, CHUNK])
-            for n in range(N // P):
+        def make_d(i):
+            d_banks[i] = bank(6 + i % 2, [P, HALF])
+            for cols, n, col0, width in piece_parts(i):
                 for a in range(PASSES):
                     at = slice(a * N + P * n, a * N + P * (n + 1))
                     table_product(
-                        d_banks[q][:, n, :], wd_codes[:, at].bitcast(FP8X4), wd_scales[:, at], a, q * CHUNK, CHUNK,
+                        d_banks[i][:, cols], wd_codes[:, at].bitcast(FP8X4), wd_scales[:, at], a, col0, width,
                         a == 0, a == PASSES - 1)
 
-        def make_squares(q):
-            nc.scalar.activation(squares[q][:], d_banks[q][:], ACT.Square)
+        def make_squares(i):
+            nc.scalar.activation(squares[i][:], d_banks[i][:], ACT.Square)
 
-        def make_damp(q):
-            nc.scalar.activation(damp[q][:], squares[q][:], ACT.Abs_reciprocal_sqrt, bias=root_one[:])
+        def make_damp(i):
+            nc.scalar.activation(damp[i][:], squares[i][:], ACT.Abs_reciprocal_sqrt, bias=root_one[:])
 
-        def make_y(q):
-            y = big.tile([P, 2, CHUNK], F32, name="y%d" % q, offset=Y_AT[q])
-            nc.vector.tensor_tensor(y[:], e_banks[q][:], damp[q][:], ALU.mult)
-            nc.sync.dma_start(y_v[:, :, q * CHUNK:(q + 1) * CHUNK], y[:])
-
-        def gpsimd_chunk(q):
-            open_h(q)
-            if q < 2:
-                subtract_unit(2 * q)
-                subtract_unit(2 * q + 1)
+        def make_y(i):
+            y = big.tile([P, HALF], F32, name="y%d" % i, offset=Y_AT[i])
+            nc.vector.tensor_tensor(y[:], e_banks[i][:], damp[i][:], ALU.mult)
+            if i < 2:
+                nc.sync.dma_start(y_v[:, i, 0:HALF], y[:])
             else:
-                subtract_chunk(nc.gpsimd, q)
-            store_h(q)
-            round_h(q)
+                nc.sync.dma_start(y_v[:, :, i * CHUNK:(i + 1) * CHUNK], y[:].rearrange("p (n c) -> p n c", n=N // P))
 
-        round_wd()
+        for a in range(PASSES):
+            nc.scalar.copy(
+                wd_bf[:, a * PACK * N:(a + 1) * PACK * N].rearrange("p (c i j) -> p c j i", j=PACK, i=RUN),
+                wd_raw[a][:].rearrange("p (j c i) -> p c j i", j=PACK, i=RUN))
         for unit in range(3):
             make_f(unit)
-        for unit in range(2):
-            make_products(unit)
+        for unit in range(PACK):
+            make_f3pe(unit)
+            make_f1f2(unit)
             make_f(unit + 3)
-        gpsimd_chunk(0)
-        make_f1f2(2)
-        make_f1f2(3)
-        make_f3pe(2)
-        make_f(5)
-        quantise_wd()
-        make_f3pe(3)
-        for q in range(2):
-            make_d(q)
-            make_squares(q)
-        make_damp(0)
-        make_f(6)
-        gpsimd_chunk(1)
-        make_products(4)
+            subtract(unit)
+        store_h(0, 0, PACK)
+        interleave(nc.scalar.copy, h_bf0[:], h[0])
+        make_f3pe(4)
+        make_f1f2(4)
         make_f(7)
-        make_products(5)
-        quantise_h(0)
-        make_e(0)
+        make_f3pe(5)
+        make_f1f2(5)
+        nc.vector.quantize_mx(wd_codes[:].bitcast(FP8X4), wd_scales[:], wd_bf[:])
+        make_d(0)
+        make_d(1)
+        nc.gpsimd.tensor_tensor(h[1][:, 0:2], f1f2[2], f3pe[2], ALU.subtract)
+        store_h(1, 0, 2)
+        for i in range(2):
+            make_squares(i)
+        for i in range(2):
+            make_damp(i)
         make_d(2)
-        make_squares(2)
-        make_damp(1)
         make_d(3)
-        gpsimd_chunk(2)
-        make_products(6)
-        make_y(0)
-        make_products(7)
-        quantise_h(1)
+        for unit in (6, 7):
+            make_f3pe(unit)
+            make_f1f2(unit)
+        for s in range(2):
+            cols = slice(s * CHUNK, (s + 1) * CHUNK)
+            nc.vector.tensor_tensor(h[1][:, 2:4, cols], f1f2[3][:, :, cols], f3pe[3][:, :, cols], ALU.subtract)
+        store_h(1, 2, PACK)
+        interleave(nc.scalar.copy, h_bf1[0][:, 0:PACK * SCALAR_COLUMNS], h[1][:, :, 0:SCALAR_COLUMNS])
+        for i in (2, 3):
+            make_squares(i)
+        for i in (2, 3):
+            make_damp(i)
+        interleave(nc.vector.tensor_copy, h_bf1[0][:, PACK * SCALAR_COLUMNS:], h[1][:, :, SCALAR_COLUMNS:CHUNK])
+        nc.vector.quantize_mx(h_codes[0][:].bitcast(FP8X4), h_scales[:, 0:HALF], h_bf0[:])
+        nc.sync.dma_start(words_v[:, 0:HALF], h_codes[0][:])
+        make_e(0)
         make_e(1)
-        width = CHUNK // 2
-        last_products = products[last][:].rearrange("p (w t c) -> p w t c", w=2, t=PACK)
-        halves = [keep.tile([P, PACK, width], F32, name="h_half%d" % s) for s in range(2)]
-        halves_bf = [
-            big.tile([P, PACK * width], BF16, name="h_half_bf%d" % s, align_bytes=64, offset=HALF_BF_AT[s])
-            for s in range(2)]
+        interleave(nc.vector.tensor_copy, h_bf1[1][:], h[1][:, :, CHUNK:HALF])
         for s in range(2):
-            cols = slice(s * width, (s + 1) * width)
-            nc.vector.tensor_tensor(halves[s][:], last_products[:, 1, :, cols], last_products[:, 0, :, cols], ALU.subtract)
-            nc.sync.dma_start(h_v[:, :, last * CHUNK + s * width:last * CHUNK + (s + 1) * width], halves[s][:])
-        interleave(nc.scalar.copy, halves_bf[0], halves[0])
-        make_squares(3)
-        make_damp(2)
-        make_damp(3)
-        quantise_h(2)
-        make_e(2)
-        interleave(nc.vector.tensor_copy, halves_bf[1], halves[1])
-        for s in range(2):
-            lo = last * CHUNK + s * width
             nc.vector.quantize_mx(
-                h_codes[last][:, s * width:(s + 1) * width].bitcast(FP8X4), h_scales[:, lo:lo + width], halves_bf[s][:])
-        nc.sync.dma_start(words_v[:, last * CHUNK:S], h_codes[last][:])
-        make_e(last)
-        make_y(1)
-        make_y(2)
+                h_codes[1][:, s * CHUNK:(s + 1) * CHUNK].bitcast(FP8X4),
+                h_scales[:, HALF + s * CHUNK:HALF + (s + 1) * CHUNK], h_bf1[s][:])
+            make_e(2 + s)
+        nc.sync.dma_start(words_v[:, HALF:S], h_codes[1][:])
         for quad in range(QUADS):
             nc.scalar.dma_start(
                 out_3[0][4 * quad:4 * quad + 4, :].bitcast(I32), h_scales[32 * quad:32 * quad + 4, :].bitcast(I32))
-        make_y(last)
+        for i in range(4):
+            make_y(i)

@@ -54,7 +54,7 @@ SQUARES_AT = (88 * KIB, 90 * KIB, PRODUCTS_AT[3], PRODUCTS_AT[3] + 2 * KIB)
 DAMP_AT = (132 * KIB, 134 * KIB, 124 * KIB, 126 * KIB)
 SCALAR_COLUMNS = 128
 E_BANKS = (4, 5, 0, 1)
-Y_AT = (H_BF1_AT[0] - KIB, H_BF1_AT[0] + KIB, 128 * KIB, 130 * KIB)
+Y_AT = (112 * KIB, H_BF1_AT[0], 128 * KIB, 130 * KIB)
 
 
 def tile_list_autofocus_phase_step_kernel(
@@ -360,14 +360,14 @@ def tile_list_autofocus_phase_step_kernel(
         make_e(0)
         make_e(1)
         interleave(nc.vector.tensor_copy, h_bf1[1][:], h[1][:, :, CHUNK:HALF])
+        make_y(0)
         for s in range(2):
             nc.vector.quantize_mx(
                 h_codes[1][:, s * CHUNK:(s + 1) * CHUNK].bitcast(FP8X4),
                 h_scales[:, HALF + s * CHUNK:HALF + (s + 1) * CHUNK], h_bf1[s][:])
             make_e(2 + s)
         nc.sync.dma_start(words_v[:, HALF:S], h_codes[1][:])
-        for quad in range(QUADS):
-            nc.scalar.dma_start(
-                out_3[0][4 * quad:4 * quad + 4, :].bitcast(I32), h_scales[32 * quad:32 * quad + 4, :].bitcast(I32))
-        for i in range(4):
+        for r in range(4):
+            nc.scalar.dma_start(out_3[0][r:BLOCKS:4, :].bitcast(I32), h_scales[r:P:32, :].bitcast(I32))
+        for i in range(1, 4):
             make_y(i)

@@ -24,7 +24,7 @@ BLOCKS = 16
 HALF = S // 2
 CHUNK = 256
 CHUNKS = S // CHUNK
-RUN = 2
+RUN = 4
 
 W2_AT = S
 W3_AT = S + H

@@ -47,12 +47,12 @@ WD_BF_AT = 68 * KIB
 H_AT = (104 * KIB, 70 * KIB)
 WD_CODES_AT = PRODUCTS_AT[1]
 WD_SCALES_AT = PE_AT[2]
-H_CODES_AT = (PRODUCTS_AT[2], 80 * KIB)
+H_CODES_AT = (F2_AT[1], 80 * KIB)
 H_BF0_AT = 84 * KIB
 H_BF1_AT = (116 * KIB, 120 * KIB)
 SQUARES_AT = (88 * KIB, 90 * KIB, PRODUCTS_AT[3], PRODUCTS_AT[3] + 2 * KIB)
 DAMP_AT = (132 * KIB, 134 * KIB, 124 * KIB, 126 * KIB)
-SCALAR_COLUMNS = 128
+SCALAR_COLUMNS = 192
 E_BANKS = (4, 5, 0, 1)
 Y_AT = (112 * KIB, H_BF1_AT[0], 128 * KIB, 130 * KIB)
 
@@ -354,11 +354,11 @@ def tile_list_autofocus_phase_step_kernel(
             make_squares(i)
         for i in (2, 3):
             make_damp(i)
-        interleave(nc.vector.tensor_copy, h_bf1[0][:, PACK * SCALAR_COLUMNS:], h[1][:, :, SCALAR_COLUMNS:CHUNK])
         nc.vector.quantize_mx(h_codes[0][:].bitcast(FP8X4), h_scales[:, 0:HALF], h_bf0[:])
         nc.sync.dma_start(words_v[:, 0:HALF], h_codes[0][:])
         make_e(0)
         make_e(1)
+        interleave(nc.vector.tensor_copy, h_bf1[0][:, PACK * SCALAR_COLUMNS:], h[1][:, :, SCALAR_COLUMNS:CHUNK])
         interleave(nc.vector.tensor_copy, h_bf1[1][:], h[1][:, :, CHUNK:HALF])
         make_y(0)
         for s in range(2):
@@ -368,6 +368,6 @@ def tile_list_autofocus_phase_step_kernel(
             make_e(2 + s)
         nc.sync.dma_start(words_v[:, HALF:S], h_codes[1][:])
         for r in range(4):
-            nc.scalar.dma_start(out_3[0][r:BLOCKS:4, :].bitcast(I32), h_scales[r:P:32, :].bitcast(I32))
+            (nc.gpsimd if r == 0 else nc.scalar).dma_start(out_3[0][r:BLOCKS:4, :].bitcast(I32), h_scales[r:P:32, :].bitcast(I32))
         for i in range(1, 4):
             make_y(i)

@@ -37,8 +37,9 @@ W1_RAW_AT = (42 * KIB, 0)
 F2_AT = (96 * KIB, W1_RAW_AT[1])
 W1_SPLIT = 82
 W3_RAW_AT = 52 * KIB
-PE_AT = (8 * KIB, 12 * KIB, 16 * KIB, 54 * KIB)
-WD_RAW_AT = (20 * KIB, 50 * KIB)
+PE_AT = (8 * KIB, 12 * KIB, 16 * KIB, 20 * KIB)
+PE_SLICES = ((0, 1), (1, 2), (2, 3), (3, 4))
+WD_RAW_AT = (50 * KIB, 54 * KIB)
 WO_CODES_AT = 49 * KIB
 WO_PLANE_AT = 49 * KIB + 512
 W1_BF_AT = (32 * KIB, 36 * KIB)
@@ -46,7 +47,7 @@ PRODUCTS_AT = (26 * KIB, 34 * KIB, 58 * KIB, 41 * KIB)
 WD_BF_AT = 68 * KIB
 H_AT = (104 * KIB, 70 * KIB)
 WD_CODES_AT = PRODUCTS_AT[1]
-WD_SCALES_AT = PE_AT[2]
+WD_SCALES_AT = PE_AT[1]
 H_CODES_AT = (F2_AT[1], 80 * KIB)
 H_BF0_AT = 84 * KIB
 H_BF1_AT = (116 * KIB, 120 * KIB)
@@ -88,10 +89,10 @@ def tile_list_autofocus_phase_step_kernel(
             nc.sync.dma_start(tables[a][:], tab_words[a].rearrange("p t i -> p (t i)").bitcast(I32))
 
         load_table(0)
-        w2_raw = keep.tile([P, PASSES, 2 * H], U8, name="w2_raw", align_bytes=64)
-        nc.sync.dma_start(w2_raw[:].bitcast(I32), w2_words.rearrange("a p c -> p a c").bitcast(I32))
         w3_raw = big.tile([P, PASSES, H], I32, name="w3_raw", align_bytes=64, offset=W3_RAW_AT)
         nc.sync.dma_start(w3_raw[:], w3_words.rearrange("a p c i -> p a (c i)").bitcast(I32))
+        w2_raw = keep.tile([P, PASSES, 2 * H], U8, name="w2_raw", align_bytes=64)
+        nc.sync.dma_start(w2_raw[:].bitcast(I32), w2_words.rearrange("a p c -> p a c").bitcast(I32))
 
         for staged in (w_rows, tab_rows):
             for lo, hi in ((32, 64), (64, P)):
@@ -139,13 +140,13 @@ def tile_list_autofocus_phase_step_kernel(
 
         gather_words(0, 0)
         gather_words(0, 1)
-        deal_w2(0)
-        deal_w2(1)
         w3_codes = keep.tile([P, PASSES, H], I32, name="w3_codes", align_bytes=64)
         nc.vector.tensor_copy(
             w3_codes[:].rearrange("p a (t b m) -> p a b t m", t=PACK, m=4),
             w3_raw[:].rearrange("p a (b m t) -> p a b t m", t=PACK, m=4),
         )
+        deal_w2(1)
+        deal_w2(0)
         gather_words(1, 0)
         gather_words(1, 1)
 
@@ -160,19 +161,17 @@ def tile_list_autofocus_phase_step_kernel(
 
         nc.sync.dma_start(w1_raw[1][:], w1_v[1])
         pe_v = pe.rearrange("(p t) j -> p t j", t=PACK)
-        pes = [big.tile([P, 2, HALF], F32, name="pe%d" % i, offset=PE_AT[i]) for i in range(4)]
-
-        def load_pe(i):
-            hf, u = divmod(i, 2)
-            nc.sync.dma_start(pes[i][:], pe_v[:, 2 * u:2 * u + 2, hf * HALF:(hf + 1) * HALF])
-
-        for i in range(3):
-            load_pe(i)
+        pes = {}
+        for at, (lo, hi) in zip(PE_AT, PE_SLICES):
+            rows_of_pe = big.tile([P, hi - lo, S], F32, name="pe%d" % lo, offset=at)
+            nc.sync.dma_start(rows_of_pe[:], pe_v[:, lo:hi])
+            for t in range(lo, hi):
+                for hf in range(2):
+                    pes[PACK * hf + t] = rows_of_pe[:, t - lo, hf * HALF:(hf + 1) * HALF]
         wd_v = wd.rearrange("(a p j) n -> a p (j n)", p=P, j=PACK)
         wd_raw = [big.tile([P, PACK * N], F32, name="wd_raw%d" % a, offset=WD_RAW_AT[a]) for a in range(PASSES)]
         for a in range(PASSES):
             nc.sync.dma_start(wd_raw[a][:], wd_v[a])
-        load_pe(3)
         wo_codes = big.tile([P, 2 * N], U8, name="wo_codes", align_bytes=64, offset=WO_CODES_AT)
         nc.sync.dma_start(wo_codes[:].bitcast(I32), wo_words[0].bitcast(I32))
         wo_plane = big.tile([P, N], U8, name="wo_plane", align_bytes=64, offset=WO_PLANE_AT)
@@ -259,7 +258,7 @@ def tile_list_autofocus_phase_step_kernel(
 
         def make_f3pe(unit):
             pair, i = divmod(unit, 2)
-            nc.vector.tensor_tensor(f3pe[pair][:, i], f_banks[unit][0][:], pes[pair][:, i], ALU.mult)
+            nc.vector.tensor_tensor(f3pe[pair][:, i], f_banks[unit][0][:], pes[unit], ALU.mult)
 
         def make_f1f2(unit):
             hf, t = divmod(unit, PACK)

@@ -55,7 +55,7 @@ SQUARES_AT = (88 * KIB, 90 * KIB, PRODUCTS_AT[3], PRODUCTS_AT[3] + 2 * KIB)
 DAMP_AT = (132 * KIB, 134 * KIB, 124 * KIB, 126 * KIB)
 SCALAR_COLUMNS = 192
 E_BANKS = (4, 5, 0, 1)
-Y_AT = (112 * KIB, H_BF1_AT[0], 128 * KIB, 130 * KIB)
+Y_AT = (H_BF1_AT[0], H_BF1_AT[1], 128 * KIB, 130 * KIB)
 
 
 def tile_list_autofocus_phase_step_kernel(
@@ -243,18 +243,27 @@ def tile_list_autofocus_phase_step_kernel(
         d_banks = {}
         e_banks = {}
 
-        def make_f(unit):
-            hf, t = divmod(unit, PACK)
+        def open_banks(unit):
             pair = unit % 3
             f_banks[unit] = bank(2 * pair, [P, HALF]), bank(2 * pair + 1, [P, HALF])
-            for a in range(PASSES):
-                table_product(
-                    f_banks[unit][0][:], w3_codes[:, a, P * t:P * (t + 1)].bitcast(FP8X4),
-                    planes[a][:, W3_AT + P * t:W3_AT + P * (t + 1)], a, hf * HALF, HALF, a == 0, a == PASSES - 1)
-            for a in range(PASSES):
-                table_product(
-                    f_banks[unit][1][:], w1_codes[:, a, P * t:P * (t + 1)].bitcast(FP8X4),
-                    w1_scales[:, a, P * t:P * (t + 1)], a, hf * HALF, HALF, a == 0, a == PASSES - 1)
+
+        def f3_pass(unit, a):
+            hf, t = divmod(unit, PACK)
+            table_product(
+                f_banks[unit][0][:], w3_codes[:, a, P * t:P * (t + 1)].bitcast(FP8X4),
+                planes[a][:, W3_AT + P * t:W3_AT + P * (t + 1)], a, hf * HALF, HALF, a == 0, a == PASSES - 1)
+
+        def f1_pass(unit, a):
+            hf, t = divmod(unit, PACK)
+            table_product(
+                f_banks[unit][1][:], w1_codes[:, a, P * t:P * (t + 1)].bitcast(FP8X4),
+                w1_scales[:, a, P * t:P * (t + 1)], a, hf * HALF, HALF, a == 0, a == PASSES - 1)
+
+        def make_f(unit):
+            open_banks(unit)
+            for one_pass in (f3_pass, f1_pass):
+                for a in range(PASSES):
+                    one_pass(unit, a)
 
         def make_f3pe(unit):
             pair, i = divmod(unit, 2)
@@ -359,7 +368,6 @@ def tile_list_autofocus_phase_step_kernel(
         make_e(1)
         interleave(nc.vector.tensor_copy, h_bf1[0][:, PACK * SCALAR_COLUMNS:], h[1][:, :, SCALAR_COLUMNS:CHUNK])
         interleave(nc.vector.tensor_copy, h_bf1[1][:], h[1][:, :, CHUNK:HALF])
-        make_y(0)
         for s in range(2):
             nc.vector.quantize_mx(
                 h_codes[1][:, s * CHUNK:(s + 1) * CHUNK].bitcast(FP8X4),
@@ -368,5 +376,5 @@ def tile_list_autofocus_phase_step_kernel(
         nc.sync.dma_start(words_v[:, HALF:S], h_codes[1][:])
         for r in range(4):
             (nc.gpsimd if r == 0 else nc.scalar).dma_start(out_3[0][r:BLOCKS:4, :].bitcast(I32), h_scales[r:P:32, :].bitcast(I32))
-        for i in range(1, 4):
+        for i in range(4):
             make_y(i)

@@ -284,8 +284,6 @@ def tile_list_autofocus_phase_step_kernel(
             copy(dst.rearrange("p (c i t) -> p c t i", t=PACK, i=RUN), src.rearrange("p t (c i) -> p c t i", i=RUN))
 
         def piece_parts(i):
-            if i < 2:
-                return [(slice(0, HALF), i, 0, HALF)]
             return [(slice(n * CHUNK, (n + 1) * CHUNK), n, i * CHUNK, CHUNK) for n in range(N // P)]
 
         def make_e(i):
@@ -316,10 +314,7 @@ def tile_list_autofocus_phase_step_kernel(
         def make_y(i):
             y = big.tile([P, HALF], F32, name="y%d" % i, offset=Y_AT[i])
             nc.vector.tensor_tensor(y[:], e_banks[i][:], damp[i][:], ALU.mult)
-            if i < 2:
-                nc.sync.dma_start(y_v[:, i, 0:HALF], y[:])
-            else:
-                nc.sync.dma_start(y_v[:, :, i * CHUNK:(i + 1) * CHUNK], y[:].rearrange("p (n c) -> p n c", n=N // P))
+            nc.sync.dma_start(y_v[:, :, i * CHUNK:(i + 1) * CHUNK], y[:].rearrange("p (n c) -> p n c", n=N // P))
 
         for a in range(PASSES):
             nc.scalar.copy(

from contextlib import ExitStack

import concourse.mybir as mybir

K, T, S, H, N = 1024, 4096, 1024, 512, 256
FLOPS = 2 * S * (3 * K * H + K * N + H * N)

F32 = mybir.dt.float32
BF16 = mybir.dt.bfloat16
I32 = mybir.dt.int32
U32 = mybir.dt.uint32
U16 = mybir.dt.uint16
U8 = mybir.dt.uint8
FP8X4 = mybir.dt.float8_e4m3fn_x4
FP4X4 = mybir.dt.float4_e2m1fn_x4
ALU = mybir.AluOpType
ACT = mybir.ActivationFunctionType

P = 128
PACK = 4
PASSES = K // (P * PACK)
QUADS = 4
BLOCKS = 16
HALF = S // 2
CHUNK = 256
CHUNKS = S // CHUNK
RUN = 4

W2_AT = S
W3_AT = S + H
PLANE_WIDTH = S + 2 * H

KIB = 1024
TABLE_AT = (8 * KIB - 64, 26 * KIB)
PICKED_ROWS_AT = 42 * KIB - 512
W1_RAW_AT = (42 * KIB, 0)
F2_AT = (96 * KIB, W1_RAW_AT[1])
W1_SPLIT = 82
W3_RAW_AT = 52 * KIB
PE_AT = (8 * KIB, 12 * KIB, 16 * KIB, 20 * KIB)
PE_SLICES = ((0, 1), (1, 2), (2, 3), (3, 4))
WD_RAW_AT = (50 * KIB, 54 * KIB)
WO_CODES_AT = 49 * KIB
WO_PLANE_AT = 49 * KIB + 512
W1_BF_AT = (32 * KIB, 36 * KIB)
PRODUCTS_AT = (26 * KIB, 34 * KIB, 58 * KIB, 41 * KIB)
WD_BF_AT = 68 * KIB
H_AT = (104 * KIB, 70 * KIB)
WD_CODES_AT = PRODUCTS_AT[1]
WD_SCALES_AT = PE_AT[1]
H_CODES_AT = (F2_AT[1], 80 * KIB)
H_BF0_AT = 84 * KIB
H_BF1_AT = (116 * KIB, 120 * KIB)
SQUARES_AT = (88 * KIB, 90 * KIB, PRODUCTS_AT[3], PRODUCTS_AT[3] + 2 * KIB)
DAMP_AT = (132 * KIB, 134 * KIB, 124 * KIB, 126 * KIB)
SCALAR_COLUMNS = 192
E_BANKS = (4, 5, 0, 1)
Y_AT = (H_BF1_AT[0], H_BF1_AT[1], 128 * KIB, 130 * KIB)


def tile_list_autofocus_phase_step_kernel(
    tc, tab_words, tab_scales, offs, w1, w2_words, w2_scales, w3_words, w3_scales,
    pe, wd, wo_words, wo_scales, out_0, out_1, out_2, out_3,
):
    nc = tc.nc
    with ExitStack() as ctx:
        lists = ctx.enter_context(tc.tile_pool(name="lists", bufs=1))
        keep = ctx.enter_context(tc.tile_pool(name="keep", bufs=1))
        big = ctx.enter_context(tc.tile_pool(name="big", bufs=1))
        psum = ctx.enter_context(tc.psum_pool(name="psum", bufs=1))

        def bank(b, shape):
            return psum.tile(shape, F32, name="bank%d" % b, tag="bank%d" % b)

        rows = PASSES * BLOCKS
        tab_rows = keep.tile([P, T], U8, name="tab_rows", align_bytes=64)
        w_rows = keep.tile([P, 2 * H], U8, name="w_rows", align_bytes=64)
        plane0 = keep.tile([P, PLANE_WIDTH], U8, name="plane0", align_bytes=64)
        plane1 = keep.tile([P, PLANE_WIDTH], U8, name="plane1", align_bytes=64)
        planes = [plane0, plane1]
        nc.sync.dma_start(w_rows[0:rows, 0:H].bitcast(I32), w2_scales.rearrange("a q c -> (a q) c").bitcast(I32))
        nc.sync.dma_start(w_rows[0:rows, H:].bitcast(I32), w3_scales.rearrange("a q c -> (a q) c").bitcast(I32))
        nc.sync.dma_start(tab_rows[0:rows, :].bitcast(I32), tab_scales.rearrange("a q c -> (a q) c").bitcast(I32))
        offsets = lists.tile([P, S // 16], U16, name="offsets")
        nc.sync.dma_start(offsets[:], offs)
        tables = [big.tile([P, T], I32, name="table%d" % a, offset=TABLE_AT[a]) for a in range(PASSES)]

        def load_table(a):
            nc.sync.dma_start(tables[a][:], tab_words[a].rearrange("p t i -> p (t i)").bitcast(I32))

        load_table(0)
        w3_raw = big.tile([P, PASSES, H], I32, name="w3_raw", align_bytes=64, offset=W3_RAW_AT)
        nc.sync.dma_start(w3_raw[:], w3_words.rearrange("a p c i -> p a (c i)").bitcast(I32))
        w2_raw = keep.tile([P, PASSES, 2 * H], U8, name="w2_raw", align_bytes=64)
        nc.sync.dma_start(w2_raw[:].bitcast(I32), w2_words.rearrange("a p c -> p a c").bitcast(I32))

        for staged in (w_rows, tab_rows):
            for lo, hi in ((32, 64), (64, P)):
                nc.vector.memset(staged[lo:hi, :].bitcast(I32), 0)
        nc.gpsimd.memset(plane1[:].bitcast(I32), 0)
        one = keep.tile([P, 1], F32, name="one")
        nc.gpsimd.memset(one[:], 1.0)
        root_one = keep.tile([P, 1], F32, name="root_one")
        nc.scalar.activation(root_one[:], one[:], ACT.Abs_reciprocal_sqrt)

        nc.vector.tensor_copy(
            plane0[:, W2_AT:PLANE_WIDTH].rearrange("p (w t b m) -> p w b t m", w=2, t=PACK, m=16),
            w_rows[:].rearrange("p (w b m t) -> p w b t m", w=2, t=PACK, m=16),
        )
        picked_rows = big.tile([P, S], U8, name="picked_rows", align_bytes=64, offset=PICKED_ROWS_AT)
        nc.vector.tensor_copy(picked_rows[:], tab_rows[:].indirect(offsets[:]))
        nc.vector.tensor_copy(plane0[:, 0:S].bitcast(I32), picked_rows[:].bitcast(I32))
        for quad in range(1, QUADS):
            nc.sync.dma_start(
                plane0[32 * quad:32 * quad + 4, :].bitcast(I32), plane0[4 * quad:4 * quad + 4, :].bitcast(I32))
        load_table(1)
        for quad in range(QUADS):
            nc.sync.dma_start(
                plane1[32 * quad:32 * quad + 4, :].bitcast(I32),
                plane0[BLOCKS + 4 * quad:BLOCKS + 4 * quad + 4, 0:PLANE_WIDTH].bitcast(I32))
        w1_v = w1.rearrange("(a p j) c -> a p j c", p=P, j=PACK)
        w1_raw = [big.tile([P, PACK, H], F32, name="w1_raw%d" % a, offset=W1_RAW_AT[a]) for a in range(PASSES)]
        nc.sync.dma_start(w1_raw[0][:], w1_v[0])

        picked = {}

        def gather_words(a, hf):
            columns = HALF // 16
            picked[a, hf] = keep.tile([P, HALF], U32, name="picked%d%d" % (a, hf), align_bytes=64)
            nc.vector.tensor_copy(
                picked[a, hf][:], tables[a][:].bitcast(U32).indirect(offsets[:, hf * columns:(hf + 1) * columns]))

        w2_codes = keep.tile([P, PASSES, 2 * H], U8, name="w2_codes", align_bytes=64)

        def deal_w2(a):
            nc.vector.tensor_copy(
                w2_codes[:, a, :].bitcast(U16).rearrange("p (t b m) -> p b t m", t=PACK, m=8),
                w2_raw[:, a, :].bitcast(U16).rearrange("p (b m t) -> p b t m", t=PACK, m=8),
            )

        gather_words(0, 0)
        gather_words(0, 1)
        w3_codes = keep.tile([P, PASSES, H], I32, name="w3_codes", align_bytes=64)
        nc.vector.tensor_copy(
            w3_codes[:].rearrange("p a (t b m) -> p a b t m", t=PACK, m=4),
            w3_raw[:].rearrange("p a (b m t) -> p a b t m", t=PACK, m=4),
        )
        deal_w2(1)
        deal_w2(0)
        gather_words(1, 0)
        gather_words(1, 1)

        def table_product(out, codes, scales, a, col0, width, start, stop):
            hf, c = divmod(col0, HALF)
            nc.tensor.matmul_mx(
                out, lhsT=codes, lhsT_scale=scales,
                rhs=picked[a, hf][:, c:c + width].bitcast(FP8X4),
                rhs_scale=planes[a][:, col0:col0 + width],
                start=start, stop=stop,
            )

        nc.sync.dma_start(w1_raw[1][:], w1_v[1])
        pe_v = pe.rearrange("(p t) j -> p t j", t=PACK)
        pes = {}
        for at, (lo, hi) in zip(PE_AT, PE_SLICES):
            rows_of_pe = big.tile([P, hi - lo, S], F32, name="pe%d" % lo, offset=at)
            nc.sync.dma_start(rows_of_pe[:], pe_v[:, lo:hi])
            for t in range(lo, hi):
                for hf in range(2):
                    pes[PACK * hf + t] = rows_of_pe[:, t - lo, hf * HALF:(hf + 1) * HALF]
        wd_v = wd.rearrange("(a p j) n -> a p (j n)", p=P, j=PACK)
        wd_raw = [big.tile([P, PACK * N], F32, name="wd_raw%d" % a, offset=WD_RAW_AT[a]) for a in range(PASSES)]
        for a in range(PASSES):
            nc.sync.dma_start(wd_raw[a][:], wd_v[a])
        wo_codes = big.tile([P, 2 * N], U8, name="wo_codes", align_bytes=64, offset=WO_CODES_AT)
        nc.sync.dma_start(wo_codes[:].bitcast(I32), wo_words[0].bitcast(I32))
        wo_plane = big.tile([P, N], U8, name="wo_plane", align_bytes=64, offset=WO_PLANE_AT)
        nc.gpsimd.memset(wo_plane[:].bitcast(I32), 0)
        for quad in range(QUADS):
            nc.sync.dma_start(
                wo_plane[32 * quad:32 * quad + 4, :].bitcast(I32), wo_scales[0][4 * quad:4 * quad + 4, :].bitcast(I32))

        f2 = [big.tile([P, PACK, HALF], F32, name="f2_%d" % hf, offset=F2_AT[hf]) for hf in range(2)]
        f2_banks = [[bank(b, [P, HALF]) for b in bs] for bs in ((0, 2, 1, 3), (4, 5, 6, 7))]
        for a in range(PASSES):
            for hf in range(2):
                for t in range(PACK):
                    table_product(
                        f2_banks[hf][t][:], w2_codes[:, a, 2 * P * t:2 * P * (t + 1)].bitcast(FP4X4),
                        planes[a][:, W2_AT + P * t:W2_AT + P * (t + 1)], a, hf * HALF, HALF,
                        a == 0, a == PASSES - 1)

        def empty_f2(hf):
            for t in range(PACK):
                nc.scalar.copy(f2[hf][:, t, :], f2_banks[hf][t][:])

        w1_codes = keep.tile([P, PASSES, H], I32, name="w1_codes", align_bytes=64)
        w1_scales = keep.tile([P, PASSES, H], U8, name="w1_scales", align_bytes=64)

        def quantise_w1(a, split):
            half = H // 2
            by_column = w1_raw[a][:].rearrange("p j (m u i) -> p u m j i", u=2, i=2)
            tiles = []
            for u in range(2):
                w1_bf = big.tile(
                    [P, PACK * half], BF16, name="w1_bf%d%d" % (a, u), align_bytes=64, offset=W1_BF_AT[u])
                tiles.append(w1_bf)
                dealt = w1_bf[:].rearrange("p (i m j) -> p m j i", i=2, j=PACK)
                nc.vector.tensor_copy(dealt[:, 0:split], by_column[:, u, 0:split])
                if split < P:
                    nc.scalar.copy(dealt[:, split:P], by_column[:, u, split:P])
            for u in range(2):
                nc.vector.quantize_mx(
                    w1_codes[:, a, half * u:half * (u + 1)].bitcast(FP8X4),
                    w1_scales[:, a, half * u:half * (u + 1)], tiles[u][:])

        empty_f2(0)
        quantise_w1(0, P)
        quantise_w1(1, W1_SPLIT)
        empty_f2(1)

        h_v = out_1.rearrange("(p t) j -> p t j", t=PACK)
        y_v = out_0.rearrange("(n p) j -> p n j", p=P)
        words_v = out_2[0].rearrange("p m t -> p (m t)").bitcast(I32)
        h_flat = [
            big.tile([P, PACK * HALF], F32, name="h%d" % hf, align_bytes=64, offset=H_AT[hf]) for hf in range(2)]
        h = [flat[:].rearrange("p (t c) -> p t c", t=PACK) for flat in h_flat]
        h_bf0 = big.tile([P, PACK * HALF], BF16, name="h_bf0", align_bytes=64, offset=H_BF0_AT)
        h_bf1 = [big.tile([P, PACK * CHUNK], BF16, name="h_bf1%d" % s, align_bytes=64, offset=H_BF1_AT[s])
                 for s in range(2)]
        h_codes = [big.tile([P, HALF], I32, name="h_codes%d" % hf, align_bytes=64, offset=H_CODES_AT[hf])
                   for hf in range(2)]
        h_scales = keep.tile([P, S], U8, name="h_scales", align_bytes=64)
        wd_bf = big.tile([P, PASSES * PACK * N], BF16, name="wd_bf", align_bytes=64, offset=WD_BF_AT)
        wd_codes = big.tile([P, PASSES * N], I32, name="wd_codes", align_bytes=64, offset=WD_CODES_AT)
        wd_scales = big.tile([P, PASSES * N], U8, name="wd_scales", align_bytes=64, offset=WD_SCALES_AT)
        products = [big.tile([P, 2, 2, HALF], F32, name="products%d" % i, offset=PRODUCTS_AT[i]) for i in range(4)]
        f3pe = [tile[:, 0] for tile in products]
        f1f2 = [tile[:, 1] for tile in products]
        squares = [big.tile([P, HALF], F32, name="squares%d" % i, offset=SQUARES_AT[i]) for i in range(4)]
        damp = [big.tile([P, HALF], F32, name="damp%d" % i, offset=DAMP_AT[i]) for i in range(4)]
        f_banks = {}
        d_banks = {}
        e_banks = {}

        def open_banks(unit):
            pair = unit % 3
            f_banks[unit] = bank(2 * pair, [P, HALF]), bank(2 * pair + 1, [P, HALF])

        def f3_pass(unit, a):
            hf, t = divmod(unit, PACK)
            table_product(
                f_banks[unit][0][:], w3_codes[:, a, P * t:P * (t + 1)].bitcast(FP8X4),
                planes[a][:, W3_AT + P * t:W3_AT + P * (t + 1)], a, hf * HALF, HALF, a == 0, a == PASSES - 1)

        def f1_pass(unit, a):
            hf, t = divmod(unit, PACK)
            table_product(
                f_banks[unit][1][:], w1_codes[:, a, P * t:P * (t + 1)].bitcast(FP8X4),
                w1_scales[:, a, P * t:P * (t + 1)], a, hf * HALF, HALF, a == 0, a == PASSES - 1)

        def make_f(unit):
            open_banks(unit)
            for one_pass in (f3_pass, f1_pass):
                for a in range(PASSES):
                    one_pass(unit, a)

        def make_f3pe(unit):
            pair, i = divmod(unit, 2)
            nc.vector.tensor_tensor(f3pe[pair][:, i], f_banks[unit][0][:], pes[unit], ALU.mult)

        def make_f1f2(unit):
            hf, t = divmod(unit, PACK)
            nc.vector.tensor_tensor(f1f2[unit // 2][:, unit % 2], f_banks[unit][1][:], f2[hf][:, t], ALU.mult)

        def subtract(unit):
            pair, i = divmod(unit, 2)
            nc.gpsimd.tensor_tensor(h[0][:, unit], f1f2[pair][:, i], f3pe[pair][:, i], ALU.subtract)

        def store_h(hf, lo, hi):
            nc.sync.dma_start(h_v[:, lo:hi, hf * HALF:(hf + 1) * HALF], h[hf][:, lo:hi])

        def interleave(copy, dst, src):
            copy(dst.rearrange("p (c i t) -> p c t i", t=PACK, i=RUN), src.rearrange("p t (c i) -> p c t i", i=RUN))

        def piece_parts(i):
            return [(slice(n * CHUNK, (n + 1) * CHUNK), n, i * CHUNK, CHUNK) for n in range(N // P)]

        def make_e(i):
            e_banks[i] = bank(E_BANKS[i], [P, HALF])
            for cols, n, col0, width in piece_parts(i):
                hf, lo = divmod(col0, HALF)
                nc.tensor.matmul_mx(
                    e_banks[i][:, cols], lhsT=wo_codes[:, 2 * P * n:2 * P * (n + 1)].bitcast(FP4X4),
                    lhsT_scale=wo_plane[:, P * n:P * (n + 1)],
                    rhs=h_codes[hf][:, lo:lo + width].bitcast(FP8X4), rhs_scale=h_scales[:, col0:col0 + width],
                    start=True, stop=True)

        def make_d(i):
            d_banks[i] = bank(6 + i % 2, [P, HALF])
            for cols, n, col0, width in piece_parts(i):
                for a in range(PASSES):
                    at = slice(a * N + P * n, a * N + P * (n + 1))
                    table_product(
                        d_banks[i][:, cols], wd_codes[:, at].bitcast(FP8X4), wd_scales[:, at], a, col0, width,
                        a == 0, a == PASSES - 1)

        def make_squares(i):
            nc.scalar.activation(squares[i][:], d_banks[i][:], ACT.Square)

        def make_damp(i):
            nc.scalar.activation(damp[i][:], squares[i][:], ACT.Abs_reciprocal_sqrt, bias=root_one[:])

        def make_y(i):
            y = big.tile([P, HALF], F32, name="y%d" % i, offset=Y_AT[i])
            nc.vector.tensor_tensor(y[:], e_banks[i][:], damp[i][:], ALU.mult)
            nc.sync.dma_start(y_v[:, :, i * CHUNK:(i + 1) * CHUNK], y[:].rearrange("p (n c) -> p n c", n=N // P))

        for a in range(PASSES):
            nc.scalar.copy(
                wd_bf[:, a * PACK * N:(a + 1) * PACK * N].rearrange("p (c i j) -> p c j i", j=PACK, i=RUN),
                wd_raw[a][:].rearrange("p (j c i) -> p c j i", j=PACK, i=RUN))
        for unit in range(3):
            make_f(unit)
        for unit in range(PACK):
            make_f3pe(unit)
            make_f1f2(unit)
            make_f(unit + 3)
            subtract(unit)
        store_h(0, 0, PACK)
        interleave(nc.scalar.copy, h_bf0[:], h[0])
        make_f3pe(4)
        make_f1f2(4)
        make_f(7)
        make_f3pe(5)
        make_f1f2(5)
        nc.vector.quantize_mx(wd_codes[:].bitcast(FP8X4), wd_scales[:], wd_bf[:])
        make_d(0)
        make_d(1)
        nc.gpsimd.tensor_tensor(h[1][:, 0:2], f1f2[2], f3pe[2], ALU.subtract)
        store_h(1, 0, 2)
        for i in range(2):
            make_squares(i)
        for i in range(2):
            make_damp(i)
        make_d(2)
        make_d(3)
        for unit in (6, 7):
            make_f3pe(unit)
            make_f1f2(unit)
        for s in range(2):
            cols = slice(s * CHUNK, (s + 1) * CHUNK)
            nc.vector.tensor_tensor(h[1][:, 2:4, cols], f1f2[3][:, :, cols], f3pe[3][:, :, cols], ALU.subtract)
        store_h(1, 2, PACK)
        interleave(nc.scalar.copy, h_bf1[0][:, 0:PACK * SCALAR_COLUMNS], h[1][:, :, 0:SCALAR_COLUMNS])
        for i in (2, 3):
            make_squares(i)
        for i in (2, 3):
            make_damp(i)
        nc.vector.quantize_mx(h_codes[0][:].bitcast(FP8X4), h_scales[:, 0:HALF], h_bf0[:])
        nc.sync.dma_start(words_v[:, 0:HALF], h_codes[0][:])
        make_e(0)
        make_e(1)
        interleave(nc.vector.tensor_copy, h_bf1[0][:, PACK * SCALAR_COLUMNS:], h[1][:, :, SCALAR_COLUMNS:CHUNK])
        interleave(nc.vector.tensor_copy, h_bf1[1][:], h[1][:, :, CHUNK:HALF])
        for s in range(2):
            nc.vector.quantize_mx(
                h_codes[1][:, s * CHUNK:(s + 1) * CHUNK].bitcast(FP8X4),
                h_scales[:, HALF + s * CHUNK:HALF + (s + 1) * CHUNK], h_bf1[s][:])
            make_e(2 + s)
        nc.sync.dma_start(words_v[:, HALF:S], h_codes[1][:])
        for r in range(4):
            (nc.gpsimd if r == 0 else nc.scalar).dma_start(out_3[0][r:BLOCKS:4, :].bitcast(I32), h_scales[r:P:32, :].bitcast(I32))
        for i in range(4):
            make_y(i)
